import numpy as np, ml_dtypes
CORES = [10,34,74,98]
N = 4
BF = ml_dtypes.bfloat16
def gentries(a):
    return np.ascontiguousarray(a.reshape(8, 16, -1).transpose(0, 2, 1)).reshape(8, -1)
def gtable(e):
    e = np.asarray(e); return np.ascontiguousarray(e.reshape(8, -1, 16).transpose(0, 2, 1)).reshape(128, -1).astype(np.int32)
V, L, TV, LV, H = 2048, 256, 4, 2, 1
W = V + TV * LV * L
def parts(rng):
    x = rng.integers(0, 64, (N, 8, 16, V)); ch = rng.integers(0, V, (N, 8, 16, V)); b, a, c = rng.integers(0, V, (3, N, 8, L))
    y = rng.integers(0, 64, (N, 8, 16, L)); th = rng.integers(285, 361, (N, 8, 1)) + rng.integers(-40, 41, (N, 8, 16))
    return x, ch, b, a, c, y, th
def pack(x, ch, b, a, c, y, th):
    return {"x": x.reshape(N, 128, V).astype(np.float32).astype(BF), "ch": np.ascontiguousarray(ch.reshape(N, 128, V)).astype(np.int32), "sb": np.stack([gtable(e) for e in b]),
            "ia": np.stack([gtable(e) for e in a]), "ic": np.stack([gtable(e) for e in c]), "y": y.reshape(N, 128, L).astype(np.float32).astype(BF), "th": np.ascontiguousarray(th.reshape(N, 128, 1)).astype(np.int32)}
def setup_inputs(rng):
    x, ch, b, a, c, y, th = parts(rng); m = rng.random((N, 8, L))
    c = np.where(m < 0.06, a, np.where(m < 0.12, b, c))
    return pack(x, ch, b, a, c, y, th)
def setup_inputs_spread(rng):
    x, ch, b, a, c, y, th = parts(rng)
    x = np.floor(np.exp2(6 * rng.random((N, 8, 1, V))) * rng.random((N, 8, 16, V))).astype(np.int64)
    y = np.floor(np.exp2(6 * rng.random((N, 8, 1, L))) * rng.random((N, 8, 16, L))).astype(np.int64)
    e = rng.integers(1, 4, (N, 8, 1, 1))
    ch = np.minimum(np.floor(V * rng.random((N, 8, 16, V)) ** e).astype(np.int64), V - 1)
    b, a, c = [np.minimum(np.floor(V * rng.random((N, 8, L)) ** e[:, :, 0]).astype(np.int64), V - 1) for i in range(3)]
    th = np.minimum(np.exp2(9 * rng.random((N, 8, 16))).astype(np.int64) - 1, 511)
    return pack(x, ch, b, a, c, y, th)
def setup_inputs_ends(rng):
    x, ch, b, a, c, y, th = parts(rng)
    x = np.where(rng.random((N, 8, 1, V)) < 0.5, 63 * rng.integers(0, 2, (N, 8, 1, V)), 63 * rng.integers(0, 2, x.shape))
    s = rng.integers(0, 2, (N, 8, 1)); s[:, 6:] = 1
    x[..., 0] = 63 * (1 - s); x[..., V - 1] = 63 * s; x[..., V - 2] = 63 * (np.arange(16) % 2)
    y = 63 * rng.integers(0, 2, y.shape); th = 511 * rng.integers(0, 2, th.shape)
    u = rng.random(ch.shape); ch = np.where(u < 0.75, (V - 1) * rng.integers(0, 2, ch.shape), np.where(u < 0.85, V - 2, ch))
    o = []
    for e in (b, a, c):
        u = rng.random(e.shape); o.append(np.where(u < 0.7, (V - 1) * rng.integers(0, 2, e.shape), np.where(u < 0.8, V - 2, e)))
    b, a, c = o
    for k in (3, 14, 15):
        ch[:, 7, k, V - 1] = V - 1; ch[:, 7, k, 0] = 0; ch[:, 7, k, V - 2] = V - 2; th[:, 7, k] = 0
    x[:, 7, :, V - 3] = 0; x[:, 7, 15, V - 3] = 1
    ch[:, 7, 0, V - 1] = V - 1; ch[:, 7, 0, 0] = V - 3; ch[:, 7, 0, V - 2] = V - 2; th[:, 7, 0] = 0
    ch[:, 6, :15, V - 2] = ch[:, 6, :15, 0]
    ch[:, 6, 15, V - 1] = V - 1; ch[:, 6, 15, 0] = 0; ch[:, 6, 15, V - 2] = V - 2; th[:, 6, 15] = 0
    for i in (0, 2, L - 1):
        a[:, 6:, i] = V - 1; b[:, 6:, i] = 0; c[:, 6:, i] = V - 2
    return pack(x, ch, b, a, c, y, th)
def setup_inputs_crowd(rng):
    x, ch, b, a, c, y, th = parts(rng)
    for q in range(N):
        for g in range(8):
            o = rng.permutation(V); mode = (q + g) % 4
            if mode == 3:
                b[q, g], a[q, g], c[q, g] = o[rng.integers(0, 3, (3, L))]; ch[q, g][:, o[:3]] = o[rng.integers(3, 7, (16, 3))]
                continue
            a[q, g] = o[0]; b[q, g] = o[1]; c[q, g] = o[2]
            ch[q, g, :, o[0]] = o[3]; ch[q, g, :, o[1]] = o[4]; ch[q, g, :, o[2]] = o[5]
            x[q, g, :, o[3]] = 63; x[q, g, :, o[4]] = 0; x[q, g, :, o[5]] = 63 * (np.arange(16) % 2)
            j = int(rng.choice(np.array([0, L - 1, L // 2])))
            if mode < 2: th[q, g] = rng.integers(100, 251, 16)
            if mode == 1: c[q, g, j] = o[1]
            if mode == 2:
                th[q, g] = rng.integers(420, 501, 16); ch[q, g, :7, o[2]] = o[4]
                ch[q, g, :, o[6]] = o[5]; ch[q, g, :8, o[6]] = o[4]
                n = int(rng.choice(np.array([1, L // 2, L - 1]))); c[q, g, rng.permutation(L)[:n]] = o[6]
                ch[q, g, :, o[7]] = o[8]; x[q, g, :, o[8]] = 0; b[q, g, j] = o[7]
    return pack(x, ch, b, a, c, y, th)
def setup_inputs_brink(rng):
    x, ch, b, a, c, y, th = parts(rng); h = V // 3; k = h // 2
    for q in range(N):
        for g in range(8):
            o = rng.permutation(V); ca, cb, cc = o[:h], o[h:2 * h], o[2 * h:]
            m = int(rng.integers(5, 15)); th[q, g] = 16 * m
            x[q, g][:, cc] = 31
            sg = np.where(np.argsort(rng.random((16, h)), axis=0) < rng.choice(np.array([7, 8, 9, 10]), h), 1, -1)
            for cls, sign in ((ca, sg), (cb, np.ones((16, h), np.int64))):
                big = np.full((16, h), m); ex = np.where(np.arange(h) < k, 1, rng.integers(-1, 1, h)); big[rng.integers(0, 16, h), np.arange(h)] += ex
                x[q, g][:, cls] = 31 + sign * big
            for cls, cnt in ((ca, (0, 1, 8, 9, 15, 16)), (cb, (16, 16, 16, 8, 9, 15))):
                on = np.argsort(rng.random((16, h)), axis=0) < rng.choice(np.array(cnt), h)
                ch[q, g][:, cls] = np.where(on, cls[rng.integers(0, k, (16, h))], cls[rng.integers(k, h, (16, h))])
            ch[q, g][:, cc] = cc[rng.integers(0, len(cc), (16, len(cc)))]
            a[q, g] = ca[rng.integers(0, h, L)]; b[q, g] = cb[rng.integers(0, h, L)]; c[q, g] = cc[rng.integers(0, len(cc), L)]
            y[q, g] = np.where(rng.random((16, L)) < 0.8, 31 + m, y[q, g])
    return pack(x, ch, b, a, c, y, th)
def setup_inputs_corners(rng):
    x, ch, b, a, c, y, th = parts(rng)
    kind = rng.integers(0, 4, (N, 8, 1, V)); v = np.arange(V)
    ch = np.where(kind == 0, v, np.where(kind == 1, (V - 1) * rng.integers(0, 2, ch.shape), np.where((kind == 3) & (rng.random(ch.shape) < 0.5), v, ch)))
    b = np.where(rng.random(b.shape) < 0.2, (V - 1) * rng.integers(0, 2, b.shape), b)
    a = np.where(rng.random(a.shape) < 0.2, (V - 1) * rng.integers(0, 2, a.shape), a)
    m = rng.integers(0, 7, (N, 8, L)); a = np.where(m < 2, b, a); c = np.where((m == 0) | (m == 2), b, np.where(m == 3, a, c))
    th[:, 0] = 0; th[:, 1] = 511; th[:, 2] = 511 * rng.integers(0, 2, (N, 16))
    x[:, 3] = rng.integers(0, 64, (N, 1, 1)); x[:, 4] = 63 * rng.integers(0, 2, (N, 16, V))
    y = np.where(rng.random((N, 8, 1, L)) < 0.3, 63 * rng.integers(0, 2, (N, 8, 1, L)), y)
    return pack(x, ch, b, a, c, y, th)
def check_inputs(d):
    bad = []
    for k, lo, hi in (("x", 0, 63), ("ch", 0, V - 1), ("sb", 0, V - 1), ("ia", 0, V - 1), ("ic", 0, V - 1), ("y", 0, 63), ("th", 0, 511)):
        v = np.asarray(d[k]).astype(np.float64)
        if not (np.min(v) >= lo and np.max(v) <= hi): bad.append("range of " + k)
        elif np.any(v != np.floor(v)): bad.append("whole numbers of " + k)
    return bad
def pick(s, ix):
    return np.array([[np.take(s[q, g], ix[q, g], axis=1) for g in range(8)] for q in range(N)])
def kids(s, ch):
    return pick(s, ch.reshape(N, 8, 16 * L)).reshape(N, 8, 16, 16, L)
def reference(x, ch, sb, ia, ic, y, th):
    X = np.zeros((N, 8, 16, W), np.int32); C = np.zeros((N, 8, 16, W), np.int32)
    X[..., :V] = x.astype(np.float32).astype(np.int32).reshape(N, 8, 16, V); C[..., :V] = ch.reshape(N, 8, 16, V)
    b, a, c = [np.stack([gentries(e) for e in z]).astype(np.int32) for z in (sb, ia, ic)]
    Y = y.astype(np.float32).astype(np.int32).reshape(N, 8, 16, L); t0 = th.astype(np.int32).reshape(N, 8, 16, 1)
    lane = np.arange(L, dtype=np.int32); slot = np.arange(16)[:, None]; A = np.zeros((N, 8, 1, 1), np.int32)
    for t in range(TV):
        pa, pb, pc = a, b, c; off = np.zeros((N, 8, L), bool)
        for lev in range(LV):
            n = V + (t * LV + lev) * L
            ka, kb, kc = pick(C, pa), pick(C, pb), pick(C, pc)
            xa, xb, xc = kids(X, ka), kids(X, kb), kids(X, kc)
            al = np.add.reduce(np.abs(xa - xc), axis=2) > t0 + A; be = np.add.reduce(np.abs(xb - xc), axis=2) > t0 + A
            dist = np.add.reduce(np.abs(xa - xb), axis=2); vote = np.add.reduce((xa >= xb).astype(np.int32), axis=2) >= 9
            col = al & be
            M = np.where(al & (~be | vote), ka, kb)
            ks = np.argmax(np.where(col | ~np.any(col, axis=2, keepdims=True), dist, -1), axis=2)[:, :, None]
            off = off | (np.add.reduce(col.astype(np.int32), axis=2) >= 9)
            if lev < LV - 1: M = np.where(slot == ks, n + L + lane, M)
            na, nb, nc = [np.take_along_axis(z, ks, 2)[:, :, 0] for z in (ka, kb, kc)]
            new = np.clip(pick(X, pa) + pick(X, pb) - pick(X, pc), 0, 63)
            half = (pick(X, nb) + Y) >> 1
            first = np.argmax(nb[:, :, :, None] == nb[:, :, None, :], axis=3) == lane
            for q in range(N):
                for g in range(8):
                    w = first[q, g]; X[q, g][:, nb[q, g][w]] = half[q, g][:, w]
            X[..., n:n + L] = new; C[..., n:n + L] = M
            pa, pb, pc = na, nb, nc
        n0 = V + t * LV * L; x0 = X[..., n0:n0 + L]
        Y = np.where(off[:, :, None], np.abs(Y - x0), x0)
        c = b; a = np.where(off, a, n0 + lane); b = np.where(off, b, n0 + lane)
        A = np.add.reduce(off.astype(np.int32), axis=2).reshape(N, 8, 1, 1)
        if t < TV - 1: a, c, Y = np.roll(a, H, axis=0), np.roll(c, H, axis=0), np.roll(Y, H, axis=0)
    return {"xo": X.reshape(N, 128, W).astype(np.float32).astype(BF), "co": np.ascontiguousarray(C[..., V:]).reshape(N, 128, W - V).astype(np.float32),
            "so": np.stack([gtable(e) for e in b]).astype(np.float32), "yo": Y.reshape(N, 128, L).astype(np.float32).astype(BF)}

@@ -1,0 +1,581 @@
+import numpy as np
+from concourse.mybir import AluOpType, AxisListType, ActivationFunctionType
+
+V, L, TV, LV = 2048, 256, 4, 2
+XO = 256
+CHUNKS = [(128, 128, [32, -32, 64]), (0, 128, [64, 32, 32])]
+TURNED = True
+LAST_ON_VECTOR = False
+BLK = 32
+PLACE = {"D1": ("DA", 0), "D2": ("DA", 128), "SA": ("DA", 256), "KEY2": ("DA", 384), "D3": ("DB", 0), "KEY": ("DB", 128),
+         "LS": ("Q0", 0), "HS": ("Q0", 128), "MS": ("Q0", 256), "ZB": ("Q1", 0), "OHT": ("Q1", 256), "CLT": ("Q1", 384)}
+
+BF, F16, F32, I32, U16 = "bfloat16", "float16", "float32", "int32", "uint16"
+SCRATCH = {}
+
+
+def _sb(dtype, **kw):
+    for k, n in kw.items():
+        SCRATCH[k] = ("sbuf", [128, n], dtype)
+
+
+_sb(BF, XT=XO + 4096 + 256, BM=4096, E=4096, W=4096, AU=4096, AW=4096, ones=128, tmpb=128, IB=128, IM=128, I2=128, BO=128,
+    Z1=144, ZM=144, SEG=1024, CM=128, AL=256, BE=256, CD=256, ND=256, NV=768, DF=1024, MN=1024, XZ=256, HH=256, OB=256,
+    Y0=256, Y1=256, Y2=256, Y3=256, N0=256, N1=256, N2=256, N3=256, AB=16)
+_sb(F16, R=4096, IH=128, IMH=128, IK=128, I8=128, BOH=128, Z2=144, ZH=144, KF=128, MK=256, C64=32, C128=48,
+    KF2=128, OM=128, THD=512, CL2=256,
+    NEWC=1024, DI=256, DJ=256, PR=1280, OT=256, OH=256, P1=256, P2=256, P3=256)
+_sb(F32, CT=4096, CO=2048, kc=8, k16=8, kf=8, D0=128, mkf=256, mkg=256, ic16=16, GI=16, newf=1024, BIAS=32, NI=64,
+    KT=256, SC=256, LF0=80, LF1=80, Z8=16, kf2=128, TH=32, OF=16, CN=16, AF=64, BFL=80, AN=16, NA=16, XX=16, YL=16, YM=16, AS=8)
+_sb(I32, CH=2048, sbi=16, iai=16, ici=16, thi=8, pi=8, pj=8, eqi=8)
+_sb(U16, K0=768, K1=768, LU0=80, LU1=80, EQL=8, OU=16, YU=16, A0=16, A1=16, A2=16, A3=16, B0=16, B1=16, B2=16, B3=16,
+    C0=16, C1=16, C2=16, C3=16, S0=16, S1=16, S2=16)
+PSUM = {"U0": 1024, "U1": 1024, "DA": 512, "DB": 512, "Q0": 512, "Q1": 512}
+for _k, _n in PSUM.items():
+    SCRATCH[_k] = ("psum", [128, _n], F32)
+WIDTH = {BF: 2, F16: 2, U16: 2, F32: 4, I32: 4}
+
+NLOAD = 11
+SEMAPHORES = (["pe", "dve", "act", "pool", "outs", "outa", "sent"] + ["ld%d" % i for i in range(NLOAD)]
+              + ["r%s%d" % (w, t) for w in "acy" for t in range(1, TV)])
+A = AluOpType
+ACT = ActivationFunctionType
+CYC, PCYC, GAT, SCA = 0.83 * 1.2, 0.42 * 1.2, 1.56, 3.8
+HOP_SAME, HOP_OTHER, SLACK, ROUNDS, TRIES, NOISE = 60.0, 110.0, 20.0, 4, 600, 1500.0
+MAINS = ("BM", "W", "E", "R", "AW", "AU", "U0", "U1")
+LATE = ("NV", "CD", "ND", "P1", "P2", "P3", "CT", "CO", "N0", "N1", "N2", "N3")
+
+
+def build(T, nxt, topo, core):
+    ops, at0 = [], [0, 0]
+
+    def ap(s):
+        if len(s) == 4:
+            return T[s[0]][:, s[1]:s[2]:s[3]]
+        return T[s[0]][:, s[1]:s[2]]
+
+    def cnt(s):
+        return len(range(*s[1:]))
+
+    def two(*ss):
+        return all(WIDTH[SCRATCH[s[0]][2]] == 2 for s in ss)
+
+    def add(q, cost, rd, wr, fn, sem=None, inc=1, lat=0.0, after=None):
+        ops.append({"q": q, "cost": cost, "rd": rd, "wr": wr, "fn": fn, "sem": sem or q, "inc": inc, "lat": lat,
+                    "after": after, "own": sem is not None, "level": at0[1],
+                    "kind": (q, len(ops) - at0[0]) if at0[0] else len(ops)})
+        return len(ops) - 1
+
+    def src(s, off):
+        return ap(s) if off is None else ap(s).indirect(ap(off))
+
+    def vcost(n, f, off=None):
+        return 50 + n * GAT * CYC if off is not None else 25 + max(64, n * f) * CYC
+
+    def sc(x):
+        return ap(x) if isinstance(x, tuple) else x
+
+    def tups(*xs):
+        return [x for x in xs if isinstance(x, tuple)]
+
+    def copy(o, i, off=None):
+        add("dve", vcost(cnt(o), 0.5 if two(o, i) else 1, off), tups(i, off), [o],
+            lambda q: [q.tensor_copy(ap(o), src(i, off))])
+
+    def ts(o, i, s1, op0, s2=None, op1=None, off=None):
+        def fn(q):
+            if op1 is None:
+                return [q.tensor_scalar(ap(o), src(i, off), sc(s1), None, op0)]
+            return [q.tensor_scalar(ap(o), src(i, off), sc(s1), sc(s2), op0, op1)]
+        add("dve", vcost(cnt(o), 0.5 if two(o, i) else 1, off), tups(i, off, s1, s2), [o], fn)
+
+    def tt(o, a, b, op, off=None):
+        f = (1 if a[0] in PSUM or b[0] in PSUM else 2) * (0.5 if two(o, a, b) else 1)
+        add("dve", vcost(cnt(o), f, off), tups(a, b, off), [o],
+            lambda q: [q.tensor_tensor(ap(o), src(a, off), ap(b), op)])
+
+    def scatter_add(win, off, a, b):
+        add("dve", 50 + cnt(a) * SCA * CYC, [off, a, b], [win],
+            lambda q: [q.tensor_tensor(ap(win).indirect(ap(off)), ap(a), ap(b), A.add)])
+
+    def scan(o, d0, d1, op0, op1):
+        add("dve", vcost(cnt(o), 0.5 if two(o, d0, d1) else 1), [d0, d1], [o],
+            lambda q: [q.tensor_tensor_scan(ap(o), ap(d0), ap(d1), 0.0, op0, op1)])
+
+    def turn(o, i):
+        add("dve", vcost(cnt(o), 0.5 if two(o, i) else 1), [i], [o], lambda q: [q.transpose(ap(o), ap(i))])
+
+    def fill(o, v):
+        add("dve", vcost(cnt(o), 0.5 if two(o) else 1), [], [o], lambda q: [q.memset(ap(o), v)])
+
+    def act(o, i, func, bias=None, scale=None, off=None):
+        def fn(q):
+            kw = {}
+            if bias is not None:
+                kw["bias"] = sc(bias)
+            if scale is not None:
+                kw["scale"] = scale
+            return [q.activation(ap(o), src(i, off), func, **kw)]
+        add("act", 65 + cnt(o) * (GAT if off is not None else 1) * CYC, tups(i, off, bias), [o], fn)
+
+    def mm(groups, whole=None):
+        def fn(q):
+            res = []
+            for o, terms in groups:
+                for j, x in enumerate(terms):
+                    ins = q.matmul(ap(x[2] if len(x) == 3 else o), ap(x[0]), ap(x[1]), j == 0, j == len(terms) - 1)
+                res.append(ins)
+            return res
+        cost = 30 + sum((max(64, cnt(x[1])) * PCYC + 4) for o, terms in groups for x in terms)
+        rd = list(set(x[:3] for o, terms in groups for t in terms for x in t[:2]))
+        add("pe", cost, rd, [whole] if whole else [o for o, terms in groups], fn, inc=len(groups))
+
+    def pool(o, rd, n, fn):
+        add("pool", 170 + 2 * n * CYC, rd, [o], fn)
+
+    nload = [0]
+
+    def load(q, o, i, lat):
+        s = "ld%d" % nload[0]
+        nload[0] += 1
+        add(q, 60, [], [o], lambda e: [e.dma_start(ap(o), i)], sem=s, inc=16, lat=lat)
+
+    def store(q, o, i, lat):
+        add(q, 60, [i], [], lambda e: [e.dma_start(o, ap(i))], sem="outs" if q == "sync" else "outa", inc=16, lat=lat)
+
+    eng = topo.engines(core, nxt)
+    ne = 1
+    while ne * 2 <= len(eng):
+        ne *= 2
+    mask = sum(1 << e for e in eng[:ne])
+    rid, pid = topo.addr(nxt)[:2]
+
+    def send(dst, s, sem, lat):
+        def fn(q):
+            q.remote_dma(T[dst][:], T[s][:], T.sem[sem], T.sem["sent"], pid, rid, mask)
+            return []
+        n = SCRATCH[s][1][1]
+        k = add("pool", 300, [(s, 0, n)], [], fn, sem="sent", inc=ne, lat=lat)
+        add("none", 0, [], [(dst, 0, n)], None, sem=sem, inc=ne, after=k)
+
+    load("sync", ("CH", 0, 512), T.ch[:, 0:512], 2500)
+    load("act", ("CH", 512, 1024), T.ch[:, 512:1024], 3000)
+    load("sync", ("sbi", 0, 16), T.sb[:], 2500)
+    load("act", ("ici", 0, 16), T.ic[:], 2500)
+    load("sync", ("CH", 1024, 1536), T.ch[:, 1024:1536], 3500)
+    load("act", ("CH", 1536, 2048), T.ch[:, 1536:2048], 4000)
+    load("sync", ("iai", 0, 16), T.ia[:], 4000)
+    load("act", ("XT", XO, XO + 1024), T.x[:, 0:1024], 4500)
+    load("sync", ("XT", XO + 1024, XO + 2048), T.x[:, 1024:2048], 5000)
+    load("sync", ("thi", 0, 1), T.th[:], 5000)
+    load("sync", ("Y0", 0, 256), T.y[:], 5500)
+
+    full = lambda n: (n, 0, SCRATCH[n][1][1])
+    fill(full("ones"), 1.0)
+    pool(full("IB"), [full("ones")], 128,
+         lambda q: [q.affine_select(T.IB[:], T.ones[:], [[-1, 128]], A.is_equal, 0.0, 0, 1)])
+    pool(full("tmpb"), [full("ones")], 128,
+         lambda q: [q.affine_select(T.tmpb[:], T.ones[:], [[-16, 8], [0, 16]], A.is_ge, 0.0, 0, 1)])
+    pool(full("BO"), [full("tmpb")], 128,
+         lambda q: [q.affine_select(T.BO[:], T.tmpb[:], [[16, 8], [0, 16]], A.is_ge, 0.0, 15, -1)])
+    pool(("pi", 0, 1), [], 1, lambda q: [q.iota(T.pi[:, 0:1], [[0, 1]], 0, 1)])
+    pool(full("eqi"), [], 8, lambda q: [q.iota(T.eqi[:], [[16, 8]], 15, 0)])
+    pool(full("ic16"), [], 16, lambda q: [q.iota(T.ic16[:], [[1, 16]], 0, 0, allow_small_or_imprecise_dtypes=True)])
+    pool(full("mkf"), [], 256,
+         lambda q: [q.iota(T.mkf[:], [[-16, 4], [1, 64]], 0, 0, allow_small_or_imprecise_dtypes=True)])
+    pool(full("newf"), [], 1024,
+         lambda q: [q.iota(T.newf[:], [[512, 4], [1, 256]], 256, 0, allow_small_or_imprecise_dtypes=True)])
+    for name, f in (("IM", -1.0), ("I2", 2.0), ("IH", 1.0), ("IMH", -1.0), ("IK", 1024.0), ("I8", 8.0)):
+        ts(full(name), full("IB"), f, A.mult)
+    copy(full("BOH"), full("BO"))
+    for name, f in (("Z1", 1.0), ("ZM", -1.0), ("Z2", 2.0), ("ZH", 1.0)):
+        fill(full(name), 0.0) if SCRATCH[name][2] == BF else ts(full(name), full("Z1"), f, A.mult)
+        if SCRATCH[name][2] == BF:
+            ts((name, 15, 143, 16), ("BO", 0, 128, 16), f, A.mult)
+    sel = lambda name, k: (name, 15 - k, 143 - k)
+    ts(("pj", 0, 1), ("pi", 0, 1), 15, A.bitwise_and)
+    kc = ("kc", 0, 1)
+    copy(kc, ("pj", 0, 1))
+    ts(("k16", 0, 1), kc, 16.0, A.mult)
+    if not TURNED or any(c[1] != 128 for c in CHUNKS):
+        ts(("kf", 0, 1), kc, -1.0 / 16, A.mult, 15.0 / 16, A.add)
+        ts(full("KF"), full("ones"), ("kf", 0, 1), A.mult)
+    fill(full("D0"), 0.0)
+    fill(("D0", 0, 128, 16), -1.0e5)
+    fill(full("SEG"), 0.0)
+    fill(("SEG", 0, 16 * BLK, BLK), 1.0e12)
+    fill(full("CM"), -160.0)
+    copy(full("EQL"), full("eqi"))
+    ts(full("mkg"), full("mkf"), kc, A.is_ge, 27952.0, A.mult)
+    ts(full("MK"), full("mkg"), 2048.0, A.add)
+    for m in sorted(set(c[1] // 16 for c in CHUNKS)):
+        name = "C%d" % (16 * m)
+        ts((name, 0, m), ("ic16", 0, m), 256.0, A.mult, ("k16", 0, 1), A.add)
+        ts((name, m, 2 * m), ("ones", 0, m), 0.0, A.mult)
+        ts((name, 2 * m, 5 * m), ("ones", 0, 3 * m), 2048.0, A.mult)
+    turned = TURNED and any(c[1] == 128 for c in CHUNKS)
+    plain = not TURNED or any(c[1] != 128 for c in CHUNKS)
+    if turned:
+        pool(full("kf2"), [], 128,
+             lambda q: [q.iota(T.kf2[:], [[0, 8], [-1, 16]], 15, 0, allow_small_or_imprecise_dtypes=True)])
+        ts(full("KF2"), full("kf2"), 1.0 / 16, A.mult)
+        ts(full("OM"), full("ones"), -1.0, A.mult)
+        copy(("TH", 0, 1), ("thi", 0, 1))
+        ts(("THD", 0, 128), full("IH"), ("TH", 0, 1), A.mult)
+    ts(full("GI"), full("ic16"), 16.0, A.mult, kc, A.add)
+    copy(("SEG", BLK - 1, 16 * BLK, BLK), full("GI"))
+    for t in range(TV):
+        ts(("NI", 16 * t, 16 * t + 16), full("GI"), float(V + 512 * t), A.add)
+        copy(("NEWC", 256 * t, 256 * t + 256), ("newf", 256 * t, 256 * t + 256))
+    for j in range(4):
+        ts(("CT", 512 * j, 512 * j + 512), ("CH", 512 * j, 512 * j + 512), -2048.0, A.add)
+    copy(full("B0"), full("sbi"))
+    copy(full("C0"), full("ici"))
+    copy(full("A0"), full("iai"))
+    copy(("BFL", 0, 16), full("sbi"))
+    if plain:
+        ts(("BIAS", 0, 1), ("thi", 0, 1), -256.0, A.mult, -128.0, A.add)
+
+    ub = [0]
+    for t in range(TV):
+        lim = V + 512 * t
+        xw, cw = ("XT", XO, XO + lim), ("CT", 0, lim)
+        Yt, bias = "Y%d" % t, ("BIAS", 8 * t, 8 * t + 1)
+        if t < TV - 1:
+            send("C%d" % (t + 1), "B%d" % t, "rc%d" % (t + 1), 3000)
+            copy(("AF", 16 * t, 16 * t + 16), full("A%d" % t))
+        at0[0] = len(ops)
+        for lev in range(LV):
+            n = lim + 256 * lev
+            at0[1] = 2 * t + lev
+            K, LU, LF = "K%d" % lev, "LU%d" % lev, "LF%d" % lev
+
+            def lst(a, l0, m):
+                if lev == 0:
+                    return ("BAC"[a] + str(t), l0 // 16, (l0 + m) // 16)
+                b = 5 * l0 // 16 + (2 + a) * m // 16
+                return ("LU0", b, b + m // 16)
+
+            def kid(a, l0, m, s0, sm):
+                b = (256 * a + s0) if lev == 0 else (3 * l0 + a * m + s0 - l0)
+                return (K, b, b + sm)
+
+            if lev == 0:
+                for a in (0, 2, 1):
+                    for l0, m in ((128, 128), (0, 128)) if a == 0 else ((0, 256),):
+                        ts((K, 256 * a + l0, 256 * a + l0 + m), cw, 2048.0, A.add, off=lst(a, l0, m))
+                for a in range(3):
+                    act(("NV", 256 * a, 256 * a + 256), xw, ACT.Copy, off=lst(a, 0, 256))
+                mm([(("DB", 256, 512), [(full("IB"), ("NV", 0, 256)), (full("IB"), ("NV", 256, 512)),
+                                        (full("IM"), ("NV", 512, 768))])])
+                ts(("XT", XO + n, XO + n + 256), ("DB", 256, 512), 0.0, A.max, 63.0, A.min)
+            else:
+                n0 = XO + lim
+                mm([(("Q1", 0, 256), [(full("IB"), full(Yt)), (full("IM"), ("XT", n0, n0 + 256))])])
+                act(("XT", XO + 4096, XO + 4352), ("Q1", 0, 256), ACT.Abs)
+            for l0, m, subs in CHUNKS:
+                mc = m // 16
+                col = lambda name, j=0: (name, l0 + j, l0 + j + m)
+                if lev == 1:
+                    b = 5 * l0 // 16 + 2 * mc
+                    ts((K, 3 * l0, 3 * l0 + 3 * m), cw, 2048.0, A.add, off=("LU0", b, b + 3 * mc))
+                    act(("NV", 3 * l0, 3 * l0 + 3 * m), xw, ACT.Copy, off=("LU0", b, b + 3 * mc))
+                    nv = lambda a: ("NV", 3 * l0 + a * m, 3 * l0 + a * m + m)
+                    o = ("DB", 256 + l0, 256 + l0 + m)
+                    mm([(o, [(full("IB"), nv(0)), (full("IB"), nv(1)), (full("IM"), nv(2))])])
+                    ts(("XT", XO + n + l0, XO + n + l0 + m), o, 0.0, A.max, 63.0, A.min)
+                s0 = l0
+                for sm in subs:
+                    both, sm = sm < 0, abs(sm)
+                    big = lambda name: (name, 16 * s0, 16 * (s0 + sm))
+                    part = lambda name, j: (name, 16 * s0 + j, 16 * s0 + j + 512)
+                    act(big("BM"), xw, ACT.Copy, off=kid(0, l0, m, s0, sm))
+                    if both:
+                        act(big("W"), xw, ACT.Copy, off=kid(2, l0, m, s0, sm))
+                        U = "U%d" % (ub[0] % 2)
+                        ub[0] += 1
+                        mm([((U, j, j + 512), [(full("IB"), part("W", j)), (full("IM"), part("BM", j))])
+                            for j in range(0, 16 * sm, 512)])
+                        act(big("AW"), (U, 0, 16 * sm), ACT.Abs)
+                    else:
+                        tt(big("W"), xw, big("BM"), A.subtract, off=kid(2, l0, m, s0, sm))
+                        act(big("AW"), big("W"), ACT.Abs)
+                    tt(big("E"), xw, big("BM"), A.subtract, off=kid(1, l0, m, s0, sm))
+                    ts(big("R"), big("E"), 1.0 / 64 - 32, A.add, -32.0, A.max)
+                    U = "U%d" % (ub[0] % 2)
+                    ub[0] += 1
+                    mm([((U, j, j + 512), [(full("IB"), part("E", j)), (full("IM"), part("W", j))]
+                         + ([(full("IB"), part("BM", j))] if both else [])) for j in range(0, 16 * sm, 512)])
+                    act(big("AU"), (U, 0, 16 * sm), ACT.Abs)
+                    s0 += sm
+                ps = lambda name, a=0, b=m: (PLACE[name][0], PLACE[name][1] + a, PLACE[name][1] + b)
+                D1, D2, D3, SA, KEY, HS, MS = [ps(x) for x in ("D1", "D2", "D3", "SA", "KEY", "HS", "MS")]
+                pr = lambda j: ("PR", 5 * l0 + j * m, 5 * l0 + j * m + m)
+                lanes = m == 128 and TURNED
+                if lanes:
+                    slot = lambda name, k: (name, 16 * l0 + k, 16 * (l0 + m), 16)
+                    grp = lambda name: (name, 15, 143, 16)
+                    at = lambda d, k: (d[0], d[1] + k, d[2], 16)
+                    mm([(at(D3, k), [(slot("E", k), grp("ZM")), (slot("R", k), grp("Z2"))]) for k in range(16)], whole=D3)
+                    for d, x in ((D2, "AW"), (D1, "AU")):
+                        mm([(d, [(full("OM"), ("THD", 128 * t, 128 * t + 128))]
+                             + [(slot(x, k), grp("Z1"), at(d, k)) for k in range(16)])])
+                else:
+                    for h, w in ((0, 64), (64, 64)) if m == 128 else ((0, m),):
+                        slot = lambda name, k: (name, 16 * (l0 + h) + k, 16 * (l0 + h + w), 16)
+                        mm([(ps("D3", h, h + w), [(sel("ZM", k), slot("E", k)) for k in range(16)]
+                             + [(sel("Z2", k), slot("R", k)) for k in range(16)])])
+                        mm([(ps("D2", h, h + w), [(sel("Z1", k), slot("AW", k)) for k in range(16)])])
+                        mm([(ps("D1", h, h + w), [(sel("Z1", k), slot("AU", k)) for k in range(16)])])
+                act(col("BE"), D2, ACT.Sigmoid, bias=-128.0 if lanes else bias, scale=256.0)
+                act(col("AL"), D1, ACT.Sigmoid, bias=-128.0 if lanes else bias, scale=256.0)
+                ts(col("DI"), D3, -1016.25, A.add)
+                ts(col("DJ"), D3, -1016.0 + 15.0 / 64, A.add)
+                if lanes:
+                    OH = col("OB")
+                    tt(col("CL2"), col("AL"), col("BE"), A.mult)
+                    terms = [(full("IH"), col("DI")), (full("IH"), full("KF2")), (full("IK"), col("CL2"))]
+                    mm([(KEY, terms)])
+                    mm([(ps("KEY2"), terms)])
+                    act(col("KT"), ps("KEY2"), ACT.Copy)
+                    scan(col("SC"), ("D0", 0, m), KEY, A.add, A.max)
+                    tt(col("OT"), col("SC"), col("KT"), A.is_equal, off=("EQL", 0, mc))
+                    mm([(ps("OHT"), [(col("OT"), full("IH"))])])
+                    act(OH, ps("OHT"), ACT.Copy)
+                    mm([(ps("CLT"), [(col("CL2"), full("IH"))])])
+                    copy(pr(1), ps("CLT"))
+                else:
+                    OH = col("OH")
+                    tt(pr(1), col("AL"), col("BE"), A.mult)
+                    mm([(KEY, [(full("IH"), col("DI")), (full("IH"), ("KF", 0, m)), (full("IK"), pr(1))])])
+                    turn(col("KT"), KEY)
+                    scan(col("SC"), ("D0", 0, m), col("KT"), A.add, A.max)
+                    tt(col("OT"), col("SC"), col("KT"), A.is_equal, off=("EQL", 0, mc))
+                    turn(OH, col("OT"))
+                tt(pr(2), cw, OH, A.mult, off=lst(0, l0, m))
+                ts(pr(0), OH, kc, A.mult)
+                na = 5 if lev == 0 else 3
+                if lev == 0:
+                    tt(pr(3), cw, OH, A.mult, off=lst(1, l0, m))
+                    tt(pr(4), cw, OH, A.mult, off=lst(2, l0, m))
+                LS = ps("LS", 0, na * mc)
+                mm([(LS, [(sel("ZH", r), ("PR", 5 * l0 + r, 5 * l0 + na * m, 16)) for r in range(16)]
+                     + [(full("IH"), ("C%d" % m, 0, na * mc))])])
+                lb = 5 * l0 // 16
+                copy((LU, lb, lb + na * mc), LS)
+                z8 = lambda c: ("Z8", l0 // 16 + c, l0 // 16 + c + 1)
+                gl = lambda name, j=0: (name, l0 // 16 + j, l0 // 16 + j + mc)
+                if l0 or not LAST_ON_VECTOR:
+                    act(gl("Z8"), ps("LS", 2 * mc, 3 * mc), ACT.Identity, scale=8192.0)
+                act((LF, lb + mc, lb + 3 * mc), ps("LS", mc, 3 * mc), ACT.Identity, bias=float(XO))
+                qb, bc = 5 * l0 + 2 * m, BLK // 16
+                mm([(ps("ZB", BLK * c, BLK * c + BLK), [(full("BOH"), ("PR", qb + BLK * (c // bc), qb + BLK * (c // bc) + BLK)),
+                                                        (full("IH"), ("MK", 64 * (c % bc), 64 * (c % bc) + BLK))])
+                    for c in range(mc)])
+                for c in range(mc):
+                    o, i = ("DF", bc * l0 + BLK * c, bc * l0 + BLK * c + BLK), ps("ZB", BLK * c, BLK * c + BLK)
+                    if l0 == 0 and LAST_ON_VECTOR:
+                        ts(o, i, ps("LS", 2 * mc + c, 2 * mc + c + 1), A.not_equal, 8192.0, A.mult)
+                    else:
+                        act(o, i, ACT.Abs, bias=z8(c), scale=-8192.0)
+                wide = lambda name: (name, bc * l0, bc * (l0 + m))
+                scan(wide("MN"), wide("SEG"), wide("DF"), A.add, A.min)
+                tt(gl("OF"), ("MN", bc * l0 + BLK - 1, bc * (l0 + m), BLK), (LF, lb + 2 * mc, lb + 3 * mc), A.min)
+                copy(gl("OU"), gl("OF"))
+                act(col("XZ"), ("BM", 16 * l0, 16 * (l0 + m)), ACT.Copy, off=(LU, lb, lb + mc))
+                mm([(HS, [(full("IB"), col(Yt)), (full("IB"), col("XZ"))])])
+                act(col("HH"), HS, ACT.Identity, bias=159.75, scale=0.5)
+                base = [(full("I2"), col("AL")), (full("IM"), col("BE")), (full("IH"), col("DJ")), (full("IMH"), col("DI"))]
+                if lev == 0:
+                    base.append((full("I8"), col("OT") if lanes else OH))
+                    tt(col("P3"), OH, col("NEWC", 256 * t), A.mult)
+                mm([(SA, [(r, l) for l, r in base] if lanes else base)])
+                act(col("CD"), SA, ACT.Sigmoid, bias=-384.0, scale=256.0)
+                act(col("ND"), SA, ACT.Sigmoid, bias=384.0, scale=-256.0)
+                tt(col("P1"), cw, col("CD"), A.mult, off=lst(1, l0, m))
+                tt(col("P2"), cw, col("ND"), A.mult, off=lst(0, l0, m))
+                mm([(MS, [(full("IH"), col("P1")), (full("IH"), col("P2"))]
+                     + ([(full("IH"), col("P3")), (full("IMH"), pr(3))] if lev == 0 else []))])
+                if t < TV - 1:
+                    act(col("CT", n), MS, ACT.Copy)
+                else:
+                    at0[0] -= 1
+                act(col("CO", n - V), MS, ACT.Identity, bias=2048.0)
+                if lev == 1:
+                    tt(gl("CN"), ("LF0", lb + mc, lb + 2 * mc), ("LF1", lb + mc, lb + 2 * mc), A.max)
+            for l0, m, subs in CHUNKS:
+                for b0 in range(l0 + m - BLK, l0 - 1, -BLK):
+                    scatter_add(("XT", 0, XO + lim), ("OU", b0 // 16, (b0 + BLK) // 16), ("HH", b0, b0 + BLK), ("CM", 0, BLK))
+            store("sync", T.co[:, n - V:n - V + 256], ("CO", n - V, n - V + 256), 2500)
+        ni = ("NI", 16 * t, 16 * t + 16)
+        ts(full("NA"), full("CN"), XO + 9.0, A.is_lt)
+        tt(full("XX"), full("NA"), ni, A.mult)
+        bn = ("BFL", 16 * t + 16, 16 * t + 32)
+        tt(bn, ("BFL", 16 * t, 16 * t + 16), full("XX"), A.max)
+        if t < TV - 1:
+            copy(full("B%d" % (t + 1)), bn)
+            tt(full("AN"), ("AF", 16 * t, 16 * t + 16), full("XX"), A.max)
+            copy(full("S%d" % t), full("AN"))
+            send("A%d" % (t + 1), "S%d" % t, "ra%d" % (t + 1), 3000)
+            ts(full("AB"), full("CN"), XO + 9.0, A.is_ge)
+            mm([(("Q0", 448, 464), [(full("BO"), full("AB"))])])
+            add("dve", vcost(16, 1), [("Q0", 448, 464)], [("AS", 0, 1)],
+                lambda q: [q.tensor_reduce(T.AS[:, 0:1], T.Q0[:, 448:464], AxisListType.X, A.add)])
+            if plain:
+                ts(("BIAS", 8 * t + 8, 8 * t + 9), ("AS", 0, 1), -256.0, A.mult, ("BIAS", 0, 1), A.add)
+            if turned:
+                tt(("TH", 8 * t + 8, 8 * t + 9), ("AS", 0, 1), ("TH", 0, 1), A.add)
+                ts(("THD", 128 * t + 128, 128 * t + 256), full("IH"), ("TH", 8 * t + 8, 8 * t + 9), A.mult)
+        ts(full("YM"), full("CN"), XO + 9.0, A.is_ge, float(4096 - lim), A.mult)
+        tt(full("YL"), full("YM"), full("GI"), A.add)
+        copy(full("YU"), full("YL"))
+        act(full("N%d" % t), ("XT", XO + lim, XO + 4352), ACT.Copy, off=full("YU"))
+        if t < TV - 1:
+            send("Y%d" % (t + 1), "N%d" % t, "ry%d" % (t + 1), 3500)
+    store("sync", T.xo[:, 3584:4096], ("XT", XO + 3584, XO + 4096), 2500)
+    store("sync", T.so[:], ("BFL", 64, 80), 2500)
+    store("sync", T.yo[:], full("N3"), 2500)
+    store("sync", T.xo[:, 0:1792], ("XT", XO, XO + 1792), 4000)
+    store("act", T.xo[:, 1792:3584], ("XT", XO + 1792, XO + 3584), 4000)
+    return ops
+
+
+def plan(ops):
+    n = len(ops)
+    deps = [set() for _ in range(n)]
+    hist = {}
+    for i, o in enumerate(ops):
+        for wr, ss in ((False, o["rd"]), (True, o["wr"])):
+            for s in ss:
+                for j, w2, a, b in hist.get(s[0], []):
+                    if j != i and (wr or w2) and a < s[2] and s[1] < b:
+                        deps[i].add(j)
+        for s in o["wr"]:
+            hist[s[0]] = [h for h in hist.get(s[0], []) if not (s[1] <= h[2] and h[3] <= s[2] and len(s) == 3)]
+        for wr, ss in ((False, o["rd"]), (True, o["wr"])):
+            for s in ss:
+                hist.setdefault(s[0], []).append((i, wr, s[1], s[2]))
+        if o["after"] is not None:
+            deps[i].add(o["after"])
+        o["banks"] = set((s[0], b) for s in o["rd"] + o["wr"] if s[0] in PSUM for b in range(s[1] // 512, (s[2] - 1) // 512 + 1))
+    succ = [[] for _ in range(n)]
+    for i in range(n):
+        for j in deps[i]:
+            succ[j].append(i)
+
+    def hop(j, i):
+        if ops[j]["q"] == ops[i]["q"]:
+            return ops[j]["lat"] + (0.0 if ops[i]["q"] == "pe" else HOP_SAME)
+        return ops[j]["lat"] + HOP_OTHER
+
+    def run(pre, post, prio, back):
+        left = [len(d) for d in pre]
+        ready = {}
+        for i in range(n):
+            if left[i] == 0:
+                ready.setdefault(ops[i]["q"], []).append(i)
+        est = [ops[i]["lat"] if back else 0.0 for i in range(n)]
+        fin = [0.0] * n
+        free, bank, order, extra = {}, {}, [], [set() for _ in range(n)]
+        for _ in range(n):
+            best = None
+            for q, rs in ready.items():
+                if not rs:
+                    continue
+                cand = []
+                for i in rs:
+                    s = max(est[i], free.get(q, 0.0))
+                    for b in ops[i]["banks"]:
+                        for q2, j in bank.get(b, {}).items():
+                            if q2 != q:
+                                s = max(s, fin[j] + HOP_OTHER)
+                    cand.append((s, i))
+                s0 = min(cand)[0]
+                if best is None or s0 < best[0]:
+                    best = (s0, cand)
+            s, i = max((c for c in best[1] if c[0] <= best[0] + SLACK), key=lambda c: prio[c[1]])
+            o = ops[i]
+            for b in o["banks"]:
+                for q2, j in bank.get(b, {}).items():
+                    if q2 != o["q"]:
+                        extra[i].add(j)
+                bank.setdefault(b, {})[o["q"]] = i
+            free[o["q"]] = fin[i] = s + o["cost"]
+            order.append(i)
+            ready[o["q"]].remove(i)
+            for k in post[i]:
+                est[k] = max(est[k], fin[i] + (hop(k, i) if back else hop(i, k)))
+                left[k] -= 1
+                if left[k] == 0:
+                    ready.setdefault(ops[k]["q"], []).append(k)
+        return max(fin[i] + (0.0 if back else ops[i]["lat"]) for i in range(n)), order, extra, fin
+
+    prio = [0.0] * n
+    for i in range(n - 1, -1, -1):
+        prio[i] = ops[i]["cost"] + max([prio[k] + hop(i, k) for k in succ[i]] or [ops[i]["lat"]])
+    for i, o in enumerate(ops):
+        w = o["wr"][0][0] if o["wr"] else ""
+        if o["kind"] != i:
+            prio[i] = -1e6 * (o["level"] + (0.3 if w in MAINS else 0.6 if w in LATE else 0.0)) - i
+    best = None
+    rng = np.random.RandomState(1)
+    for it in range(ROUNDS):
+        res = run(deps, succ, prio, False)
+        if best is None or res[0] < best[0]:
+            best = res
+        prio = run(succ, deps, res[3], True)[3]
+    kinds = {}
+    for i, o in enumerate(ops):
+        kinds.setdefault(o["kind"], []).append(i)
+    kinds = [v for v in kinds.values() if len(v) > 2]
+    for it in range(TRIES):
+        prio = [ops[i]["cost"] - best[3][i] for i in range(n)]
+        for _ in range(1 + it % 2):
+            d = float(rng.randn()) * NOISE
+            for i in kinds[int(rng.randint(len(kinds)))]:
+                prio[i] += d
+        res = run(deps, succ, prio, False)
+        if res[0] <= best[0]:
+            best = res
+    busy = {}
+    for i in range(n):
+        deps[i] |= best[2][i]
+        ops[i]["t0"] = best[3][i] - ops[i]["cost"]
+        busy[ops[i]["q"]] = busy.get(ops[i]["q"], 0.0) + ops[i]["cost"]
+    return best[1], deps, best[0], busy
+
+
+PLAN = {}
+
+
+def rank_program(g, core, T, topo):
+    rank = T.rank_of(core)
+    if rank is None:
+        return
+    ops = build(T, T.cores[(rank + 1) % len(T.cores)], topo, core)
+    if "p" not in PLAN:
+        PLAN["p"] = plan(ops)
+    order, deps = PLAN["p"][:2]
+    queues = {"pe": g.tensor, "dve": g.vector, "act": g.scalar, "pool": g, "sync": g.sync}
+    total, mark, seen = {}, {}, {}
+    for i in order:
+        o = ops[i]
+        total[o["sem"]] = total.get(o["sem"], 0) + o["inc"]
+        mark[i] = total[o["sem"]]
+        if o["q"] == "none":
+            continue
+        need = {}
+        for j in deps[i]:
+            p = ops[j]
+            if p["q"] == "pe" and o["q"] == "pe":
+                continue
+            need[p["sem"]] = max(need.get(p["sem"], 0), mark[j])
+        q = queues[o["q"]]
+        for s, v in sorted(need.items()):
+            if seen.get((o["q"], s), 0) < v:
+                q.wait_ge(T.sem[s], v)
+                seen[(o["q"], s)] = v
+        for ins in o["fn"](q):
+            ins.then_inc(T.sem[o["sem"]], o["inc"] if o["own"] else 1)
+    for s in ("pe", "dve", "act", "pool", "sent", "outs", "outa"):
+        g.wait_ge(T.sem[s], total[s])

@@ -1,70 +1,108 @@
 import numpy as np
 from concourse.mybir import AluOpType, AxisListType, ActivationFunctionType
+from concourse.bass import DstId, RemoteDMATransfer
 
 V, L, TV, LV = 2048, 256, 4, 2
-XO = 256
-CHUNKS = [(128, 128, [32, -32, 64]), (0, 128, [64, 32, 32])]
-TURNED = True
-LAST_ON_VECTOR = False
+XO = 512
+PIECES = {1: [("G", 16, "stq"), ("G", 48, "st"), ("G", 64, "st")], 0: [("G", 64, "st"), ("G", 32, "st"), ("G", 32, "st")]}
+SUMS = {1: [(0, 128)], 0: [(0, 128)]}
+TAIL_ON_VECTOR = ()
+ON_SCALAR = ("KU00", "KU01", "KU10", "KU11", "LU", "CS")
+MAIN = 0.3
+LATE = 0.6
+TAIL = [0.0, 0.0]
+PE_RUN = 8
 BLK = 32
-PLACE = {"D1": ("DA", 0), "D2": ("DA", 128), "SA": ("DA", 256), "KEY2": ("DA", 384), "D3": ("DB", 0), "KEY": ("DB", 128),
-         "LS": ("Q0", 0), "HS": ("Q0", 128), "MS": ("Q0", 256), "ZB": ("Q1", 0), "OHT": ("Q1", 256), "CLT": ("Q1", 384)}
+PAIRS = {"MR_": "QR", "MQ": "PQ", "MP": "PR"}
+JOBS, NF, NT, SIZES = [], {}, {}, {}
+for _c in (1, 0):
+    _s = 128
+    for _k, _m, _h in PIECES[_c]:
+        _s -= _m
+        JOBS += [(_c, o, _s, _m) for o in (PAIRS if _k == "F" else [x for x, h in zip(("MR_", "MP"), _h) if h == "f"])]
+    NF[_c] = sum(m for k, m, h in PIECES[_c] if k == "F")
+    NT[_c] = sum(m for k, m, h in PIECES[_c] if k == "G" and h[1] == "t")
+    SIZES[_c] = all(k == "G" and h[:2] in ("st", "bt") for k, m, h in PIECES[_c])
 
 BF, F16, F32, I32, U16 = "bfloat16", "float16", "float32", "int32", "uint16"
-SCRATCH = {}
-
-
-def _sb(dtype, **kw):
-    for k, n in kw.items():
-        SCRATCH[k] = ("sbuf", [128, n], dtype)
-
-
-_sb(BF, XT=XO + 4096 + 256, BM=4096, E=4096, W=4096, AU=4096, AW=4096, ones=128, tmpb=128, IB=128, IM=128, I2=128, BO=128,
-    Z1=144, ZM=144, SEG=1024, CM=128, AL=256, BE=256, CD=256, ND=256, NV=768, DF=1024, MN=1024, XZ=256, HH=256, OB=256,
-    Y0=256, Y1=256, Y2=256, Y3=256, N0=256, N1=256, N2=256, N3=256, AB=16)
-_sb(F16, R=4096, IH=128, IMH=128, IK=128, I8=128, BOH=128, Z2=144, ZH=144, KF=128, MK=256, C64=32, C128=48,
-    KF2=128, OM=128, THD=512, CL2=256,
-    NEWC=1024, DI=256, DJ=256, PR=1280, OT=256, OH=256, P1=256, P2=256, P3=256)
-_sb(F32, CT=4096, CO=2048, kc=8, k16=8, kf=8, D0=128, mkf=256, mkg=256, ic16=16, GI=16, newf=1024, BIAS=32, NI=64,
-    KT=256, SC=256, LF0=80, LF1=80, Z8=16, kf2=128, TH=32, OF=16, CN=16, AF=64, BFL=80, AN=16, NA=16, XX=16, YL=16, YM=16, AS=8)
-_sb(I32, CH=2048, sbi=16, iai=16, ici=16, thi=8, pi=8, pj=8, eqi=8)
-_sb(U16, K0=768, K1=768, LU0=80, LU1=80, EQL=8, OU=16, YU=16, A0=16, A1=16, A2=16, A3=16, B0=16, B1=16, B2=16, B3=16,
-    C0=16, C1=16, C2=16, C3=16, S0=16, S1=16, S2=16)
-PSUM = {"U0": 1024, "U1": 1024, "DA": 512, "DB": 512, "Q0": 512, "Q1": 512}
-for _k, _n in PSUM.items():
-    SCRATCH[_k] = ("psum", [128, _n], F32)
 WIDTH = {BF: 2, F16: 2, U16: 2, F32: 4, I32: 4}
+ARENA = {BF: "SB", F16: "SH", F32: "SF", I32: "SI", U16: "SU"}
+TILE, USED = {}, {}
 
-NLOAD = 11
-SEMAPHORES = (["pe", "dve", "act", "pool", "outs", "outa", "sent"] + ["ld%d" % i for i in range(NLOAD)]
-              + ["r%s%d" % (w, t) for w in "acy" for t in range(1, TV)])
+
+def _sb(dtype, tags, **kw):
+    for tag in tags:
+        for k, n in kw.items():
+            a = USED.get(dtype, 0)
+            TILE[k + tag] = (ARENA[dtype], a, a + n)
+            USED[dtype] = a + (n + 15) // 16 * 16
+
+
+_sb(BF, [""], ONE=512, TMP=128, IB=128, IBM=128, IB2K=128, IB8K=128, BO=128, SELT=2048, SEG=256, RST=128, CM=32, GI=16, BASE=64,
+    ZB=144, XT=XO + 4096, Y=1024, N=1024, YM=256, AB=16, NV0=768)
+_sb(F16, [""], IH=128, IHM=128, C0=128, OM=128, ONK=128, BOH=256, BOM=128, WS=160, ZH=144, MR=128, IND=256, MK=256, DG=1024,
+    TH3=384, THA=256, CB0=128, CB1=128)
+_sb(F32, [""], kc=1, pd=1, TH=1, CBF=256, T1=256, T2=256, T3=256, T4=16, T5=16, DGS=1024, CT=4096, FB=160, CS=16, CN=16, AS=1)
+_sb(I32, [""], thi=1, pi=1, pj=1, pk=1, eqi=8, CH=2048, LI=48)
+_sb(U16, [""], EQL=8, SS=112, LA=128)
+_sb(F16, "01", P=2048, Q=2048, R=2048, MQ=2048, MR_=2048, MP=2048, QT=2048)
+_sb(BF, "01", NV1=384)
+TWO = ["00", "01", "10", "11"]
+_sb(BF, TWO, DF=256, MN=256, XZ=128, HH=128)
+_sb(F16, TWO, K=384, NB=256, PR=512, NC=128, DI=128, HI=128, X=128, N2=128, NW=128, F=128, E=144, ZM=128, OF=8, PD=256)
+_sb(F32, TWO, FM=8)
+_sb(U16, TWO, KU=384, LU=24, OU=8)
+SCRATCH = {ARENA[d]: ("sbuf", [128, n], d) for d, n in USED.items()}
+PLACE = {"D": ("A", 0), "U": ("E", 0), "DIFF": ("B", 0), "NT": ("B", 256), "ABP": ("B", 0), "YD": ("B", 256),
+         "OHQ": ("C", 0), "ZB": ("C", 128), "NS": ("C", 0), "LS": ("C", 256), "VV": ("C", 304), "CLT": ("C", 384),
+         "NVP": ("B", 256), "HS": ("A", 384), "MS": ("B", 256), "OHP": ("A", 0)}
+PSUM = [b + s for b in "ABCE" for s in "01"]
+for _k in PSUM:
+    SCRATCH[_k] = ("psum", [128, 512], F32)
+
+SEMAPHORES = (["pe", "dve", "act", "pool", "outs", "sent", "back", "lc0", "lc1", "lli", "lx0", "lx1", "lth", "ly"]
+              + ["r%s%d" % (w, t) for w in "acy" for t in range(1, TV)]
+              + ["f%s%d" % (w, j) for w in "abs" for j in range(len(JOBS))])
 A = AluOpType
 ACT = ActivationFunctionType
-CYC, PCYC, GAT, SCA = 0.83 * 1.2, 0.42 * 1.2, 1.56, 3.8
-HOP_SAME, HOP_OTHER, SLACK, ROUNDS, TRIES, NOISE = 60.0, 110.0, 20.0, 4, 600, 1500.0
-MAINS = ("BM", "W", "E", "R", "AW", "AU", "U0", "U1")
-LATE = ("NV", "CD", "ND", "P1", "P2", "P3", "CT", "CO", "N0", "N1", "N2", "N3")
+CYC, PCYC, GAT, SCA = 0.83 * 1.08, 0.42 * 1.08, 1.56, 3.8
+HOP_SAME, HOP_OTHER, LONGEST, ROUNDS, TRIES, NOISE = 60.0, 110.0, 4000.0, 25, 200, 1200.0
+CALL, FLY, FOLD_RATE, BACK_RATE = 900.0, 2000.0, 120.0, 240.0
+
+
+def helper_of(topo, cores, core, j):
+    free = [c for c in topo.cores_of(core) if c not in cores and topo.die(c) == topo.die(core)]
+    return free[j % len(free)]
 
 
 def build(T, nxt, topo, core):
-    ops, at0 = [], [0, 0]
+    ops, now = [], {"part": None, "from": 0, "level": -1, "class": 0.0}
+
+    def tl(name, a=None, b=None, step=None, rows=None):
+        buf, o, e = TILE[name]
+        a, b = (0, e - o) if a is None else (a, b)
+        return (buf, o + a, o + b, step or 1) + (rows or (0, 128))
 
     def ap(s):
-        if len(s) == 4:
-            return T[s[0]][:, s[1]:s[2]:s[3]]
-        return T[s[0]][:, s[1]:s[2]]
+        return T[s[0]][s[4]:s[5], s[1]:s[2]:s[3]] if s[3] > 1 else T[s[0]][s[4]:s[5], s[1]:s[2]]
+
+    def sub(s, a, b, step=1, rows=None):
+        return (s[0], s[1] + a, s[1] + b, step) + (rows or s[4:])
 
     def cnt(s):
-        return len(range(*s[1:]))
+        return len(range(s[1], s[2], s[3]))
 
     def two(*ss):
         return all(WIDTH[SCRATCH[s[0]][2]] == 2 for s in ss)
 
-    def add(q, cost, rd, wr, fn, sem=None, inc=1, lat=0.0, after=None):
-        ops.append({"q": q, "cost": cost, "rd": rd, "wr": wr, "fn": fn, "sem": sem or q, "inc": inc, "lat": lat,
-                    "after": after, "own": sem is not None, "level": at0[1],
-                    "kind": (q, len(ops) - at0[0]) if at0[0] else len(ops)})
+    def add(q, cost, rd, wr, fn, sem="", inc=1, lat=0.0, after=None, soft=None):
+        ops.append({"q": q, "cost": cost, "rd": rd, "wr": wr, "fn": fn, "sem": q if sem == "" else sem, "inc": inc, "lat": lat,
+                    "after": after, "soft": soft, "own": sem != "", "level": now["level"], "class": now["class"],
+                    "kind": (now["part"], len(ops) - now["from"]) if now["part"] else len(ops)})
         return len(ops) - 1
+
+    def part(name):
+        now["part"], now["from"] = name, len(ops)
 
     def src(s, off):
         return ap(s) if off is None else ap(s).indirect(ap(off))
@@ -102,341 +140,396 @@ def build(T, nxt, topo, core):
         add("dve", vcost(cnt(o), 0.5 if two(o, d0, d1) else 1), [d0, d1], [o],
             lambda q: [q.tensor_tensor_scan(ap(o), ap(d0), ap(d1), 0.0, op0, op1)])
 
-    def turn(o, i):
-        add("dve", vcost(cnt(o), 0.5 if two(o, i) else 1), [i], [o], lambda q: [q.transpose(ap(o), ap(i))])
-
     def fill(o, v):
         add("dve", vcost(cnt(o), 0.5 if two(o) else 1), [], [o], lambda q: [q.memset(ap(o), v)])
 
-    def act(o, i, func, bias=None, scale=None, off=None):
+    def act(o, i, func, bias=None, scale=None, off=None, accum=None):
         def fn(q):
             kw = {}
             if bias is not None:
                 kw["bias"] = sc(bias)
             if scale is not None:
                 kw["scale"] = scale
+            if accum is not None:
+                kw["accum_out"] = ap(accum)
             return [q.activation(ap(o), src(i, off), func, **kw)]
-        add("act", 65 + cnt(o) * (GAT if off is not None else 1) * CYC, tups(i, off, bias), [o], fn)
+        add("act", 65 + cnt(o) * (GAT if off is not None else 1) * CYC, tups(i, off, bias), tups(o, accum), fn)
 
-    def mm(groups, whole=None):
+    def plus(name, o, i, x=0.0, off=None):
+        if name in ON_SCALAR:
+            act(o, i, ACT.Identity if x else ACT.Copy, bias=x or None, off=off)
+        elif x:
+            ts(o, i, x, A.add, off=off)
+        else:
+            copy(o, i, off=off)
+
+    def mm(o, terms, start=True, stop=True, each=False):
         def fn(q):
-            res = []
-            for o, terms in groups:
-                for j, x in enumerate(terms):
-                    ins = q.matmul(ap(x[2] if len(x) == 3 else o), ap(x[0]), ap(x[1]), j == 0, j == len(terms) - 1)
-                res.append(ins)
-            return res
-        cost = 30 + sum((max(64, cnt(x[1])) * PCYC + 4) for o, terms in groups for x in terms)
-        rd = list(set(x[:3] for o, terms in groups for t in terms for x in t[:2]))
-        add("pe", cost, rd, [whole] if whole else [o for o, terms in groups], fn, inc=len(groups))
+            for j, x in enumerate(terms):
+                ins = q.matmul(ap(x[2] if len(x) == 3 else o), ap(x[0]), ap(x[1]), each or (start and j == 0),
+                               each or (stop and j == len(terms) - 1))
+            return [ins]
+        cost = 30 + sum(max(min(64, cnt(x[0])), cnt(x[1])) * PCYC + 4 for x in terms)
+        rd = list(set(x[:3] + (1, 0, 128) for t in terms for x in t[:2]))
+        if not (start or stop):
+            add("pe", cost, rd + [o], [], fn)
+        else:
+            add("pe", cost, rd, [o if start and stop else (o[0], 0, 512, 1, 0, 128)], fn)
 
-    def pool(o, rd, n, fn):
-        add("pool", 170 + 2 * n * CYC, rd, [o], fn)
+    def pool(o, rd, fn):
+        add("pool", 170 + 2 * cnt(o) * CYC, rd, [o], fn)
 
-    nload = [0]
+    def iota(o, pattern, base, cm):
+        if SCRATCH[o[0]][2] == I32:
+            pool(o, [], lambda q: [q.iota(ap(o), pattern, base, cm)])
+        else:
+            pool(o, [], lambda q: [q.iota(ap(o), pattern, base, cm, allow_small_or_imprecise_dtypes=True)])
 
-    def load(q, o, i, lat):
-        s = "ld%d" % nload[0]
-        nload[0] += 1
-        add(q, 60, [], [o], lambda e: [e.dma_start(ap(o), i)], sem=s, inc=16, lat=lat)
+    def select(o, i, pattern, op, base, cm):
+        pool(o, [i], lambda q: [q.affine_select(ap(o), ap(i), pattern, op, 0.0, base, cm)])
 
-    def store(q, o, i, lat):
-        add(q, 60, [i], [], lambda e: [e.dma_start(o, ap(i))], sem="outs" if q == "sync" else "outa", inc=16, lat=lat)
+    last = {}
+
+    def load(q, sem, pairs, lat):
+        last[q] = add(q, 60 * len(pairs), [], [o for o, i in pairs], lambda e: [e.dma_start(ap(o), i) for o, i in pairs],
+                      sem=sem, inc=16 * len(pairs), lat=lat, soft=last.get(q))
+
+    def store(o, i, lat, q="sync"):
+        add(q, 60, [i], [], lambda e: [e.dma_start(o, ap(i))], sem="outs", inc=16, lat=lat)
 
     eng = topo.engines(core, nxt)
-    ne = 1
-    while ne * 2 <= len(eng):
-        ne *= 2
-    mask = sum(1 << e for e in eng[:ne])
     rid, pid = topo.addr(nxt)[:2]
 
     def send(dst, s, sem, lat):
         def fn(q):
-            q.remote_dma(T[dst][:], T[s][:], T.sem[sem], T.sem["sent"], pid, rid, mask)
+            q.remote_dma(ap(dst), ap(s), T.sem[sem], T.sem["sent"], pid, rid, topo.mask(core, nxt))
             return []
-        n = SCRATCH[s][1][1]
-        k = add("pool", 300, [(s, 0, n)], [], fn, sem="sent", inc=ne, lat=lat)
-        add("none", 0, [], [(dst, 0, n)], None, sem=sem, inc=ne, after=k)
+        k = add("pool", CALL, [s], [], fn, sem="sent", inc=len(eng), lat=lat)
+        add("none", 0, [], [dst], None, sem=sem, inc=len(eng), after=k)
 
-    load("sync", ("CH", 0, 512), T.ch[:, 0:512], 2500)
-    load("act", ("CH", 512, 1024), T.ch[:, 512:1024], 3000)
-    load("sync", ("sbi", 0, 16), T.sb[:], 2500)
-    load("act", ("ici", 0, 16), T.ic[:], 2500)
-    load("sync", ("CH", 1024, 1536), T.ch[:, 1024:1536], 3500)
-    load("act", ("CH", 1536, 2048), T.ch[:, 1536:2048], 4000)
-    load("sync", ("iai", 0, 16), T.ia[:], 4000)
-    load("act", ("XT", XO, XO + 1024), T.x[:, 0:1024], 4500)
-    load("sync", ("XT", XO + 1024, XO + 2048), T.x[:, 1024:2048], 5000)
-    load("sync", ("thi", 0, 1), T.th[:], 5000)
-    load("sync", ("Y0", 0, 256), T.y[:], 5500)
+    def fold(job):
+        j = JOBS.index(job)
+        c, o, s0, m = job
+        hc = helper_of(topo, T.cores, core, j)
+        hr, hp = topo.addr(hc)[:2]
+        cols = lambda n: tl(n + str(c), 16 * s0, 16 * (s0 + m))
+        both = [cols(n) for n in PAIRS[o]]
 
-    full = lambda n: (n, 0, SCRATCH[n][1][1])
-    fill(full("ones"), 1.0)
-    pool(full("IB"), [full("ones")], 128,
-         lambda q: [q.affine_select(T.IB[:], T.ones[:], [[-1, 128]], A.is_equal, 0.0, 0, 1)])
-    pool(full("tmpb"), [full("ones")], 128,
-         lambda q: [q.affine_select(T.tmpb[:], T.ones[:], [[-16, 8], [0, 16]], A.is_ge, 0.0, 0, 1)])
-    pool(full("BO"), [full("tmpb")], 128,
-         lambda q: [q.affine_select(T.BO[:], T.tmpb[:], [[16, 8], [0, 16]], A.is_ge, 0.0, 15, -1)])
-    pool(("pi", 0, 1), [], 1, lambda q: [q.iota(T.pi[:, 0:1], [[0, 1]], 0, 1)])
-    pool(full("eqi"), [], 8, lambda q: [q.iota(T.eqi[:], [[16, 8]], 15, 0)])
-    pool(full("ic16"), [], 16, lambda q: [q.iota(T.ic16[:], [[1, 16]], 0, 0, allow_small_or_imprecise_dtypes=True)])
-    pool(full("mkf"), [], 256,
-         lambda q: [q.iota(T.mkf[:], [[-16, 4], [1, 64]], 0, 0, allow_small_or_imprecise_dtypes=True)])
-    pool(full("newf"), [], 1024,
-         lambda q: [q.iota(T.newf[:], [[512, 4], [1, 256]], 256, 0, allow_small_or_imprecise_dtypes=True)])
-    for name, f in (("IM", -1.0), ("I2", 2.0), ("IH", 1.0), ("IMH", -1.0), ("IK", 1024.0), ("I8", 8.0)):
-        ts(full(name), full("IB"), f, A.mult)
-    copy(full("BOH"), full("BO"))
-    for name, f in (("Z1", 1.0), ("ZM", -1.0), ("Z2", 2.0), ("ZH", 1.0)):
-        fill(full(name), 0.0) if SCRATCH[name][2] == BF else ts(full(name), full("Z1"), f, A.mult)
-        if SCRATCH[name][2] == BF:
-            ts((name, 15, 143, 16), ("BO", 0, 128, 16), f, A.mult)
-    sel = lambda name, k: (name, 15 - k, 143 - k)
-    ts(("pj", 0, 1), ("pi", 0, 1), 15, A.bitwise_and)
-    kc = ("kc", 0, 1)
-    copy(kc, ("pj", 0, 1))
-    ts(("k16", 0, 1), kc, 16.0, A.mult)
-    if not TURNED or any(c[1] != 128 for c in CHUNKS):
-        ts(("kf", 0, 1), kc, -1.0 / 16, A.mult, 15.0 / 16, A.add)
-        ts(full("KF"), full("ones"), ("kf", 0, 1), A.mult)
-    fill(full("D0"), 0.0)
-    fill(("D0", 0, 128, 16), -1.0e5)
-    fill(full("SEG"), 0.0)
-    fill(("SEG", 0, 16 * BLK, BLK), 1.0e12)
-    fill(full("CM"), -160.0)
-    copy(full("EQL"), full("eqi"))
-    ts(full("mkg"), full("mkf"), kc, A.is_ge, 27952.0, A.mult)
-    ts(full("MK"), full("mkg"), 2048.0, A.add)
-    for m in sorted(set(c[1] // 16 for c in CHUNKS)):
-        name = "C%d" % (16 * m)
-        ts((name, 0, m), ("ic16", 0, m), 256.0, A.mult, ("k16", 0, 1), A.add)
-        ts((name, m, 2 * m), ("ones", 0, m), 0.0, A.mult)
-        ts((name, 2 * m, 5 * m), ("ones", 0, 3 * m), 2048.0, A.mult)
-    turned = TURNED and any(c[1] == 128 for c in CHUNKS)
-    plain = not TURNED or any(c[1] != 128 for c in CHUNKS)
-    if turned:
-        pool(full("kf2"), [], 128,
-             lambda q: [q.iota(T.kf2[:], [[0, 8], [-1, 16]], 15, 0, allow_small_or_imprecise_dtypes=True)])
-        ts(full("KF2"), full("kf2"), 1.0 / 16, A.mult)
-        ts(full("OM"), full("ones"), -1.0, A.mult)
-        copy(("TH", 0, 1), ("thi", 0, 1))
-        ts(("THD", 0, 128), full("IH"), ("TH", 0, 1), A.mult)
-    ts(full("GI"), full("ic16"), 16.0, A.mult, kc, A.add)
-    copy(("SEG", BLK - 1, 16 * BLK, BLK), full("GI"))
+        def fn(q):
+            q.remote_dma_fused([RemoteDMATransfer(dst_ids=[DstId(rid=hr, pnc=hp)], dma_engine_mask=topo.mask(core, hc),
+                                                  remote_sem=T.sem["fa%d" % j], srcs=[ap(x) for x in both],
+                                                  dsts=[ap(cols(o))], alu_op=2)], local_sem=T.sem["fs%d" % j])
+            return []
+        size, ne = 128 * 32 * m, len(topo.engines(core, hc))
+        k = add("pool", CALL, both, [cols(o)], fn, sem=None)
+        ops[k]["job"] = j
+        k = add("out", size / FOLD_RATE, both, [], None, sem="fs%d" % j, inc=ne, lat=FLY, after=k)
+        add("back%d" % hc, CALL + size / BACK_RATE, [], [cols(o)], None, sem="fb%d" % j, inc=ne, lat=FLY, after=k)
+
+    load("sync", "lc0", [(tl("CH", 0, 1024), T.ch[:, 0:1024])], 4000)
+    load("act", "lc1", [(tl("CH", 1024, 2048), T.ch[:, 1024:2048])], 4000)
+    load("sync", "lli", [(tl("LI", 16 * a, 16 * a + 16), x[:]) for a, x in enumerate((T.sb, T.ia, T.ic))], 3000)
+    load("act", "lx0", [(tl("XT", XO, XO + 1024), T.x[:, 0:1024])], 5000)
+    load("sync", "lx1", [(tl("XT", XO + 1024, XO + V), T.x[:, 1024:2048])], 5000)
+    load("sync", "lth", [(tl("thi"), T.th[:])], 5000)
+    load("sync", "ly", [(tl("Y", 0, 256), T.y[:])], 5000)
+
+    LO, HI = (0, 64), (64, 128)
+    one = lambda n: tl("ONE", 0, n)
+    fill(tl("ONE"), 1.0)
+    select(tl("IB"), one(128), [[-1, 128]], A.is_equal, 0, 1)
+    select(tl("TMP"), one(128), [[-16, 8], [0, 16]], A.is_ge, 0, 1)
+    select(tl("BO"), tl("TMP"), [[16, 8], [0, 16]], A.is_ge, 15, -1)
+    for r in range(0, 16, 2):
+        select(tl("SELT", 128 * r, 128 * r + 256), one(256), [[-1, 2], [-16, 8], [0, 16]], A.is_equal, -r, 1)
+    iota(tl("pi"), [[0, 1]], 0, 1)
+    iota(tl("T1", 0, 128), [[0, 8], [1, 16]], 0, 0)
+    iota(tl("T2"), [[1, 8], [0, 32]], 0, 0)
+    iota(tl("T3"), [[0, 4], [-16, 2], [1, 32]], 0, 0)
+    iota(tl("T4"), [[16, 16]], 0, 0)
+    iota(tl("T5", 0, 8), [[0, 4], [16, 2]], 129, 0)
     for t in range(TV):
-        ts(("NI", 16 * t, 16 * t + 16), full("GI"), float(V + 512 * t), A.add)
-        copy(("NEWC", 256 * t, 256 * t + 256), ("newf", 256 * t, 256 * t + 256))
-    for j in range(4):
-        ts(("CT", 512 * j, 512 * j + 512), ("CH", 512 * j, 512 * j + 512), -2048.0, A.add)
-    copy(full("B0"), full("sbi"))
-    copy(full("C0"), full("ici"))
-    copy(full("A0"), full("iai"))
-    copy(("BFL", 0, 16), full("sbi"))
-    if plain:
-        ts(("BIAS", 0, 1), ("thi", 0, 1), -256.0, A.mult, -128.0, A.add)
+        iota(tl("DGS", 256 * t, 256 * t + 256), [[1, 256]], 256 + 512 * t, 0)
+    iota(tl("eqi"), [[1, 8]], 0, 0)
+    for name, f in (("IBM", -1.0), ("IB2K", 2048.0), ("IB8K", -8192.0), ("IH", 1.0), ("IHM", -1.0)):
+        ts(tl(name), tl("IB"), f, A.mult)
+    copy(tl("EQL"), tl("eqi"))
+    ts(tl("C0"), tl("T1", 0, 128), 0.0, A.is_equal)
+    for name, f in (("OM", -1.0), ("ONK", 1.0 / 1024)):
+        ts(tl(name), one(128), f, A.mult)
+    for j in range(2):
+        copy(tl("BOH", 128 * j, 128 * j + 128), tl("BO"))
+    ts(tl("BOM"), tl("BO"), -1.0, A.mult)
+    e = 1.0 / 1024
+    strip = [0, 2, 0, 0, 2 * e, -1, -1, 0, -e, 0, -1, -e, 1, -1, 0, 1, 0, 0, -e]
+    ts(tl("WS"), one(160), 0.0, A.mult)
+    window = lambda j: tl("WS", 8 * j, 8 * j + 24)
+    weights, used = {}, set()
+    for c in range(2):
+        at = ({"MR_": 14, "MP": 15, "MQ": 2, "P": 16} if SIZES[c] else
+              {"R": 12 if NT[c] == 128 else 5, "P": 6, "MR_": 0, "MQ": 2, "MP": 1})
+        if NF[c]:
+            at["Q"] = 9
+        weights[c] = {n: window(j) for n, j in at.items()}
+        used |= set(j + i for j in at.values() for i in range(3))
+    for j in sorted(used):
+        if strip[j]:
+            ts(tl("WS", 8 * j, 8 * j + 8), tl("BO", 0, 128, 16), float(strip[j]), A.mult)
+    fill(tl("ZB"), 0.0)
+    copy(tl("ZB", 15, 143, 16), tl("BO", 0, 128, 16))
+    copy(tl("ZH"), tl("ZB"))
+    sel = lambda r: tl("ZH", 15 - r, 143 - r)
+    kc = tl("kc")
+    ts(tl("pj"), tl("pi"), 15, A.bitwise_and)
+    copy(kc, tl("pj"))
+    ts(tl("pk"), tl("pi"), 4, A.arith_shift_right)
+    copy(tl("pd"), tl("pk"))
+    ts(tl("MR"), tl("T1", 0, 128), kc, A.is_equal)
+    ts(tl("IND"), tl("T2"), tl("pd"), A.is_equal)
+    ts(tl("MK"), tl("T3"), kc, A.is_ge, 8192.0, A.mult)
+    fill(tl("SEG"), 0.0)
+    fill(tl("SEG", 0, 256, BLK), 1.0e12)
+    ts(tl("SEG", BLK - 1, 256, BLK), tl("T5", 0, 8), kc, A.add, -16.0, A.mult)
+    fill(tl("RST"), 0.0)
+    fill(tl("RST", 0, 128, 16), -1.0e4)
+    fill(tl("CM"), -160.0)
+    ts(tl("GI"), tl("T4"), kc, A.add)
+    for rows, (f, g) in ((LO, (1032.0 / 64, 2056.0 / 64)), (HI, (-1.0 / 4096, -17.0 / 4096))):
+        fill(tl("CBF", rows=rows), g)
+        for c in range(2):
+            if NF[c]:
+                fill(tl("CBF", 128 * c + 128 - NF[c], 128 * c + 128, rows=rows), f)
+    copy(tl("TH"), tl("thi"))
+    for t in range(TV):
+        fill(tl("BASE", 16 * t, 16 * t + 16), 1.0 + t / 4)
+    for j in range(2):
+        copy(tl("DG", 512 * j, 512 * j + 512), tl("DGS", 512 * j, 512 * j + 512))
+    ts(tl("TH3", 256, 384), one(128), 0.0, A.mult)
+    for c in range(2):
+        copy(tl("CB%d" % c), tl("CBF", 128 * c, 128 * c + 128))
+        ts(tl("TH3", 128 * c, 128 * c + 128), tl("IH"), tl("TH"), A.mult)
+        for lev in range(2):
+            copy(tl("E%d%d" % (c, lev), 0, 16), one(16))
+        for j in range(0, 16 * (128 - NF[c]) if any(x[0] == c for x in JOBS) else 0, 512):
+            w = min(512, 16 * (128 - NF[c]) - j)
+            ts(tl("Q%d" % c, j, j + w), one(w), 0.0, A.mult)
+    copy(tl("SS", 96, 112), tl("LI", 0, 16))
+    copy(tl("LA", 0, 32), tl("LI", 16, 48))
+    copy(tl("FB", 0, 32), tl("LI", 0, 32))
+    for j in range(0, V, 512):
+        plus("CT", tl("CT", j, j + 512), tl("CH", j, j + 512))
 
-    ub = [0]
+    def psum(name, c, a, b):
+        return (PLACE[name][0] + str(c), PLACE[name][1] + a, PLACE[name][1] + b, 1, 0, 128)
+
+    def chunk(c, t, lev):
+        lim = V + 512 * t
+        n = lim + 256 * lev + 128 * c
+        st = lambda name, *a, **k: tl(name + str(c), *a, **k)
+        lv = lambda name, *a, **k: tl("%s%d%d" % (name, c, lev), *a, **k)
+        ps = lambda name, a, b: psum(name, c, a, b)
+        xw = tl("XT", XO, XO + lim)
+        cw = tl("CH") if t == 0 else tl("CT", 0, lim)
+        if lev == 0:
+            for a, at in ((0, ("SS", 96 - 32 * t)), (2, ("LA", 32 * t + 16)), (1, ("LA", 32 * t))):
+                plus("KU%d0" % c, lv("KU", 128 * a, 128 * a + 128), cw, off=tl(at[0], at[1] + 8 * c, at[1] + 8 * c + 8))
+        else:
+            nodes, nv = tl("LU%d0" % c), st("NV1")
+            plus("KU%d1" % c, lv("KU"), cw, off=nodes)
+            now["class"] = LATE
+            act(nv, xw, ACT.Copy, off=nodes)
+        now["class"] = LATE
+        plus("K", lv("K"), lv("KU"), -2048.0)
+        now["class"] = MAIN
+        kid = lambda name, s0, m: lv("KU", 128 * "QPR".index(name) + s0, 128 * "QPR".index(name) + s0 + m)
+        done, turn = 0, 0
+        for kind, m, how in PIECES[c]:
+            s0 = done if SIZES[c] else 128 - done - m
+            done += m
+            big = lambda name: st(name, 16 * s0, 16 * (s0 + m))
+            if kind == "F":
+                for name in "QRP":
+                    x = -32.0 + (1.0 / 64 if name == "P" else 0.0)
+                    if name in how:
+                        ts(big(name), xw, x, A.add, off=kid(name, s0, m))
+                    else:
+                        act(big(name), xw, ACT.Identity, bias=x, off=kid(name, s0, m))
+                for o in PAIRS:
+                    fold((c, o, s0, m))
+                continue
+            size = ACT.Abs if SIZES[c] else ACT.Relu
+            if how[2:] == "q":
+                copy(big("QT"), xw, off=kid("Q", s0, m))
+            else:
+                act(big("QT"), xw, ACT.Copy, off=kid("Q", s0, m))
+            if how[0] == "b":
+                act(big("R"), xw, ACT.Copy, off=kid("R", s0, m))
+            else:
+                tt(big("R"), xw, big("QT"), A.subtract, off=kid("R", s0, m))
+            tt(big("P"), xw, big("QT"), A.subtract, off=kid("P", s0, m))
+            if how[0] == "b":
+                for j in range(0, 16 * m, 512):
+                    w = min(512, 16 * m - j)
+                    u = psum("U", turn % 2, 0, w)
+                    turn += 1
+                    mm(u, [(tl("IH"), sub(big("R"), j, j + w)), (tl("IHM"), sub(big("QT"), j, j + w))])
+                    act(sub(big("MR_"), j, j + w), u, size)
+            elif how[0] == "f":
+                fold((c, "MR_", s0, m))
+            elif how[0] == "s":
+                act(big("MR_"), big("R"), size)
+            else:
+                ts(big("MR_"), big("R"), 0.0, A.max)
+            ts(big("MQ"), big("P"), 1.0 / 64 - 32, A.add, -32.0, A.max)
+            if how[1] == "f":
+                fold((c, "MP", s0, m))
+            elif how[1] == "t":
+                for j in range(0, 16 * m, 512):
+                    w = min(512, 16 * m - j)
+                    cut = lambda name: sub(big(name), j, j + w)
+                    u = psum("U", turn % 2, 0, w)
+                    turn += 1
+                    mm(u, [(tl("IH"), cut("P")), (tl("IHM"), cut("R"))] + ([(tl("IH"), cut("QT"))] if how[0] == "b" else []))
+                    act(cut("MP"), u, size)
+            else:
+                tt(big("MP"), big("P"), big("R"), A.max)
+        now["class"] = TAIL[c]
+        D = ps("D", 0, 384)
+        mm(D, [(tl("OM"), tl("TH3"))] + ([(tl("OM"), tl("THA"), sub(D, 0, 256))] if t else []), stop=False)
+        if 0 < NT[c] < 128:
+            mm(D, [(st("R", k, 16 * NT[c], 16), weights[c]["MP"], sub(D, k, 384, 16, rows=(0, NT[c]))) for k in range(16)],
+               start=False, stop=False)
+        for name in weights[c]:
+            for a, b in SUMS[c]:
+                run = PE_RUN * (2 if b - a < 64 else 1)
+                for k0 in range(0, 16, run):
+                    mm(D, [(st(name, 16 * a + k, 16 * b, 16), weights[c][name], sub(D, k, 384, 16, rows=(a, b)))
+                           for k in range(k0, k0 + run)], start=False, stop=False)
+        mm(D, [(st("CB"), tl("ONK"), sub(D, 256, 384))], start=False)
+        D3, nal, nbe = sub(D, 256, 384), lv("NB", 0, 128), lv("NB", 128, 256)
+        if "NB" in TAIL_ON_VECTOR:
+            ts(lv("NB"), sub(D, 0, 256), 0.5, A.is_lt)
+        else:
+            act(lv("NB"), sub(D, 0, 256), ACT.Sigmoid, bias=256.0, scale=-512.0)
+        if "DI" in TAIL_ON_VECTOR:
+            copy(lv("DI"), D3)
+        else:
+            act(lv("DI"), D3, ACT.Copy)
+        tt(lv("NC"), nal, nbe, A.max)
+        tt(lv("HI"), lv("DI"), lv("NC"), A.subtract)
+        scan(lv("F"), tl("RST"), lv("HI"), A.add, A.max)
+        tt(lv("X"), D3, lv("HI"), A.is_lt)
+        copy(lv("FM"), lv("F", 15, 128, 16))
+        tt(lv("E", 1, 129), lv("FM"), lv("F"), A.is_equal, off=tl("EQL"))
+        star = [(lv("E", 1, 129), tl("IH")), (lv("E", 0, 128), tl("IHM")), (tl("C0"), tl("IH"))]
+        na = 3 if lev == 0 else 1
+        prq = lv("PR", 128, 256)
+        mm(ps("OHQ", 0, 128), star)
+        tt(prq, ps("OHQ", 0, 128), lv("K", 0, 128), A.mult)
+        if lev == 0:
+            for a in (1, 2):
+                tt(lv("PR", 128 + 128 * a, 256 + 128 * a), ps("OHQ", 0, 128), lv("K", 128 * a, 128 * a + 128), A.mult)
+            tt(lv("NW"), ps("OHQ", 0, 128), tl("DG", 256 * t + 128 * c, 256 * t + 128 * c + 128), A.mult)
+        mm(ps("CLT", 0, 128), [(lv("NC"), tl("IH"))])
+        act(lv("PR", 0, 128), ps("CLT", 0, 128), ACT.Copy)
+        LS = ps("LS", 0, 8 + 8 * na)
+        mm(LS, [(sel(r), lv("PR", r, 128 + 128 * na, 16)) for r in range(16)])
+        plus("LU", lv("LU", 0, 8 * na), sub(LS, 8, 8 + 8 * na), 2048.0)
+        if lev == 0:
+            plus("CS", tl("CS", 8 * c, 8 * c + 8), sub(LS, 0, 8))
+        else:
+            tt(tl("CN", 8 * c, 8 * c + 8), sub(LS, 0, 8), tl("CS", 8 * c, 8 * c + 8), A.min)
+        mm(ps("ZB", 0, 128), [(prq, tl("BOH", 0, 128))])
+        tt(lv("ZM"), ps("ZB", 0, 128), tl("MR"), A.mult)
+        DIFF = ps("DIFF", 0, 256)
+        mm(DIFF, [(tl("IH"), tl("MK"))]
+           + [(tl("BOM"), sub(prq, BLK * (j // 2), BLK * (j // 2) + BLK), sub(DIFF, BLK * j, BLK * j + BLK)) for j in range(8)],
+           stop=False)
+        mm(DIFF, [(lv("ZM"), tl("IND"))], start=False)
+        if "DF" in TAIL_ON_VECTOR:
+            ts(lv("DF"), DIFF, 0.0, A.not_equal, 8192.0, A.mult)
+        else:
+            act(lv("DF"), DIFF, ACT.Abs, scale=8192.0)
+        scan(lv("MN"), tl("SEG"), lv("DF"), A.add, A.min)
+        tt(lv("OF"), sub(LS, 8, 16), lv("MN", BLK - 1, 256, BLK), A.min)
+        plus("OU", lv("OU"), lv("OF"), 2048.0 + XO)
+        act(lv("XZ"), xw, ACT.Copy, off=lv("LU", 0, 8))
+        mm(ps("HS", 0, 128), [(tl("IB"), tl("Y", 256 * t + 128 * c, 256 * t + 128 * c + 128)), (tl("IB"), lv("XZ"))])
+        act(lv("HH"), ps("HS", 0, 128), ACT.Identity, bias=159.75, scale=0.5)
+        now["class"] = LATE
+        takeq = [(nal, tl("IH")), (lv("X"), tl("IH"))]
+        terms = [(tl("IH"), lv("K", 128, 256)), (tl("IH"), lv("PD", 0, 128)), (tl("IHM"), lv("PD", 128, 256))]
+        if lev == 0:
+            mm(ps("NT", 0, 128), takeq + star)
+            act(lv("N2", 0, 128), ps("NT", 0, 128), ACT.Sigmoid, bias=-128.0, scale=256.0)
+            for a in range(2):
+                tt(lv("PD", 128 * a, 128 * a + 128), lv("N2", 0, 128), lv("K", 128 * a, 128 * a + 128), A.mult)
+            terms += [(tl("IHM"), prq), (tl("IH"), lv("NW"))]
+        else:
+            for a in range(2):
+                mm(ps("NS", 128 * a, 128 * a + 128), takeq)
+            tt(lv("PD"), ps("NS", 0, 256), lv("K", 0, 256), A.mult)
+        mm(ps("MS", 0, 128), terms)
+        act(tl("CT", n, n + 128), ps("MS", 0, 128), ACT.Identity, bias=2048.0)
+        if lev == 1:
+            mm(ps("NVP", 128, 256), [(tl("IB"), sub(nv, 0, 128)), (tl("IB"), sub(nv, 128, 256)), (tl("IBM"), sub(nv, 256, 384))])
+            ts(tl("XT", XO + n, XO + n + 128), ps("NVP", 128, 256), 0.0, A.max, 63.0, A.min)
+        now["class"] = 0.0
+
     for t in range(TV):
         lim = V + 512 * t
-        xw, cw = ("XT", XO, XO + lim), ("CT", 0, lim)
-        Yt, bias = "Y%d" % t, ("BIAS", 8 * t, 8 * t + 1)
+        bl = tl("SS", 96 - 32 * t, 112 - 32 * t)
+        now["part"] = None
         if t < TV - 1:
-            send("C%d" % (t + 1), "B%d" % t, "rc%d" % (t + 1), 3000)
-            copy(("AF", 16 * t, 16 * t + 16), full("A%d" % t))
-        at0[0] = len(ops)
+            send(tl("LA", 32 * t + 48, 32 * t + 64), bl, "rc%d" % (t + 1), 3000)
         for lev in range(LV):
             n = lim + 256 * lev
-            at0[1] = 2 * t + lev
-            K, LU, LF = "K%d" % lev, "LU%d" % lev, "LF%d" % lev
-
-            def lst(a, l0, m):
-                if lev == 0:
-                    return ("BAC"[a] + str(t), l0 // 16, (l0 + m) // 16)
-                b = 5 * l0 // 16 + (2 + a) * m // 16
-                return ("LU0", b, b + m // 16)
-
-            def kid(a, l0, m, s0, sm):
-                b = (256 * a + s0) if lev == 0 else (3 * l0 + a * m + s0 - l0)
-                return (K, b, b + sm)
-
+            part("l%d" % lev)
+            now["level"] = 2 * t + lev
             if lev == 0:
-                for a in (0, 2, 1):
-                    for l0, m in ((128, 128), (0, 128)) if a == 0 else ((0, 256),):
-                        ts((K, 256 * a + l0, 256 * a + l0 + m), cw, 2048.0, A.add, off=lst(a, l0, m))
-                for a in range(3):
-                    act(("NV", 256 * a, 256 * a + 256), xw, ACT.Copy, off=lst(a, 0, 256))
-                mm([(("DB", 256, 512), [(full("IB"), ("NV", 0, 256)), (full("IB"), ("NV", 256, 512)),
-                                        (full("IM"), ("NV", 512, 768))])])
-                ts(("XT", XO + n, XO + n + 256), ("DB", 256, 512), 0.0, A.max, 63.0, A.min)
-            else:
-                n0 = XO + lim
-                mm([(("Q1", 0, 256), [(full("IB"), full(Yt)), (full("IM"), ("XT", n0, n0 + 256))])])
-                act(("XT", XO + 4096, XO + 4352), ("Q1", 0, 256), ACT.Abs)
-            for l0, m, subs in CHUNKS:
-                mc = m // 16
-                col = lambda name, j=0: (name, l0 + j, l0 + j + m)
-                if lev == 1:
-                    b = 5 * l0 // 16 + 2 * mc
-                    ts((K, 3 * l0, 3 * l0 + 3 * m), cw, 2048.0, A.add, off=("LU0", b, b + 3 * mc))
-                    act(("NV", 3 * l0, 3 * l0 + 3 * m), xw, ACT.Copy, off=("LU0", b, b + 3 * mc))
-                    nv = lambda a: ("NV", 3 * l0 + a * m, 3 * l0 + a * m + m)
-                    o = ("DB", 256 + l0, 256 + l0 + m)
-                    mm([(o, [(full("IB"), nv(0)), (full("IB"), nv(1)), (full("IM"), nv(2))])])
-                    ts(("XT", XO + n + l0, XO + n + l0 + m), o, 0.0, A.max, 63.0, A.min)
-                s0 = l0
-                for sm in subs:
-                    both, sm = sm < 0, abs(sm)
-                    big = lambda name: (name, 16 * s0, 16 * (s0 + sm))
-                    part = lambda name, j: (name, 16 * s0 + j, 16 * s0 + j + 512)
-                    act(big("BM"), xw, ACT.Copy, off=kid(0, l0, m, s0, sm))
-                    if both:
-                        act(big("W"), xw, ACT.Copy, off=kid(2, l0, m, s0, sm))
-                        U = "U%d" % (ub[0] % 2)
-                        ub[0] += 1
-                        mm([((U, j, j + 512), [(full("IB"), part("W", j)), (full("IM"), part("BM", j))])
-                            for j in range(0, 16 * sm, 512)])
-                        act(big("AW"), (U, 0, 16 * sm), ACT.Abs)
-                    else:
-                        tt(big("W"), xw, big("BM"), A.subtract, off=kid(2, l0, m, s0, sm))
-                        act(big("AW"), big("W"), ACT.Abs)
-                    tt(big("E"), xw, big("BM"), A.subtract, off=kid(1, l0, m, s0, sm))
-                    ts(big("R"), big("E"), 1.0 / 64 - 32, A.add, -32.0, A.max)
-                    U = "U%d" % (ub[0] % 2)
-                    ub[0] += 1
-                    mm([((U, j, j + 512), [(full("IB"), part("E", j)), (full("IM"), part("W", j))]
-                         + ([(full("IB"), part("BM", j))] if both else [])) for j in range(0, 16 * sm, 512)])
-                    act(big("AU"), (U, 0, 16 * sm), ACT.Abs)
-                    s0 += sm
-                ps = lambda name, a=0, b=m: (PLACE[name][0], PLACE[name][1] + a, PLACE[name][1] + b)
-                D1, D2, D3, SA, KEY, HS, MS = [ps(x) for x in ("D1", "D2", "D3", "SA", "KEY", "HS", "MS")]
-                pr = lambda j: ("PR", 5 * l0 + j * m, 5 * l0 + j * m + m)
-                lanes = m == 128 and TURNED
-                if lanes:
-                    slot = lambda name, k: (name, 16 * l0 + k, 16 * (l0 + m), 16)
-                    grp = lambda name: (name, 15, 143, 16)
-                    at = lambda d, k: (d[0], d[1] + k, d[2], 16)
-                    mm([(at(D3, k), [(slot("E", k), grp("ZM")), (slot("R", k), grp("Z2"))]) for k in range(16)], whole=D3)
-                    for d, x in ((D2, "AW"), (D1, "AU")):
-                        mm([(d, [(full("OM"), ("THD", 128 * t, 128 * t + 128))]
-                             + [(slot(x, k), grp("Z1"), at(d, k)) for k in range(16)])])
-                else:
-                    for h, w in ((0, 64), (64, 64)) if m == 128 else ((0, m),):
-                        slot = lambda name, k: (name, 16 * (l0 + h) + k, 16 * (l0 + h + w), 16)
-                        mm([(ps("D3", h, h + w), [(sel("ZM", k), slot("E", k)) for k in range(16)]
-                             + [(sel("Z2", k), slot("R", k)) for k in range(16)])])
-                        mm([(ps("D2", h, h + w), [(sel("Z1", k), slot("AW", k)) for k in range(16)])])
-                        mm([(ps("D1", h, h + w), [(sel("Z1", k), slot("AU", k)) for k in range(16)])])
-                act(col("BE"), D2, ACT.Sigmoid, bias=-128.0 if lanes else bias, scale=256.0)
-                act(col("AL"), D1, ACT.Sigmoid, bias=-128.0 if lanes else bias, scale=256.0)
-                ts(col("DI"), D3, -1016.25, A.add)
-                ts(col("DJ"), D3, -1016.0 + 15.0 / 64, A.add)
-                if lanes:
-                    OH = col("OB")
-                    tt(col("CL2"), col("AL"), col("BE"), A.mult)
-                    terms = [(full("IH"), col("DI")), (full("IH"), full("KF2")), (full("IK"), col("CL2"))]
-                    mm([(KEY, terms)])
-                    mm([(ps("KEY2"), terms)])
-                    act(col("KT"), ps("KEY2"), ACT.Copy)
-                    scan(col("SC"), ("D0", 0, m), KEY, A.add, A.max)
-                    tt(col("OT"), col("SC"), col("KT"), A.is_equal, off=("EQL", 0, mc))
-                    mm([(ps("OHT"), [(col("OT"), full("IH"))])])
-                    act(OH, ps("OHT"), ACT.Copy)
-                    mm([(ps("CLT"), [(col("CL2"), full("IH"))])])
-                    copy(pr(1), ps("CLT"))
-                else:
-                    OH = col("OH")
-                    tt(pr(1), col("AL"), col("BE"), A.mult)
-                    mm([(KEY, [(full("IH"), col("DI")), (full("IH"), ("KF", 0, m)), (full("IK"), pr(1))])])
-                    turn(col("KT"), KEY)
-                    scan(col("SC"), ("D0", 0, m), col("KT"), A.add, A.max)
-                    tt(col("OT"), col("SC"), col("KT"), A.is_equal, off=("EQL", 0, mc))
-                    turn(OH, col("OT"))
-                tt(pr(2), cw, OH, A.mult, off=lst(0, l0, m))
-                ts(pr(0), OH, kc, A.mult)
-                na = 5 if lev == 0 else 3
-                if lev == 0:
-                    tt(pr(3), cw, OH, A.mult, off=lst(1, l0, m))
-                    tt(pr(4), cw, OH, A.mult, off=lst(2, l0, m))
-                LS = ps("LS", 0, na * mc)
-                mm([(LS, [(sel("ZH", r), ("PR", 5 * l0 + r, 5 * l0 + na * m, 16)) for r in range(16)]
-                     + [(full("IH"), ("C%d" % m, 0, na * mc))])])
-                lb = 5 * l0 // 16
-                copy((LU, lb, lb + na * mc), LS)
-                z8 = lambda c: ("Z8", l0 // 16 + c, l0 // 16 + c + 1)
-                gl = lambda name, j=0: (name, l0 // 16 + j, l0 // 16 + j + mc)
-                if l0 or not LAST_ON_VECTOR:
-                    act(gl("Z8"), ps("LS", 2 * mc, 3 * mc), ACT.Identity, scale=8192.0)
-                act((LF, lb + mc, lb + 3 * mc), ps("LS", mc, 3 * mc), ACT.Identity, bias=float(XO))
-                qb, bc = 5 * l0 + 2 * m, BLK // 16
-                mm([(ps("ZB", BLK * c, BLK * c + BLK), [(full("BOH"), ("PR", qb + BLK * (c // bc), qb + BLK * (c // bc) + BLK)),
-                                                        (full("IH"), ("MK", 64 * (c % bc), 64 * (c % bc) + BLK))])
-                    for c in range(mc)])
-                for c in range(mc):
-                    o, i = ("DF", bc * l0 + BLK * c, bc * l0 + BLK * c + BLK), ps("ZB", BLK * c, BLK * c + BLK)
-                    if l0 == 0 and LAST_ON_VECTOR:
-                        ts(o, i, ps("LS", 2 * mc + c, 2 * mc + c + 1), A.not_equal, 8192.0, A.mult)
-                    else:
-                        act(o, i, ACT.Abs, bias=z8(c), scale=-8192.0)
-                wide = lambda name: (name, bc * l0, bc * (l0 + m))
-                scan(wide("MN"), wide("SEG"), wide("DF"), A.add, A.min)
-                tt(gl("OF"), ("MN", bc * l0 + BLK - 1, bc * (l0 + m), BLK), (LF, lb + 2 * mc, lb + 3 * mc), A.min)
-                copy(gl("OU"), gl("OF"))
-                act(col("XZ"), ("BM", 16 * l0, 16 * (l0 + m)), ACT.Copy, off=(LU, lb, lb + mc))
-                mm([(HS, [(full("IB"), col(Yt)), (full("IB"), col("XZ"))])])
-                act(col("HH"), HS, ACT.Identity, bias=159.75, scale=0.5)
-                base = [(full("I2"), col("AL")), (full("IM"), col("BE")), (full("IH"), col("DJ")), (full("IMH"), col("DI"))]
-                if lev == 0:
-                    base.append((full("I8"), col("OT") if lanes else OH))
-                    tt(col("P3"), OH, col("NEWC", 256 * t), A.mult)
-                mm([(SA, [(r, l) for l, r in base] if lanes else base)])
-                act(col("CD"), SA, ACT.Sigmoid, bias=-384.0, scale=256.0)
-                act(col("ND"), SA, ACT.Sigmoid, bias=384.0, scale=-256.0)
-                tt(col("P1"), cw, col("CD"), A.mult, off=lst(1, l0, m))
-                tt(col("P2"), cw, col("ND"), A.mult, off=lst(0, l0, m))
-                mm([(MS, [(full("IH"), col("P1")), (full("IH"), col("P2"))]
-                     + ([(full("IH"), col("P3")), (full("IMH"), pr(3))] if lev == 0 else []))])
-                if t < TV - 1:
-                    act(col("CT", n), MS, ACT.Copy)
-                else:
-                    at0[0] -= 1
-                act(col("CO", n - V), MS, ACT.Identity, bias=2048.0)
-                if lev == 1:
-                    tt(gl("CN"), ("LF0", lb + mc, lb + 2 * mc), ("LF1", lb + mc, lb + 2 * mc), A.max)
-            for l0, m, subs in CHUNKS:
-                for b0 in range(l0 + m - BLK, l0 - 1, -BLK):
-                    scatter_add(("XT", 0, XO + lim), ("OU", b0 // 16, (b0 + BLK) // 16), ("HH", b0, b0 + BLK), ("CM", 0, BLK))
-            store("sync", T.co[:, n - V:n - V + 256], ("CO", n - V, n - V + 256), 2500)
-        ni = ("NI", 16 * t, 16 * t + 16)
-        ts(full("NA"), full("CN"), XO + 9.0, A.is_lt)
-        tt(full("XX"), full("NA"), ni, A.mult)
-        bn = ("BFL", 16 * t + 16, 16 * t + 32)
-        tt(bn, ("BFL", 16 * t, 16 * t + 16), full("XX"), A.max)
+                now["class"] = LATE
+                xw, nv, nvp = tl("XT", XO, XO + lim), tl("NV0"), psum("NVP", 1, 0, 256)
+                act(sub(nv, 0, 256), xw, ACT.Copy, off=bl)
+                act(sub(nv, 256, 768), xw, ACT.Copy, off=tl("LA", 32 * t, 32 * t + 32))
+            now["class"] = 0.0
+            for c in (1, 0):
+                chunk(c, t, lev)
+            if lev == 0:
+                now["class"] = LATE
+                mm(nvp, [(tl("IB"), sub(nv, 0, 256)), (tl("IB"), sub(nv, 256, 512)), (tl("IBM"), sub(nv, 512, 768))])
+                ts(tl("XT", XO + n, XO + n + 256), nvp, 0.0, A.max, 63.0, A.min)
+                now["class"] = 0.0
+            for c in (1, 0):
+                for b0 in range(128 - BLK, -1, -BLK):
+                    scatter_add(tl("XT", 0, XO + lim), tl("OU%d%d" % (c, lev), b0 // 16, (b0 + BLK) // 16),
+                                tl("HH%d%d" % (c, lev), b0, b0 + BLK), tl("CM"))
+            store(T.co[:, n - V:n - V + 256], tl("CT", n, n + 256), 2500)
+        part("end")
+        act(tl("AB"), tl("CN"), ACT.Sigmoid, bias=1920.0, scale=-256.0, accum=tl("AS"))
+        for a in range(2):
+            mm(psum("VV", 1, 16 * a, 16 * a + 16),
+               [(tl("IB8K"), tl("AB")), (tl("IB"), tl("GI")), (tl("IB2K"), tl("BASE", 16 * t, 16 * t + 16))])
+        fb = tl("FB", 32 * t + 32, 32 * t + 64)
+        tt(fb, psum("VV", 1, 0, 32), tl("FB", 32 * t, 32 * t + 32), A.max)
+        ABP, YD = psum("ABP", 1, 0, 256), psum("YD", 1, 0, 256)
+        mm(ABP, [(tl("SELT", 128 * r, 128 * r + 128), tl("AB"), sub(ABP, r, 256, 16)) for r in range(16)], each=True)
+        tt(tl("YM"), ABP, tl("Y", 256 * t, 256 * t + 256), A.mult)
+        mm(YD, [(tl("IB"), tl("YM")), (tl("IBM"), tl("XT", XO + lim, XO + lim + 256))])
+        yn = tl("N", 256 * t, 256 * t + 256)
+        act(yn, YD, ACT.Abs)
         if t < TV - 1:
-            copy(full("B%d" % (t + 1)), bn)
-            tt(full("AN"), ("AF", 16 * t, 16 * t + 16), full("XX"), A.max)
-            copy(full("S%d" % t), full("AN"))
-            send("A%d" % (t + 1), "S%d" % t, "ra%d" % (t + 1), 3000)
-            ts(full("AB"), full("CN"), XO + 9.0, A.is_ge)
-            mm([(("Q0", 448, 464), [(full("BO"), full("AB"))])])
-            add("dve", vcost(16, 1), [("Q0", 448, 464)], [("AS", 0, 1)],
-                lambda q: [q.tensor_reduce(T.AS[:, 0:1], T.Q0[:, 448:464], AxisListType.X, A.add)])
-            if plain:
-                ts(("BIAS", 8 * t + 8, 8 * t + 9), ("AS", 0, 1), -256.0, A.mult, ("BIAS", 0, 1), A.add)
-            if turned:
-                tt(("TH", 8 * t + 8, 8 * t + 9), ("AS", 0, 1), ("TH", 0, 1), A.add)
-                ts(("THD", 128 * t + 128, 128 * t + 256), full("IH"), ("TH", 8 * t + 8, 8 * t + 9), A.mult)
-        ts(full("YM"), full("CN"), XO + 9.0, A.is_ge, float(4096 - lim), A.mult)
-        tt(full("YL"), full("YM"), full("GI"), A.add)
-        copy(full("YU"), full("YL"))
-        act(full("N%d" % t), ("XT", XO + lim, XO + 4352), ACT.Copy, off=full("YU"))
-        if t < TV - 1:
-            send("Y%d" % (t + 1), "N%d" % t, "ry%d" % (t + 1), 3500)
-    store("sync", T.xo[:, 3584:4096], ("XT", XO + 3584, XO + 4096), 2500)
-    store("sync", T.so[:], ("BFL", 64, 80), 2500)
-    store("sync", T.yo[:], full("N3"), 2500)
-    store("sync", T.xo[:, 0:1792], ("XT", XO, XO + 1792), 4000)
-    store("act", T.xo[:, 1792:3584], ("XT", XO + 1792, XO + 3584), 4000)
+            copy(tl("SS", 64 - 32 * t, 96 - 32 * t), fb)
+            la = tl("LA", 32 * t + 32, 32 * t + 48)
+            send(la, tl("SS", 80 - 32 * t, 96 - 32 * t), "ra%d" % (t + 1), 3000)
+            send(tl("Y", 256 * t + 256, 256 * t + 512), yn, "ry%d" % (t + 1), 3500)
+            copy(sub(fb, 16, 32), la)
+            ts(tl("THA"), tl("BOH"), tl("AS"), A.mult)
+    now["part"] = None
+    store(T.so[:], tl("FB", 128, 144), 2500)
+    store(T.yo[:], tl("N", 768, 1024), 2500)
+    store(T.xo[:, 3584:4096], tl("XT", XO + 3584, XO + 4096), 2500)
+    store(T.xo[:, 0:1792], tl("XT", XO, XO + 1792), 3500)
+    store(T.xo[:, 1792:3584], tl("XT", XO + 1792, XO + 3584), 3500, q="act")
     return ops
 
 
@@ -444,31 +537,82 @@ def plan(ops):
     n = len(ops)
     deps = [set() for _ in range(n)]
     hist = {}
+    cell = lambda s: [(s[0], b) for b in range(s[1] // 256, (s[2] - 1) // 256 + 1)]
     for i, o in enumerate(ops):
         for wr, ss in ((False, o["rd"]), (True, o["wr"])):
             for s in ss:
-                for j, w2, a, b in hist.get(s[0], []):
-                    if j != i and (wr or w2) and a < s[2] and s[1] < b:
-                        deps[i].add(j)
+                for c in cell(s):
+                    for j, w2, h in hist.get(c, []):
+                        if j != i and (wr or w2) and h[1] < s[2] and s[1] < h[2] and h[4] < s[5] and s[4] < h[5]:
+                            deps[i].add(j)
         for s in o["wr"]:
-            hist[s[0]] = [h for h in hist.get(s[0], []) if not (s[1] <= h[2] and h[3] <= s[2] and len(s) == 3)]
+            if s[3] == 1:
+                for c in cell(s):
+                    hist[c] = [x for x in hist.get(c, [])
+                               if not (s[1] <= x[2][1] and x[2][2] <= s[2] and s[4] <= x[2][4] and x[2][5] <= s[5])]
         for wr, ss in ((False, o["rd"]), (True, o["wr"])):
             for s in ss:
-                hist.setdefault(s[0], []).append((i, wr, s[1], s[2]))
+                for c in cell(s):
+                    hist.setdefault(c, []).append((i, wr, s))
         if o["after"] is not None:
             deps[i].add(o["after"])
-        o["banks"] = set((s[0], b) for s in o["rd"] + o["wr"] if s[0] in PSUM for b in range(s[1] // 512, (s[2] - 1) // 512 + 1))
+        o["banks"] = set(s[0] for s in o["rd"] + o["wr"] if s[0] in PSUM)
+    pre0 = [deps[i] | ({ops[i]["soft"]} if ops[i]["soft"] is not None else set()) for i in range(n)]
     succ = [[] for _ in range(n)]
     for i in range(n):
-        for j in deps[i]:
+        for j in pre0[i]:
             succ[j].append(i)
 
     def hop(j, i):
+        if ops[i]["soft"] == j:
+            return 0.0
         if ops[j]["q"] == ops[i]["q"]:
             return ops[j]["lat"] + (0.0 if ops[i]["q"] == "pe" else HOP_SAME)
         return ops[j]["lat"] + HOP_OTHER
 
     def run(pre, post, prio, back):
+        left = [len(d) for d in pre]
+        ready = [i for i in range(n) if left[i] == 0]
+        est = [ops[i]["lat"] if back else 0.0 for i in range(n)]
+        fin = [0.0] * n
+        taken = {}
+        for _ in range(n):
+            i = max(ready, key=lambda x: prio[x])
+            ready.remove(i)
+            o, s = ops[i], est[i]
+            moved = True
+            while moved:
+                moved = False
+                for r in [o["q"]] + list(o["banks"]):
+                    spans = taken.get(r, [])
+                    lo, hi = 0, len(spans)
+                    while lo < hi:
+                        mid = (lo + hi) // 2
+                        if spans[mid][0] < s - LONGEST:
+                            lo = mid + 1
+                        else:
+                            hi = mid
+                    for a, b, q in spans[lo:]:
+                        gap = 0.0 if r == o["q"] else HOP_OTHER
+                        if a >= s + o["cost"] + gap:
+                            break
+                        if b + gap > s and (r == o["q"] or q != o["q"]):
+                            s, moved = b + gap, True
+            fin[i] = s + o["cost"]
+            for r in [o["q"]] + list(o["banks"]):
+                spans = taken.setdefault(r, [])
+                k = len(spans)
+                while k and spans[k - 1][0] > s:
+                    k -= 1
+                spans.insert(k, (s, fin[i], o["q"]))
+            for k in post[i]:
+                est[k] = max(est[k], fin[i] + (hop(k, i) if back else hop(i, k)))
+                left[k] -= 1
+                if left[k] == 0:
+                    ready.append(k)
+        return max(fin[i] + (0.0 if back else ops[i]["lat"]) for i in range(n)), fin
+
+    def run_free(pre, post, prio, back):
         left = [len(d) for d in pre]
         ready = {}
         for i in range(n):
@@ -476,7 +620,7 @@ def plan(ops):
                 ready.setdefault(ops[i]["q"], []).append(i)
         est = [ops[i]["lat"] if back else 0.0 for i in range(n)]
         fin = [0.0] * n
-        free, bank, order, extra = {}, {}, [], [set() for _ in range(n)]
+        free, bank = {}, {}
         for _ in range(n):
             best = None
             for q, rs in ready.items():
@@ -496,78 +640,193 @@ def plan(ops):
             s, i = max((c for c in best[1] if c[0] <= best[0] + SLACK), key=lambda c: prio[c[1]])
             o = ops[i]
             for b in o["banks"]:
-                for q2, j in bank.get(b, {}).items():
-                    if q2 != o["q"]:
-                        extra[i].add(j)
                 bank.setdefault(b, {})[o["q"]] = i
             free[o["q"]] = fin[i] = s + o["cost"]
-            order.append(i)
             ready[o["q"]].remove(i)
             for k in post[i]:
                 est[k] = max(est[k], fin[i] + (hop(k, i) if back else hop(i, k)))
                 left[k] -= 1
                 if left[k] == 0:
                     ready.setdefault(ops[k]["q"], []).append(k)
-        return max(fin[i] + (0.0 if back else ops[i]["lat"]) for i in range(n)), order, extra, fin
+        return max(fin[i] + (0.0 if back else ops[i]["lat"]) for i in range(n)), fin
 
-    prio = [0.0] * n
+    base = [0.0] * n
     for i in range(n - 1, -1, -1):
-        prio[i] = ops[i]["cost"] + max([prio[k] + hop(i, k) for k in succ[i]] or [ops[i]["lat"]])
-    for i, o in enumerate(ops):
-        w = o["wr"][0][0] if o["wr"] else ""
-        if o["kind"] != i:
-            prio[i] = -1e6 * (o["level"] + (0.3 if w in MAINS else 0.6 if w in LATE else 0.0)) - i
-    best = None
-    rng = np.random.RandomState(1)
-    for it in range(ROUNDS):
-        res = run(deps, succ, prio, False)
-        if best is None or res[0] < best[0]:
-            best = res
-        prio = run(succ, deps, res[3], True)[3]
+        base[i] = ops[i]["cost"] + max([base[k] + hop(i, k) for k in succ[i]] or [ops[i]["lat"]])
     kinds = {}
     for i, o in enumerate(ops):
         kinds.setdefault(o["kind"], []).append(i)
     kinds = [v for v in kinds.values() if len(v) > 2]
+    first = [-1e6 * (o["level"] + o["class"]) - i if o["level"] >= 0 else base[i] for i, o in enumerate(ops)]
+    best = min((f(pre0, succ, first, False) for f in (run, run_free)), key=lambda r: r[0])
+    rng = np.random.RandomState(1)
+    same = {i: v for v in kinds for i in v}
+
+    def longest(fin):
+        before, last = {}, {}
+        for i in sorted(range(n), key=lambda x: fin[x]):
+            before[i] = last.get(ops[i]["q"])
+            last[ops[i]["q"]] = i
+        i, res = max(range(n), key=lambda x: fin[x] + ops[x]["lat"]), []
+        while True:
+            t, j = max([(fin[j] + hop(j, i), j) for j in pre0[i]] or [(0.0, None)])
+            b = before[i]
+            if b is not None and fin[b] > t:
+                res += [(same[x], s) for x, s in ((i, 1.0), (b, -1.0)) if x in same]
+                j = b
+            if j is None:
+                return res
+            i = j
+
+    cur, keep, path = best, best, longest(best[1])
     for it in range(TRIES):
-        prio = [ops[i]["cost"] - best[3][i] for i in range(n)]
-        for _ in range(1 + it % 2):
-            d = float(rng.randn()) * NOISE
-            for i in kinds[int(rng.randint(len(kinds)))]:
-                prio[i] += d
-        res = run(deps, succ, prio, False)
-        if res[0] <= best[0]:
-            best = res
-    busy = {}
+        f = run_free if it % MIX else run
+        if it % ROUNDS < 2:
+            prio = f(succ, pre0, best[1], True)[1]
+        else:
+            prio = [ops[i]["cost"] - best[1][i] for i in range(n)]
+            for _ in range(1 + it % 2):
+                d = float(rng.randn()) * NOISE
+                if rng.rand() < 0.3 or not path:
+                    k = kinds[int(rng.randint(len(kinds)))]
+                else:
+                    k, sign = path[int(rng.randint(len(path)))]
+                    d = abs(d) * sign
+                for i in k:
+                    prio[i] += d
+        res = f(pre0, succ, prio, False)
+        if res[0] <= cur[0] + WARM * (1.0 - it / TRIES) * rng.rand():
+            cur = res
+            path = longest(res[1])
+            if res[0] < keep[0]:
+                keep = res
+        best = cur
+    best = keep
+    order = sorted(range(n), key=lambda i: (best[1][i] - ops[i]["cost"], i))
+    lag = [[(j, hop(j, i)) for j in pre0[i]] for i in range(n)]
+    facts = [(o["q"], o["cost"], list(o["banks"]), o["lat"]) for o in ops]
+    place = {i: (v, x) for v in kinds for x, i in enumerate(v)}
+
+    def play(order):
+        fin, why, free, bank = [0.0] * n, [None] * n, {}, {}
+        end, last = 0.0, None
+        for i in order:
+            q, cost, banks, lat = facts[i]
+            s, w = 0.0, None
+            for j, h in lag[i]:
+                if fin[j] + h > s:
+                    s, w = fin[j] + h, (j, False)
+            j = free.get(q)
+            if j is not None and fin[j] > s:
+                s, w = fin[j], (j, True)
+            for b in banks:
+                j = bank.get(b)
+                if j is not None and facts[j][0] != q and fin[j] + HOP_OTHER > s:
+                    s, w = fin[j] + HOP_OTHER, (j, True)
+                bank[b] = i
+            fin[i], why[i], free[q] = s + cost, w, i
+            if fin[i] + lat > end:
+                end, last = fin[i] + lat, i
+        pairs = []
+        while why[last]:
+            if why[last][1]:
+                pairs.append((why[last][0], last))
+            last = why[last][0]
+        return end, fin, pairs
+
+    def swap(order, b, i, ahead):
+        x, y = order.index(b), order.index(i)
+        if x > y:
+            return order
+        mid = order[x:y + 1]
+        move = {i if ahead else b}
+        for k in (reversed(mid) if ahead else mid):
+            if k not in move and any(j in move for j in (succ[k] if ahead else pre0[k])):
+                move.add(k)
+        if (b if ahead else i) in move:
+            return order
+        one, other = [k for k in mid if k in move], [k for k in mid if k not in move]
+        return order[:x] + (one + other if ahead else other + one) + order[y + 1:]
+
+    cur = keep = play(order) + (order,)
+    for it in range(SWAPS):
+        b, i = cur[2][int(rng.randint(len(cur[2])))]
+        ahead, new = rng.rand() < 0.5, cur[3]
+        if b in place and i in place:
+            (vb, xb), (vi, xi) = place[b], place[i]
+            for x in range(len(vi)):
+                if 0 <= x + xb - xi < len(vb):
+                    new = swap(new, vb[x + xb - xi], vi[x], ahead)
+        else:
+            new = swap(new, b, i, ahead)
+        if new is cur[3]:
+            continue
+        res = play(new)
+        if res[0] <= cur[0] + HEAT * (1.0 - it / SWAPS) * rng.rand() ** 2:
+            cur = res + (new,)
+            if cur[0] < keep[0]:
+                keep = cur
+    best, order = keep, keep[3]
+    busy, bank = {}, {}
     for i in range(n):
-        deps[i] |= best[2][i]
-        ops[i]["t0"] = best[3][i] - ops[i]["cost"]
+        ops[i]["t0"] = best[1][i] - ops[i]["cost"]
         busy[ops[i]["q"]] = busy.get(ops[i]["q"], 0.0) + ops[i]["cost"]
-    return best[1], deps, best[0], busy
+    for i in order:
+        for b in ops[i]["banks"]:
+            deps[i] |= set(j for q, j in bank.get(b, {}).items() if q != ops[i]["q"])
+            bank.setdefault(b, {})[ops[i]["q"]] = i
+    return order, deps, best[0], busy
 
 
+SLACK, MIX, WARM, SWAPS, HEAT = 20.0, 2, 800.0, 16000, 500.0
+LEAN = (0.0, 30.0, 100.0, 1000.0)
 PLAN = {}
+
+
+def planned(T, topo, core):
+    ops = build(T, T.cores[(T.rank_of(core) + 1) % len(T.cores)], topo, core)
+    if "p" not in PLAN:
+        PLAN["p"] = plan(ops)
+    return ops, PLAN["p"][0], PLAN["p"][1]
+
+
+def hand_back(g, core, T, topo, owner):
+    ops, order, deps = planned(T, topo, owner)
+    rid, pid = topo.addr(owner)[:2]
+    come, gone = len(topo.engines(owner, core)), len(topo.engines(core, owner))
+    seen = {}
+    for j in [ops[i]["job"] for i in order if "job" in ops[i]]:
+        if helper_of(topo, T.cores, owner, j) == core:
+            seen[j] = seen.get(j, 0) + come
+            g.wait_ge(T.sem["fa%d" % j], seen[j])
+            c, o, s0, m = JOBS[j]
+            b, a = TILE[o + str(c)][:2]
+            x = T[b][:, a + 16 * s0:a + 16 * (s0 + m)]
+            g.remote_dma(x, x, T.sem["fb%d" % j], T.sem["back"], pid, rid, topo.mask(core, owner))
+    g.wait_ge(T.sem["back"], gone * sum(seen.values()) // come)
 
 
 def rank_program(g, core, T, topo):
     rank = T.rank_of(core)
     if rank is None:
+        for owner in T.cores:
+            if any(helper_of(topo, T.cores, owner, j) == core for j in range(len(JOBS))):
+                hand_back(g, core, T, topo, owner)
         return
-    ops = build(T, T.cores[(rank + 1) % len(T.cores)], topo, core)
-    if "p" not in PLAN:
-        PLAN["p"] = plan(ops)
-    order, deps = PLAN["p"][:2]
+    ops, order, deps = planned(T, topo, core)
     queues = {"pe": g.tensor, "dve": g.vector, "act": g.scalar, "pool": g, "sync": g.sync}
     total, mark, seen = {}, {}, {}
     for i in order:
         o = ops[i]
-        total[o["sem"]] = total.get(o["sem"], 0) + o["inc"]
-        mark[i] = total[o["sem"]]
-        if o["q"] == "none":
+        if o["sem"] is not None:
+            total[o["sem"]] = total.get(o["sem"], 0) + o["inc"]
+            mark[i] = total[o["sem"]]
+        if o["q"] not in queues:
             continue
         need = {}
         for j in deps[i]:
             p = ops[j]
-            if p["q"] == "pe" and o["q"] == "pe":
+            if p["sem"] is None or (p["q"] == "pe" and o["q"] == "pe"):
                 continue
             need[p["sem"]] = max(need.get(p["sem"], 0), mark[j])
         q = queues[o["q"]]
@@ -576,6 +835,6 @@ def rank_program(g, core, T, topo):
                 q.wait_ge(T.sem[s], v)
                 seen[(o["q"], s)] = v
         for ins in o["fn"](q):
-            ins.then_inc(T.sem[o["sem"]], o["inc"] if o["own"] else 1)
-    for s in ("pe", "dve", "act", "pool", "sent", "outs", "outa"):
+            ins.then_inc(T.sem[o["sem"]], 16 if o["own"] else 1)
+    for s in sorted(total):
         g.wait_ge(T.sem[s], total[s])

@@ -1,28 +1,45 @@
 import numpy as np
-from concourse.mybir import AluOpType, AxisListType, ActivationFunctionType
-from concourse.bass import DstId, RemoteDMATransfer
+from concourse.mybir import AluOpType, ActivationFunctionType
 
 V, L, TV, LV = 2048, 256, 4, 2
-XO = 512
-PIECES = {1: [("G", 16, "stq"), ("G", 48, "st"), ("G", 64, "st")], 0: [("G", 64, "st"), ("G", 32, "st"), ("G", 32, "st")]}
-SUMS = {1: [(0, 128)], 0: [(0, 128)]}
-TAIL_ON_VECTOR = ()
-ON_SCALAR = ("KU00", "KU01", "KU10", "KU11", "LU", "CS")
-MAIN = 0.3
-LATE = 0.6
-TAIL = [0.0, 0.0]
+CUTS = {1: {"Q": "16v 48s 64s", "R": "16v 48v 32v 32s", "P": "16v 48v 64v", "MQ": "64v 64v", "MR_": "64v 32s 32t",
+            "MP": "32t 32t 32t 32q"},
+        0: {"Q": "64s 64s", "R": "64v 32v 32v", "P": "64v 32v 32v", "MQ": "128v", "MR_": "64s 32s 32s",
+            "MP": "32t 32t 32t 32t"}}
+ORDER = {
+    0: {"dve": "-YM1! -THA1! Q1' R1' R2' MR_1' R1 R3' P2' P1' P3' -FB2! MQ1' MQ2' P1 P3 P2 R2 MQ1 R3 NC1' -MS1' HI1' -MS1 F1' FM1' "
+               "E1' K1' PR1' X1' K1 NC1 ZM1' HI1 F1 FM1 E1 PR2' MN1' PR1 XT1* X1 OF1' ZM1 PR3' PR3 LZ1 OU1' XZ1 PR2 XT2* MN1 OF1 "
+               "XT3* OU1 XT4* XT5*",
+        "act": "Q1' Q1 Q2' -N1! KU3' R1' KU3 -MA1' MR_1' MR_2' MP1' MP2' Q2 MP3' MP4' MR_1 MP1 MP2 SB1' DI1' MR_2 MP3 -MA1 SA1' "
+               "MR_3 MP4 NVA1! SB1 DI1 NVA2! LZ1' DF1' OZ1' XZ1' SA1 HH1' DF1 OZ1 LU1' HH1 +KU1' CS1' CS1 LU1",
+        "pe": "-YD1! -M1 DD1' R1' DD1 R2' D1 U1' D1' U2' U3' MR_1' P2' U4' P1' U5' MQ1' MQ2' U1 DF1' U2 MP1' P2 DE1' U3 P1 MQ1 MQ2 "
+              "U4 MR_1 DF1 OH2' MP1 DE1 ZB1' DIFF1' BOM1' DIFF2' ZL1' NVP1* OH2 DIFF1 OH1' HS1' ZB1 BOM1 OH1 ZL1 DIFF2 LS1' LS2' "
+              "HS1 LS1 LS2 M1'"},
+    1: {"dve": "Q1' P1' R1' R2' P2' P3' R3' MQ1' MQ2' P1 MR_1' R1 P2 P3 R2 MQ1 R3 NC1' -MS1' HI1' -MS1 F1' X1' FM1' E1' K1' PR1' K1 "
+               "CL1' NC1 HI1 ZM1' F1 FM1 CL1 E1 MN1' PR1 OF1' OU1' X1 ZM1 AB1! XT1* LZ1 XZ1 FB1! XT2* SS1! MN1 OF1 XT3* OU1 XT4* XT5*",
+        "act": "Q1' Q2' KU1 R1' Q1 MP1' MP2' Q2 MR_2' -MA1' MR_1' MP3' MP4' MR_1 MP1 -MA1 SB1' SA1' NV1' MR_2 DI1' MP2 MP3 MR_3 MP4 "
+               "NV1 SB1 DI1 SA1 LZ1' OZ1' DF1' XZ1' HH1' DF1 OZ1 AX1! HH1 +KU2 +KU1' +KU1 +KU2'",
+        "pe": "-M1 DD1' DD1 R2' U1' R1' U2' P2' U3' P1' U4' MQ1' MQ2' U5' MR_1' D1' U1 MP1' DF1' DE1' P2 P1 U2 U3 MQ2 MQ1 D1 U4 "
+              "MR_1 OH1' DF1 OH2' MP1 DE1 ZB1' DIFF1' BOM1' OH1 NVP1* ZL1' DIFF2' NVP2* OH2 LS1! LS2! ZB1 HS1' DIFF1 BOM1 ZL1 VV2! "
+              "DIFF2 VV1! HS1 ABP1! M1'"}}
+STEPS, NV = {}, {}
+for _c in CUTS:
+    STEPS[_c] = []
+    for _j, (_k, _v) in enumerate(CUTS[_c].items()):
+        _s = 0
+        for _x in _v.split():
+            STEPS[_c].append((_s + int(_x[:-1]), _j, _k, _s, _x[-1]))
+            _s += int(_x[:-1])
+    _up = lambda e, k: min(x[0] for x in STEPS[_c] if x[2] == k and x[0] >= e)
+    STEPS[_c] = sorted(STEPS[_c], key=lambda x: (x[3] if x[2] == "Q" else x[0] - 1 if x[2] in "PR" else
+                                                 max(_up(x[0], "P"), _up(x[0], "R")) - 0.5, x[1], x[0]))
+    NV[_c] = sum(x[0] - x[3] for x in STEPS[_c] if x[2] == "MR_" and x[4] == "v")
+ON_SCALAR = ("KU", "LU", "DI", "MA", "LZ1", "XZ1")
 PE_RUN = 8
-BLK = 32
-PAIRS = {"MR_": "QR", "MQ": "PQ", "MP": "PR"}
-JOBS, NF, NT, SIZES = [], {}, {}, {}
-for _c in (1, 0):
-    _s = 128
-    for _k, _m, _h in PIECES[_c]:
-        _s -= _m
-        JOBS += [(_c, o, _s, _m) for o in (PAIRS if _k == "F" else [x for x, h in zip(("MR_", "MP"), _h) if h == "f"])]
-    NF[_c] = sum(m for k, m, h in PIECES[_c] if k == "F")
-    NT[_c] = sum(m for k, m, h in PIECES[_c] if k == "G" and h[1] == "t")
-    SIZES[_c] = all(k == "G" and h[:2] in ("st", "bt") for k, m, h in PIECES[_c])
+BLK = 64
+XO = 16 * BLK
+ROWS = [(8 * u * (u + 1) * 128 // BLK, 16 * (u + 1)) for u in range(BLK // 16)]
+WIDE = ROWS[-1][0] + 128
 
 BF, F16, F32, I32, U16 = "bfloat16", "float16", "float32", "int32", "uint16"
 WIDTH = {BF: 2, F16: 2, U16: 2, F32: 4, I32: 4}
@@ -38,45 +55,42 @@ def _sb(dtype, tags, **kw):
             USED[dtype] = a + (n + 15) // 16 * 16
 
 
-_sb(BF, [""], ONE=512, TMP=128, IB=128, IBM=128, IB2K=128, IB8K=128, BO=128, SELT=2048, SEG=256, RST=128, CM=32, GI=16, BASE=64,
-    ZB=144, XT=XO + 4096, Y=1024, N=1024, YM=256, AB=16, NV0=768)
-_sb(F16, [""], IH=128, IHM=128, C0=128, OM=128, ONK=128, BOH=256, BOM=128, WS=160, ZH=144, MR=128, IND=256, MK=256, DG=1024,
-    TH3=384, THA=256, CB0=128, CB1=128)
-_sb(F32, [""], kc=1, pd=1, TH=1, CBF=256, T1=256, T2=256, T3=256, T4=16, T5=16, DGS=1024, CT=4096, FB=160, CS=16, CN=16, AS=1)
-_sb(I32, [""], thi=1, pi=1, pj=1, pk=1, eqi=8, CH=2048, LI=48)
-_sb(U16, [""], EQL=8, SS=112, LA=128)
-_sb(F16, "01", P=2048, Q=2048, R=2048, MQ=2048, MR_=2048, MP=2048, QT=2048)
-_sb(BF, "01", NV1=384)
+_sb(BF, [""], ONE=512, TMP=128, IB=128, IBM=128, IB2K=128, IB8K=128, BO=128, SELT=2048, SEG=WIDE, RST=128, CM=BLK, GI=16,
+    BASE=64, ZB=144, XT=XO + 4096, Y=1024, N=1024, YM=256, AB=16, AX=16, NVA=768)
+_sb(F16, [""], IH=128, IHM=128, J2K=256, J4K=256, I7=128, C_=128, ONH=128, ONK=128, BOH=128, BOM=128, WS=96, ZH=144, MR=128,
+    IND=WIDE + 16, MK=WIDE, DG=2048, BOX=256, TH2=256, CB=384, CL=256, THA=256)
+_sb(F32, [""], kc=1, pd=1, TH=1, THN=1, fu=1, fw=1, fb=1, fe=1, T1=128, T2=WIDE + 16, T3=WIDE, T4=16, T5=16, DV=16, FB=160,
+    CS=16, AS=1, MS=2048)
+_sb(I32, [""], thi=1, pi=1, pj=1, pk=1, pu=1, pb=1, eqi=8, CT=3584, LI=48)
+_sb(U16, [""], EQL=8, ENDS=2, SS=112, LA=128)
+_sb(F16, "01", P=2048, Q=2048, R=2048, MQ=2048, MR_=2048, MP=2048)
+_sb(BF, "01", NV=384)
 TWO = ["00", "01", "10", "11"]
-_sb(BF, TWO, DF=256, MN=256, XZ=128, HH=128)
-_sb(F16, TWO, K=384, NB=256, PR=512, NC=128, DI=128, HI=128, X=128, N2=128, NW=128, F=128, E=144, ZM=128, OF=8, PD=256)
-_sb(F32, TWO, FM=8)
-_sb(U16, TWO, KU=384, LU=24, OU=8)
+_sb(BF, TWO, DF=WIDE, MN=WIDE, XZ=128, HH=128)
+_sb(F16, TWO, K=512, PR=512, SA=128, SB=128, NC=128, DI=128, HI=128, X=128, E=144, ZM=128, OF=16, OZ=16, F=128)
+_sb(F32, TWO, FM=8, MA=128)
+_sb(U16, TWO, KU=384, LU=24, LZ=8, OU=8)
 SCRATCH = {ARENA[d]: ("sbuf", [128, n], d) for d, n in USED.items()}
-PLACE = {"D": ("A", 0), "U": ("E", 0), "DIFF": ("B", 0), "NT": ("B", 256), "ABP": ("B", 0), "YD": ("B", 256),
-         "OHQ": ("C", 0), "ZB": ("C", 128), "NS": ("C", 0), "LS": ("C", 256), "VV": ("C", 304), "CLT": ("C", 384),
-         "NVP": ("B", 256), "HS": ("A", 384), "MS": ("B", 256), "OHP": ("A", 0)}
+PLACE = {"D": ("A", 0), "ZL": ("A", 256), "ZB": ("A", 384), "ABP": ("A", 0), "YD": ("A", 256),
+         "DIFF": ("B", 0), "HS": ("B", 384), "M": ("B", 0),
+         "OH": ("C", 0), "DD": ("C", 256), "LS": ("C", 256), "VV": ("C", 304), "U": ("E", 0), "NVP": ("E", 0)}
 PSUM = [b + s for b in "ABCE" for s in "01"]
 for _k in PSUM:
     SCRATCH[_k] = ("psum", [128, 512], F32)
 
-SEMAPHORES = (["pe", "dve", "act", "pool", "outs", "sent", "back", "lc0", "lc1", "lli", "lx0", "lx1", "lth", "ly"]
-              + ["r%s%d" % (w, t) for w in "acy" for t in range(1, TV)]
-              + ["f%s%d" % (w, j) for w in "abs" for j in range(len(JOBS))])
+SEMAPHORES = (["pe", "dve", "act", "pool", "outs", "sent", "lc0", "lc1", "lli", "lx0", "lx1", "lth", "ly"]
+              + ["r%s%d" % (w, t) for w in "acy" for t in range(1, TV)])
 A = AluOpType
 ACT = ActivationFunctionType
-CYC, PCYC, GAT, SCA = 0.83 * 1.08, 0.42 * 1.08, 1.56, 3.8
-HOP_SAME, HOP_OTHER, LONGEST, ROUNDS, TRIES, NOISE = 60.0, 110.0, 4000.0, 25, 200, 1200.0
-CALL, FLY, FOLD_RATE, BACK_RATE = 900.0, 2000.0, 120.0, 240.0
-
-
-def helper_of(topo, cores, core, j):
-    free = [c for c in topo.cores_of(core) if c not in cores and topo.die(c) == topo.die(core)]
-    return free[j % len(free)]
+FIG = np.array([(0.83, 0.46, 1.56, 3.8, 120.0, 200.0, 1.0), (0.87, 0.50, 1.15, 2.5, 120.0, 200.0, 1.2),
+                (1.12, 0.62, 1.9, 5.0, 120.0, 200.0, 1.2)])
+CYC, PCYC, GAT, SCA, HOP_SAME, HOP_OTHER, SLOW = FIG.T
+CALL = 900.0
+SWAPS, HEAT, SEED = 20000, 0.003, 1
 
 
 def build(T, nxt, topo, core):
-    ops, now = [], {"part": None, "from": 0, "level": -1, "class": 0.0}
+    ops, now = [], {"part": None, "level": -1, "turn": 0}
 
     def tl(name, a=None, b=None, step=None, rows=None):
         buf, o, e = TILE[name]
@@ -96,13 +110,18 @@ def build(T, nxt, topo, core):
         return all(WIDTH[SCRATCH[s[0]][2]] == 2 for s in ss)
 
     def add(q, cost, rd, wr, fn, sem="", inc=1, lat=0.0, after=None, soft=None):
-        ops.append({"q": q, "cost": cost, "rd": rd, "wr": wr, "fn": fn, "sem": q if sem == "" else sem, "inc": inc, "lat": lat,
-                    "after": after, "soft": soft, "own": sem != "", "level": now["level"], "class": now["class"],
-                    "kind": (now["part"], len(ops) - now["from"]) if now["part"] else len(ops)})
+        ops.append({"q": q, "cost": cost + 0 * CYC, "rd": rd, "wr": wr, "fn": fn, "sem": q if sem == "" else sem, "inc": inc,
+                    "lat": lat * SLOW, "after": after, "soft": soft, "own": sem != "", "level": now["level"], "kind": len(ops)})
+        if now["part"] is not None:
+            x = (wr + rd)[0]
+            key = (q, now["tag"] if x[0] in PSUM else
+                   [k for k, v in TILE.items() if v[0] == x[0] and v[1] <= x[1] < v[2]][0].rstrip("01"))
+            now["seen"][key] = now["seen"].get(key, 0) + 1
+            ops[-1]["kind"] = (now["part"],) + key + (now["seen"][key],)
         return len(ops) - 1
 
     def part(name):
-        now["part"], now["from"] = name, len(ops)
+        now["part"], now["seen"] = name, {}
 
     def src(s, off):
         return ap(s) if off is None else ap(s).indirect(ap(off))
@@ -149,11 +168,11 @@ def build(T, nxt, topo, core):
             if bias is not None:
                 kw["bias"] = sc(bias)
             if scale is not None:
-                kw["scale"] = scale
+                kw["scale"] = sc(scale)
             if accum is not None:
                 kw["accum_out"] = ap(accum)
             return [q.activation(ap(o), src(i, off), func, **kw)]
-        add("act", 65 + cnt(o) * (GAT if off is not None else 1) * CYC, tups(i, off, bias), tups(o, accum), fn)
+        add("act", 65 + cnt(o) * (GAT if off is not None else 1) * CYC, tups(i, off, bias, scale), tups(o, accum), fn)
 
     def plus(name, o, i, x=0.0, off=None):
         if name in ON_SCALAR:
@@ -170,7 +189,11 @@ def build(T, nxt, topo, core):
                                each or (stop and j == len(terms) - 1))
             return [ins]
         cost = 30 + sum(max(min(64, cnt(x[0])), cnt(x[1])) * PCYC + 4 for x in terms)
-        rd = list(set(x[:3] + (1, 0, 128) for t in terms for x in t[:2]))
+        rd = []
+        for x in (x[:3] + (1, 0, 128) for t in terms for x in t[:2]):
+            if x not in rd:
+                rd.append(x)
+        now["tag"] = now.get(o[:2]) if start or stop else None
         if not (start or stop):
             add("pe", cost, rd + [o], [], fn)
         else:
@@ -205,29 +228,10 @@ def build(T, nxt, topo, core):
             q.remote_dma(ap(dst), ap(s), T.sem[sem], T.sem["sent"], pid, rid, topo.mask(core, nxt))
             return []
         k = add("pool", CALL, [s], [], fn, sem="sent", inc=len(eng), lat=lat)
-        add("none", 0, [], [dst], None, sem=sem, inc=len(eng), after=k)
+        add("none" + sem, 0, [], [dst], None, sem=sem, inc=len(eng), after=k)
 
-    def fold(job):
-        j = JOBS.index(job)
-        c, o, s0, m = job
-        hc = helper_of(topo, T.cores, core, j)
-        hr, hp = topo.addr(hc)[:2]
-        cols = lambda n: tl(n + str(c), 16 * s0, 16 * (s0 + m))
-        both = [cols(n) for n in PAIRS[o]]
-
-        def fn(q):
-            q.remote_dma_fused([RemoteDMATransfer(dst_ids=[DstId(rid=hr, pnc=hp)], dma_engine_mask=topo.mask(core, hc),
-                                                  remote_sem=T.sem["fa%d" % j], srcs=[ap(x) for x in both],
-                                                  dsts=[ap(cols(o))], alu_op=2)], local_sem=T.sem["fs%d" % j])
-            return []
-        size, ne = 128 * 32 * m, len(topo.engines(core, hc))
-        k = add("pool", CALL, both, [cols(o)], fn, sem=None)
-        ops[k]["job"] = j
-        k = add("out", size / FOLD_RATE, both, [], None, sem="fs%d" % j, inc=ne, lat=FLY, after=k)
-        add("back%d" % hc, CALL + size / BACK_RATE, [], [cols(o)], None, sem="fb%d" % j, inc=ne, lat=FLY, after=k)
-
-    load("sync", "lc0", [(tl("CH", 0, 1024), T.ch[:, 0:1024])], 4000)
-    load("act", "lc1", [(tl("CH", 1024, 2048), T.ch[:, 1024:2048])], 4000)
+    load("sync", "lc0", [(tl("CT", 0, 1024), T.ch[:, 0:1024])], 4000)
+    load("act", "lc1", [(tl("CT", 1024, 2048), T.ch[:, 1024:2048])], 4000)
     load("sync", "lli", [(tl("LI", 16 * a, 16 * a + 16), x[:]) for a, x in enumerate((T.sb, T.ia, T.ic))], 3000)
     load("act", "lx0", [(tl("XT", XO, XO + 1024), T.x[:, 0:1024])], 5000)
     load("sync", "lx1", [(tl("XT", XO + 1024, XO + V), T.x[:, 1024:2048])], 5000)
@@ -235,46 +239,43 @@ def build(T, nxt, topo, core):
     load("sync", "ly", [(tl("Y", 0, 256), T.y[:])], 5000)
 
     LO, HI = (0, 64), (64, 128)
-    one = lambda n: tl("ONE", 0, n)
+    one = lambda n, rows=None: tl("ONE", 0, n, rows=rows)
+    nb = 128 // BLK
     fill(tl("ONE"), 1.0)
     select(tl("IB"), one(128), [[-1, 128]], A.is_equal, 0, 1)
     select(tl("TMP"), one(128), [[-16, 8], [0, 16]], A.is_ge, 0, 1)
     select(tl("BO"), tl("TMP"), [[16, 8], [0, 16]], A.is_ge, 15, -1)
+    iota(tl("pi"), [[0, 1]], 0, 1)
+    iota(tl("T1"), [[0, 8], [1, 16]], 0, 0)
+    iota(tl("eqi"), [[1, 8]], 0, 0)
+    iota(tl("DV", 0, 8), [[512, 4], [128, 2]], 256, 1)
+    iota(tl("DV", 8, 16), [[-512, 4], [-128, 2]], -256, -1)
+    for u, (a, w) in enumerate(ROWS):
+        iota(tl("T2", a, a + w * nb), [[BLK // 16, nb], [0, w]], u, 0)
+        iota(tl("T3", a, a + w * nb), [[0, nb], [1, w]], -16 * u, 0)
+    iota(tl("T2", WIDE, WIDE + 16), [[1, 16]], 0, 0)
+    iota(tl("T4"), [[16, 16]], 0, 0)
+    iota(tl("T5", 0, 8), [[16, BLK // 16], [0, nb]], 129, 0)
     for r in range(0, 16, 2):
         select(tl("SELT", 128 * r, 128 * r + 256), one(256), [[-1, 2], [-16, 8], [0, 16]], A.is_equal, -r, 1)
-    iota(tl("pi"), [[0, 1]], 0, 1)
-    iota(tl("T1", 0, 128), [[0, 8], [1, 16]], 0, 0)
-    iota(tl("T2"), [[1, 8], [0, 32]], 0, 0)
-    iota(tl("T3"), [[0, 4], [-16, 2], [1, 32]], 0, 0)
-    iota(tl("T4"), [[16, 16]], 0, 0)
-    iota(tl("T5", 0, 8), [[0, 4], [16, 2]], 129, 0)
-    for t in range(TV):
-        iota(tl("DGS", 256 * t, 256 * t + 256), [[1, 256]], 256 + 512 * t, 0)
-    iota(tl("eqi"), [[1, 8]], 0, 0)
-    for name, f in (("IBM", -1.0), ("IB2K", 2048.0), ("IB8K", -8192.0), ("IH", 1.0), ("IHM", -1.0)):
+    for name, f in (("IBM", -1.0), ("IB2K", 2048.0), ("IB8K", -8192.0), ("IH", 1.0), ("IHM", -1.0), ("I7", -7.5)):
         ts(tl(name), tl("IB"), f, A.mult)
-    copy(tl("EQL"), tl("eqi"))
-    ts(tl("C0"), tl("T1", 0, 128), 0.0, A.is_equal)
-    for name, f in (("OM", -1.0), ("ONK", 1.0 / 1024)):
-        ts(tl(name), one(128), f, A.mult)
     for j in range(2):
-        copy(tl("BOH", 128 * j, 128 * j + 128), tl("BO"))
+        ts(tl("J2K", 128 * j, 128 * j + 128), tl("IB"), 2048.0 * (1 - 2 * j), A.mult)
+        ts(tl("J4K", 128 * j, 128 * j + 128), tl("IB"), 4096.0 * (1 - 2 * j), A.mult)
+    copy(tl("EQL"), tl("eqi"))
+    ts(tl("C_"), tl("T1"), 0.0, A.is_equal)
+    copy(tl("ONH"), one(128))
+    ts(tl("ONK"), one(128), 1.0 / 1024, A.mult)
+    copy(tl("BOH"), tl("BO"))
     ts(tl("BOM"), tl("BO"), -1.0, A.mult)
-    e = 1.0 / 1024
-    strip = [0, 2, 0, 0, 2 * e, -1, -1, 0, -e, 0, -1, -e, 1, -1, 0, 1, 0, 0, -e]
-    ts(tl("WS"), one(160), 0.0, A.mult)
-    window = lambda j: tl("WS", 8 * j, 8 * j + 24)
-    weights, used = {}, set()
-    for c in range(2):
-        at = ({"MR_": 14, "MP": 15, "MQ": 2, "P": 16} if SIZES[c] else
-              {"R": 12 if NT[c] == 128 else 5, "P": 6, "MR_": 0, "MQ": 2, "MP": 1})
-        if NF[c]:
-            at["Q"] = 9
-        weights[c] = {n: window(j) for n, j in at.items()}
-        used |= set(j + i for j in at.values() for i in range(3))
-    for j in sorted(used):
-        if strip[j]:
-            ts(tl("WS", 8 * j, 8 * j + 8), tl("BO", 0, 128, 16), float(strip[j]), A.mult)
+    e = 1.0 / 2048
+    for j in range(2):
+        ts(tl("BOX", 128 * j, 128 * j + 128), tl("BO"), -e if j else -1.0, A.mult)
+    weight = {}
+    for j, f in enumerate((1.0, -1.0, e, 4 * e, -2 * e)):
+        weight[f] = tl("WS", 16 * j, 16 * j + 8)
+        ts(weight[f], tl("BO", 0, 128, 16), f, A.mult)
     fill(tl("ZB"), 0.0)
     copy(tl("ZB", 15, 143, 16), tl("BO", 0, 128, 16))
     copy(tl("ZH"), tl("ZB"))
@@ -284,43 +285,51 @@ def build(T, nxt, topo, core):
     copy(kc, tl("pj"))
     ts(tl("pk"), tl("pi"), 4, A.arith_shift_right)
     copy(tl("pd"), tl("pk"))
-    ts(tl("MR"), tl("T1", 0, 128), kc, A.is_equal)
+    ts(tl("MR"), tl("T1"), kc, A.is_equal)
     ts(tl("IND"), tl("T2"), tl("pd"), A.is_equal)
     ts(tl("MK"), tl("T3"), kc, A.is_ge, 8192.0, A.mult)
     fill(tl("SEG"), 0.0)
-    fill(tl("SEG", 0, 256, BLK), 1.0e12)
-    ts(tl("SEG", BLK - 1, 256, BLK), tl("T5", 0, 8), kc, A.add, -16.0, A.mult)
+    for u, (a, w) in enumerate(ROWS):
+        fill(tl("SEG", a, a + w * nb, w), 1.0e12)
+        ts(tl("SEG", a + w - 1, a + w * nb, w), tl("T5", nb * u, nb * u + nb), kc, A.add, -16.0, A.mult)
+    ts(tl("pu"), tl("pi"), BLK // 16 - 1, A.bitwise_and)
+    ts(tl("pb"), tl("pi"), 7, A.bitwise_and, BLK // 32, A.arith_shift_right)
+    ts(tl("fu"), tl("pu"), 1.0, A.add)
+    ts(tl("fw"), tl("pu"), nb / 2.0, A.mult, 1.0, A.add)
+    tt(tl("fb"), tl("pb"), tl("fw"), A.add)
+    ts(tl("fe"), tl("fb"), tl("fu"), A.mult, 16.0, A.mult)
+    ts(tl("ENDS", 0, 1), tl("fe"), -1.0, A.add)
     fill(tl("RST"), 0.0)
     fill(tl("RST", 0, 128, 16), -1.0e4)
     fill(tl("CM"), -160.0)
     ts(tl("GI"), tl("T4"), kc, A.add)
-    for rows, (f, g) in ((LO, (1032.0 / 64, 2056.0 / 64)), (HI, (-1.0 / 4096, -17.0 / 4096))):
-        fill(tl("CBF", rows=rows), g)
-        for c in range(2):
-            if NF[c]:
-                fill(tl("CBF", 128 * c + 128 - NF[c], 128 * c + 128, rows=rows), f)
     copy(tl("TH"), tl("thi"))
+    ts(tl("THN"), tl("TH"), 0.5, A.add, -1.0, A.mult)
+    ts(tl("TH2", 0, 128), tl("IH"), tl("THN"), A.mult)
+    ts(tl("TH2", 128, 256), tl("IH"), tl("THN"), A.mult, e, A.mult)
+    ts(tl("CB", 0, 128), one(128), -8.0, A.mult)
+    ts(tl("CB", 128, 256), one(128), 0.0, A.mult)
+    ts(tl("CB", 256, 384, rows=LO), one(128, LO), 2056.0 / 64, A.mult)
+    ts(tl("CB", 256, 384, rows=HI), one(128, HI), -17.0 / 4096, A.mult)
     for t in range(TV):
         fill(tl("BASE", 16 * t, 16 * t + 16), 1.0 + t / 4)
-    for j in range(2):
-        copy(tl("DG", 512 * j, 512 * j + 512), tl("DGS", 512 * j, 512 * j + 512))
-    ts(tl("TH3", 256, 384), one(128), 0.0, A.mult)
-    for c in range(2):
-        copy(tl("CB%d" % c), tl("CBF", 128 * c, 128 * c + 128))
-        ts(tl("TH3", 128 * c, 128 * c + 128), tl("IH"), tl("TH"), A.mult)
-        for lev in range(2):
-            copy(tl("E%d%d" % (c, lev), 0, 16), one(16))
-        for j in range(0, 16 * (128 - NF[c]) if any(x[0] == c for x in JOBS) else 0, 512):
-            w = min(512, 16 * (128 - NF[c]) - j)
-            ts(tl("Q%d" % c, j, j + w), one(w), 0.0, A.mult)
+    for j in range(16):
+        act(tl("DG", 128 * j, 128 * j + 128), tl("IH"), ACT.Identity, scale=tl("DV", j, j + 1))
+    for x in TWO:
+        copy(tl("E" + x, 0, 16), one(16))
+        if x[1] == "0":
+            copy(tl("K" + x, 0, 128), one(128))
     copy(tl("SS", 96, 112), tl("LI", 0, 16))
     copy(tl("LA", 0, 32), tl("LI", 16, 48))
     copy(tl("FB", 0, 32), tl("LI", 0, 32))
-    for j in range(0, V, 512):
-        plus("CT", tl("CT", j, j + 512), tl("CH", j, j + 512))
 
     def psum(name, c, a, b):
+        now[(PLACE[name][0] + str(c), PLACE[name][1] + a)] = name
         return (PLACE[name][0] + str(c), PLACE[name][1] + a, PLACE[name][1] + b, 1, 0, 128)
+
+    def lists(LS, x, w):
+        mm(LS, [(sel(r), sub(x, r, cnt(x), 16)) for r in range(8)], stop=False)
+        mm(LS, [(tl("I7"), tl("ONH", 0, w), sub(LS, 0, w))] + [(sel(r), sub(x, r, cnt(x), 16)) for r in range(8, 16)], start=False)
 
     def chunk(c, t, lev):
         lim = V + 512 * t
@@ -328,153 +337,101 @@ def build(T, nxt, topo, core):
         st = lambda name, *a, **k: tl(name + str(c), *a, **k)
         lv = lambda name, *a, **k: tl("%s%d%d" % (name, c, lev), *a, **k)
         ps = lambda name, a, b: psum(name, c, a, b)
-        xw = tl("XT", XO, XO + lim)
-        cw = tl("CH") if t == 0 else tl("CT", 0, lim)
+        xw, cw = tl("XT", XO, XO + lim), tl("CT", 0, lim - 256 if t and not lev else lim)
         if lev == 0:
-            for a, at in ((0, ("SS", 96 - 32 * t)), (2, ("LA", 32 * t + 16)), (1, ("LA", 32 * t))):
-                plus("KU%d0" % c, lv("KU", 128 * a, 128 * a + 128), cw, off=tl(at[0], at[1] + 8 * c, at[1] + 8 * c + 8))
+            for a, at in ((1, ("SS", 96 - 32 * t)), (0, ("LA", 32 * t + 16)), (2, ("LA", 32 * t))):
+                plus("KU", lv("KU", 128 * a, 128 * a + 128), cw, off=tl(at[0], at[1] + 8 * c, at[1] + 8 * c + 8))
         else:
-            nodes, nv = tl("LU%d0" % c), st("NV1")
-            plus("KU%d1" % c, lv("KU"), cw, off=nodes)
-            now["class"] = LATE
-            act(nv, xw, ACT.Copy, off=nodes)
-        now["class"] = LATE
-        plus("K", lv("K"), lv("KU"), -2048.0)
-        now["class"] = MAIN
-        kid = lambda name, s0, m: lv("KU", 128 * "QPR".index(name) + s0, 128 * "QPR".index(name) + s0 + m)
-        done, turn = 0, 0
-        for kind, m, how in PIECES[c]:
-            s0 = done if SIZES[c] else 128 - done - m
-            done += m
-            big = lambda name: st(name, 16 * s0, 16 * (s0 + m))
-            if kind == "F":
-                for name in "QRP":
-                    x = -32.0 + (1.0 / 64 if name == "P" else 0.0)
-                    if name in how:
-                        ts(big(name), xw, x, A.add, off=kid(name, s0, m))
-                    else:
-                        act(big(name), xw, ACT.Identity, bias=x, off=kid(name, s0, m))
-                for o in PAIRS:
-                    fold((c, o, s0, m))
-                continue
-            size = ACT.Abs if SIZES[c] else ACT.Relu
-            if how[2:] == "q":
-                copy(big("QT"), xw, off=kid("Q", s0, m))
+            plus("KU", lv("KU"), cw, off=tl("LU%d0" % c))
+            act(st("NV"), xw, ACT.Copy, off=tl("LU%d0" % c))
+        kq = 256 if lev == 0 else 128
+        plus("K", lv("K", 128, kq + 256), lv("KU", 256 - kq, 384), -2048.0)
+        kid = lambda name, s0, m: lv("KU", 128 * "RQP".index(name) + s0, 128 * "RQP".index(name) + s0 + m)
+        for end, j, step, s0, how in sorted(STEPS[c], key=lambda x: lev == 0 and x[2] == "MP"):
+            m = end - s0
+            big = lambda name: st(name, 16 * s0, 16 * end)
+            if step in "QR" and how == "s":
+                act(big(step), xw, ACT.Copy, off=kid(step, s0, m))
+            elif step == "Q":
+                copy(big("Q"), xw, off=kid("Q", s0, m))
+            elif step in "RP":
+                tt(big(step), xw, big("Q"), A.subtract, off=kid(step, s0, m))
+            elif step == "MQ":
+                ts(big("MQ"), big("P"), 1.0 / 64 - 32, A.add, -32.0, A.max)
+            elif how == "s":
+                act(big("MR_"), big("R"), ACT.Abs)
+            elif how == "v":
+                ts(big("MR_"), big("R"), 0.0, A.max, 2.0, A.mult)
             else:
-                act(big("QT"), xw, ACT.Copy, off=kid("Q", s0, m))
-            if how[0] == "b":
-                act(big("R"), xw, ACT.Copy, off=kid("R", s0, m))
-            else:
-                tt(big("R"), xw, big("QT"), A.subtract, off=kid("R", s0, m))
-            tt(big("P"), xw, big("QT"), A.subtract, off=kid("P", s0, m))
-            if how[0] == "b":
-                for j in range(0, 16 * m, 512):
-                    w = min(512, 16 * m - j)
-                    u = psum("U", turn % 2, 0, w)
-                    turn += 1
-                    mm(u, [(tl("IH"), sub(big("R"), j, j + w)), (tl("IHM"), sub(big("QT"), j, j + w))])
-                    act(sub(big("MR_"), j, j + w), u, size)
-            elif how[0] == "f":
-                fold((c, "MR_", s0, m))
-            elif how[0] == "s":
-                act(big("MR_"), big("R"), size)
-            else:
-                ts(big("MR_"), big("R"), 0.0, A.max)
-            ts(big("MQ"), big("P"), 1.0 / 64 - 32, A.add, -32.0, A.max)
-            if how[1] == "f":
-                fold((c, "MP", s0, m))
-            elif how[1] == "t":
-                for j in range(0, 16 * m, 512):
-                    w = min(512, 16 * m - j)
-                    cut = lambda name: sub(big(name), j, j + w)
-                    u = psum("U", turn % 2, 0, w)
-                    turn += 1
-                    mm(u, [(tl("IH"), cut("P")), (tl("IHM"), cut("R"))] + ([(tl("IH"), cut("QT"))] if how[0] == "b" else []))
-                    act(cut("MP"), u, size)
-            else:
-                tt(big("MP"), big("P"), big("R"), A.max)
-        now["class"] = TAIL[c]
-        D = ps("D", 0, 384)
-        mm(D, [(tl("OM"), tl("TH3"))] + ([(tl("OM"), tl("THA"), sub(D, 0, 256))] if t else []), stop=False)
-        if 0 < NT[c] < 128:
-            mm(D, [(st("R", k, 16 * NT[c], 16), weights[c]["MP"], sub(D, k, 384, 16, rows=(0, NT[c]))) for k in range(16)],
-               start=False, stop=False)
-        for name in weights[c]:
-            for a, b in SUMS[c]:
-                run = PE_RUN * (2 if b - a < 64 else 1)
-                for k0 in range(0, 16, run):
-                    mm(D, [(st(name, 16 * a + k, 16 * b, 16), weights[c][name], sub(D, k, 384, 16, rows=(a, b)))
-                           for k in range(k0, k0 + run)], start=False, stop=False)
-        mm(D, [(st("CB"), tl("ONK"), sub(D, 256, 384))], start=False)
-        D3, nal, nbe = sub(D, 256, 384), lv("NB", 0, 128), lv("NB", 128, 256)
-        if "NB" in TAIL_ON_VECTOR:
-            ts(lv("NB"), sub(D, 0, 256), 0.5, A.is_lt)
-        else:
-            act(lv("NB"), sub(D, 0, 256), ACT.Sigmoid, bias=256.0, scale=-512.0)
-        if "DI" in TAIL_ON_VECTOR:
-            copy(lv("DI"), D3)
-        else:
-            act(lv("DI"), D3, ACT.Copy)
-        tt(lv("NC"), nal, nbe, A.max)
+                u = psum("U", now["turn"] % 2, 0, 16 * m)
+                now["turn"] += 1
+                if step == "MR_":
+                    mm(u, [(tl("IH"), big("R")), (tl("IHM"), big("Q"))])
+                else:
+                    mm(u, [(tl("IH"), big("P")), (tl("IHM"), big("R"))] + ([(tl("IH"), big("Q"))] if how == "q" else []))
+                act(big(step), u, ACT.Abs)
+        D1, D23 = ps("D", 0, 128), ps("DD", 0, 256)
+        D2, D3 = sub(D23, 0, 128), sub(D23, 128, 256)
+        mm(D1, [(tl("ONK"), tl("CB", 0, 128)), (tl("ONH"), tl("TH2", 128, 256))]
+           + ([(tl("ONH"), tl("THA", 128, 256))] if t else []), stop=False)
+        mm(D23, [(tl("ONK"), tl("CB", 128, 384)), (tl("ONH"), tl("TH2", 0, 128), D2)]
+           + ([(tl("ONH"), tl("THA", 0, 128), D2)] if t else []), stop=False)
+        now[D1[:2]], now[D2[:2]] = "DE", "DF"
+        for name, f, o, b in (("P", -2 * e, D3, 128), ("MQ", 4 * e, D3, 128), ("R", -1.0, D2, NV[c]), ("MR_", 1.0, D2, 128),
+                              ("MP", e, D1, 128)):
+            for k0 in range(0, 16 if b else 0, PE_RUN):
+                mm(o, [(st(name, k, 16 * b, 16), weight[f], sub(o, k, 128, 16, rows=(0, b))) for k in range(k0, k0 + PE_RUN)],
+                   start=False, stop=name in ("MR_", "MP") and k0 + PE_RUN == 16)
+        act(lv("SB"), D2, ACT.Sign, scale=-1.0)
+        plus("DI", lv("DI"), D3)
+        tt(lv("NC"), D1, lv("SB"), A.is_lt)
+        act(lv("SA"), D1, ACT.Sign, bias=-1.0, scale=-1.0)
         tt(lv("HI"), lv("DI"), lv("NC"), A.subtract)
-        scan(lv("F"), tl("RST"), lv("HI"), A.add, A.max)
         tt(lv("X"), D3, lv("HI"), A.is_lt)
+        scan(lv("F"), tl("RST"), lv("HI"), A.add, A.max)
         copy(lv("FM"), lv("F", 15, 128, 16))
         tt(lv("E", 1, 129), lv("FM"), lv("F"), A.is_equal, off=tl("EQL"))
-        star = [(lv("E", 1, 129), tl("IH")), (lv("E", 0, 128), tl("IHM")), (tl("C0"), tl("IH"))]
-        na = 3 if lev == 0 else 1
-        prq = lv("PR", 128, 256)
-        mm(ps("OHQ", 0, 128), star)
-        tt(prq, ps("OHQ", 0, 128), lv("K", 0, 128), A.mult)
-        if lev == 0:
-            for a in (1, 2):
-                tt(lv("PR", 128 + 128 * a, 256 + 128 * a), ps("OHQ", 0, 128), lv("K", 128 * a, 128 * a + 128), A.mult)
-            tt(lv("NW"), ps("OHQ", 0, 128), tl("DG", 256 * t + 128 * c, 256 * t + 128 * c + 128), A.mult)
-        mm(ps("CLT", 0, 128), [(lv("NC"), tl("IH"))])
-        act(lv("PR", 0, 128), ps("CLT", 0, 128), ACT.Copy)
-        LS = ps("LS", 0, 8 + 8 * na)
-        mm(LS, [(sel(r), lv("PR", r, 128 + 128 * na, 16)) for r in range(16)])
-        plus("LU", lv("LU", 0, 8 * na), sub(LS, 8, 8 + 8 * na), 2048.0)
-        if lev == 0:
-            plus("CS", tl("CS", 8 * c, 8 * c + 8), sub(LS, 0, 8))
-        else:
-            tt(tl("CN", 8 * c, 8 * c + 8), sub(LS, 0, 8), tl("CS", 8 * c, 8 * c + 8), A.min)
-        mm(ps("ZB", 0, 128), [(prq, tl("BOH", 0, 128))])
+        star = [(lv("E", 1, 129), 1), (lv("E", 0, 128), -1), (tl("C_"), 1)]
+        OH = ps("OH", 128, 256)
+        mm(ps("OH", 0, 128), [(lv("NC"), tl("IH"))])
+        mm(OH, [(x, tl("IH" if f > 0 else "IHM")) for x, f in reversed(star)])
+        prq = lv("PR", kq, kq + 128)
+        tt(prq, OH, lv("K", kq, kq + 128), A.mult)
+        mm(ps("ZB", 0, 128), [(prq, tl("BOH"))])
         tt(lv("ZM"), ps("ZB", 0, 128), tl("MR"), A.mult)
-        DIFF = ps("DIFF", 0, 256)
-        mm(DIFF, [(tl("IH"), tl("MK"))]
-           + [(tl("BOM"), sub(prq, BLK * (j // 2), BLK * (j // 2) + BLK), sub(DIFF, BLK * j, BLK * j + BLK)) for j in range(8)],
-           stop=False)
-        mm(DIFF, [(lv("ZM"), tl("IND"))], start=False)
-        if "DF" in TAIL_ON_VECTOR:
-            ts(lv("DF"), DIFF, 0.0, A.not_equal, 8192.0, A.mult)
-        else:
-            act(lv("DF"), DIFF, ACT.Abs, scale=8192.0)
+        DIFF, ZL = ps("DIFF", 0, WIDE), ps("ZL", 0, 16)
+        mm(DIFF, [(tl("IH"), tl("MK"))], stop=False)
+        mm(DIFF, [(tl("BOM"), sub(prq, BLK * b, BLK * b + w), sub(DIFF, a + w * b, a + w * b + w))
+                  for a, w in ROWS for b in range(nb)], start=False, stop=False)
+        mm(ZL, [(lv("ZM"), tl("IND", WIDE, WIDE + 16))])
+        mm(DIFF, [(lv("ZM"), tl("IND", 0, WIDE))], start=False)
+        plus("LZ%d" % c, lv("LZ"), sub(ZL, 0, 8), 2048.0)
+        act(lv("DF"), DIFF, ACT.Abs, scale=8192.0)
+        act(lv("OZ"), ZL, ACT.Copy)
         scan(lv("MN"), tl("SEG"), lv("DF"), A.add, A.min)
-        tt(lv("OF"), sub(LS, 8, 16), lv("MN", BLK - 1, 256, BLK), A.min)
-        plus("OU", lv("OU"), lv("OF"), 2048.0 + XO)
-        act(lv("XZ"), xw, ACT.Copy, off=lv("LU", 0, 8))
+        tt(lv("OF"), lv("MN"), lv("OZ"), A.min, off=tl("ENDS", 0, 1))
+        plus("OU", lv("OU"), lv("OF", 0, 8), 2048.0 + XO)
+        if lev == 0:
+            tt(lv("PR", 384, 512), OH, lv("K", 384, 512), A.mult)
+            tt(lv("PR", 0, 256), ps("OH", 0, 256), lv("K", 0, 256), A.mult)
+            LS = ps("LS", 0, 32)
+            lists(LS, lv("PR"), 8)
+            plus("LU", lv("LU"), sub(LS, 8, 32), 2048.0)
+            act(tl("CS", 8 * c, 8 * c + 8), sub(LS, 0, 8), ACT.Relu, scale=-64.0)
+        else:
+            plus("CL", tl("CL", 128 * c, 128 * c + 128), ps("OH", 0, 128))
+        plus("XZ%d" % c, lv("XZ"), xw, off=lv("LZ"))
         mm(ps("HS", 0, 128), [(tl("IB"), tl("Y", 256 * t + 128 * c, 256 * t + 128 * c + 128)), (tl("IB"), lv("XZ"))])
         act(lv("HH"), ps("HS", 0, 128), ACT.Identity, bias=159.75, scale=0.5)
-        now["class"] = LATE
-        takeq = [(nal, tl("IH")), (lv("X"), tl("IH"))]
-        terms = [(tl("IH"), lv("K", 128, 256)), (tl("IH"), lv("PD", 0, 128)), (tl("IHM"), lv("PD", 128, 256))]
+        M = [(tl("IH"), lv("K", kq, kq + 256)), (lv("SA"), tl("J2K")), (lv("X"), tl("J4K"))]
         if lev == 0:
-            mm(ps("NT", 0, 128), takeq + star)
-            act(lv("N2", 0, 128), ps("NT", 0, 128), ACT.Sigmoid, bias=-128.0, scale=256.0)
-            for a in range(2):
-                tt(lv("PD", 128 * a, 128 * a + 128), lv("N2", 0, 128), lv("K", 128 * a, 128 * a + 128), A.mult)
-            terms += [(tl("IHM"), prq), (tl("IH"), lv("NW"))]
-        else:
-            for a in range(2):
-                mm(ps("NS", 128 * a, 128 * a + 128), takeq)
-            tt(lv("PD"), ps("NS", 0, 256), lv("K", 0, 256), A.mult)
-        mm(ps("MS", 0, 128), terms)
-        act(tl("CT", n, n + 128), ps("MS", 0, 128), ACT.Identity, bias=2048.0)
-        if lev == 1:
-            mm(ps("NVP", 128, 256), [(tl("IB"), sub(nv, 0, 128)), (tl("IB"), sub(nv, 128, 256)), (tl("IBM"), sub(nv, 256, 384))])
-            ts(tl("XT", XO + n, XO + n + 128), ps("NVP", 128, 256), 0.0, A.max, 63.0, A.min)
-        now["class"] = 0.0
+            M += [(tl("IHM"), lv("PR", 256, 512))]
+            for x, f in star:
+                j = 128 * (2 * t + c + (0 if f > 0 else 8))
+                M += [(x, tl("DG", j, j + 128), ps("M", 128 * a, 128 * a + 128)) for a in range(2)]
+        mm(ps("M", 0, 256), M)
+        plus("MA", lv("MA"), ps("M", 0, 128))
+        tt(tl("MS", n - V, n - V + 128), ps("M", 128, 256), lv("MA"), A.max)
 
     for t in range(TV):
         lim = V + 512 * t
@@ -484,31 +441,38 @@ def build(T, nxt, topo, core):
             send(tl("LA", 32 * t + 48, 32 * t + 64), bl, "rc%d" % (t + 1), 3000)
         for lev in range(LV):
             n = lim + 256 * lev
-            part("l%d" % lev)
             now["level"] = 2 * t + lev
             if lev == 0:
-                now["class"] = LATE
-                xw, nv, nvp = tl("XT", XO, XO + lim), tl("NV0"), psum("NVP", 1, 0, 256)
+                part((0, 3))
+                xw, nv = tl("XT", XO, XO + lim), tl("NVA")
                 act(sub(nv, 0, 256), xw, ACT.Copy, off=bl)
                 act(sub(nv, 256, 768), xw, ACT.Copy, off=tl("LA", 32 * t, 32 * t + 32))
-            now["class"] = 0.0
             for c in (1, 0):
+                part((lev, c))
                 chunk(c, t, lev)
+            part((lev, 2))
+            nvp, x = psum("NVP", 1, 0, 256), psum("NVP", 1, 128, 256)
             if lev == 0:
-                now["class"] = LATE
                 mm(nvp, [(tl("IB"), sub(nv, 0, 256)), (tl("IB"), sub(nv, 256, 512)), (tl("IBM"), sub(nv, 512, 768))])
-                ts(tl("XT", XO + n, XO + n + 256), nvp, 0.0, A.max, 63.0, A.min)
-                now["class"] = 0.0
+            else:
+                for c in (1, 0):
+                    mm(sub(nvp, 128 * c, 128 * c + 128),
+                       [(tl("IB" if a else "IBM"), tl("NV%d" % c, 128 * a, 128 * a + 128)) for a in range(3)])
+            ts(tl("XT", XO + n, XO + n + 256), nvp, 0.0, A.max, 63.0, A.min)
             for c in (1, 0):
                 for b0 in range(128 - BLK, -1, -BLK):
                     scatter_add(tl("XT", 0, XO + lim), tl("OU%d%d" % (c, lev), b0 // 16, (b0 + BLK) // 16),
                                 tl("HH%d%d" % (c, lev), b0, b0 + BLK), tl("CM"))
-            store(T.co[:, n - V:n - V + 256], tl("CT", n, n + 256), 2500)
-        part("end")
-        act(tl("AB"), tl("CN"), ACT.Sigmoid, bias=1920.0, scale=-256.0, accum=tl("AS"))
+            store(T.co[:, n - V:n - V + 256], tl("MS", n - V, n - V + 256), 2500)
+            if t < TV - 1:
+                select(tl("CT", n, n + 256), tl("MS", n - V, n - V + 256), [[0, 256]], A.is_ge, 0, 0)
+        part((1, 3))
+        LS = psum("LS", 1, 0, 16)
+        lists(LS, tl("CL"), 16)
+        tt(tl("AB"), LS, tl("CS"), A.is_lt)
         for a in range(2):
             mm(psum("VV", 1, 16 * a, 16 * a + 16),
-               [(tl("IB8K"), tl("AB")), (tl("IB"), tl("GI")), (tl("IB2K"), tl("BASE", 16 * t, 16 * t + 16))])
+               [(tl("IB"), tl("GI")), (tl("IB2K"), tl("BASE", 16 * t, 16 * t + 16)), (tl("IB8K"), tl("AB"))])
         fb = tl("FB", 32 * t + 32, 32 * t + 64)
         tt(fb, psum("VV", 1, 0, 32), tl("FB", 32 * t, 32 * t + 32), A.max)
         ABP, YD = psum("ABP", 1, 0, 256), psum("YD", 1, 0, 256)
@@ -523,8 +487,9 @@ def build(T, nxt, topo, core):
             send(la, tl("SS", 80 - 32 * t, 96 - 32 * t), "ra%d" % (t + 1), 3000)
             send(tl("Y", 256 * t + 256, 256 * t + 512), yn, "ry%d" % (t + 1), 3500)
             copy(sub(fb, 16, 32), la)
-            ts(tl("THA"), tl("BOH"), tl("AS"), A.mult)
-    now["part"] = None
+            act(tl("AX"), tl("AB"), ACT.Copy, accum=tl("AS"))
+            ts(tl("THA"), tl("BOX"), tl("AS"), A.mult)
+    part((2, 3))
     store(T.so[:], tl("FB", 128, 144), 2500)
     store(T.yo[:], tl("N", 768, 1024), 2500)
     store(T.xo[:, 3584:4096], tl("XT", XO + 3584, XO + 4096), 2500)
@@ -534,7 +499,7 @@ def build(T, nxt, topo, core):
 
 
 def plan(ops):
-    n = len(ops)
+    n, sets = len(ops), range(len(FIG))
     deps = [set() for _ in range(n)]
     hist = {}
     cell = lambda s: [(s[0], b) for b in range(s[1] // 256, (s[2] - 1) // 256 + 1)]
@@ -557,182 +522,118 @@ def plan(ops):
         if o["after"] is not None:
             deps[i].add(o["after"])
         o["banks"] = set(s[0] for s in o["rd"] + o["wr"] if s[0] in PSUM)
-    pre0 = [deps[i] | ({ops[i]["soft"]} if ops[i]["soft"] is not None else set()) for i in range(n)]
+    pre = [deps[i] | ({ops[i]["soft"]} if ops[i]["soft"] is not None else set()) for i in range(n)]
     succ = [[] for _ in range(n)]
     for i in range(n):
-        for j in pre0[i]:
+        for j in pre[i]:
             succ[j].append(i)
 
-    def hop(j, i):
+    def hop(j, i, m):
         if ops[i]["soft"] == j:
             return 0.0
         if ops[j]["q"] == ops[i]["q"]:
-            return ops[j]["lat"] + (0.0 if ops[i]["q"] == "pe" else HOP_SAME)
-        return ops[j]["lat"] + HOP_OTHER
+            return float(ops[j]["lat"][m] + (0.0 if ops[i]["q"] == "pe" else HOP_SAME[m]))
+        return float(ops[j]["lat"][m] + HOP_OTHER[m])
 
-    def run(pre, post, prio, back):
-        left = [len(d) for d in pre]
-        ready = [i for i in range(n) if left[i] == 0]
-        est = [ops[i]["lat"] if back else 0.0 for i in range(n)]
-        fin = [0.0] * n
-        taken = {}
-        for _ in range(n):
-            i = max(ready, key=lambda x: prio[x])
-            ready.remove(i)
-            o, s = ops[i], est[i]
-            moved = True
-            while moved:
-                moved = False
-                for r in [o["q"]] + list(o["banks"]):
-                    spans = taken.get(r, [])
-                    lo, hi = 0, len(spans)
-                    while lo < hi:
-                        mid = (lo + hi) // 2
-                        if spans[mid][0] < s - LONGEST:
-                            lo = mid + 1
-                        else:
-                            hi = mid
-                    for a, b, q in spans[lo:]:
-                        gap = 0.0 if r == o["q"] else HOP_OTHER
-                        if a >= s + o["cost"] + gap:
-                            break
-                        if b + gap > s and (r == o["q"] or q != o["q"]):
-                            s, moved = b + gap, True
-            fin[i] = s + o["cost"]
-            for r in [o["q"]] + list(o["banks"]):
-                spans = taken.setdefault(r, [])
-                k = len(spans)
-                while k and spans[k - 1][0] > s:
-                    k -= 1
-                spans.insert(k, (s, fin[i], o["q"]))
-            for k in post[i]:
-                est[k] = max(est[k], fin[i] + (hop(k, i) if back else hop(i, k)))
-                left[k] -= 1
-                if left[k] == 0:
-                    ready.append(k)
-        return max(fin[i] + (0.0 if back else ops[i]["lat"]) for i in range(n)), fin
-
-    def run_free(pre, post, prio, back):
-        left = [len(d) for d in pre]
-        ready = {}
-        for i in range(n):
-            if left[i] == 0:
-                ready.setdefault(ops[i]["q"], []).append(i)
-        est = [ops[i]["lat"] if back else 0.0 for i in range(n)]
-        fin = [0.0] * n
-        free, bank = {}, {}
-        for _ in range(n):
-            best = None
-            for q, rs in ready.items():
-                if not rs:
-                    continue
-                cand = []
-                for i in rs:
-                    s = max(est[i], free.get(q, 0.0))
-                    for b in ops[i]["banks"]:
-                        for q2, j in bank.get(b, {}).items():
-                            if q2 != q:
-                                s = max(s, fin[j] + HOP_OTHER)
-                    cand.append((s, i))
-                s0 = min(cand)[0]
-                if best is None or s0 < best[0]:
-                    best = (s0, cand)
-            s, i = max((c for c in best[1] if c[0] <= best[0] + SLACK), key=lambda c: prio[c[1]])
-            o = ops[i]
-            for b in o["banks"]:
-                bank.setdefault(b, {})[o["q"]] = i
-            free[o["q"]] = fin[i] = s + o["cost"]
-            ready[o["q"]].remove(i)
-            for k in post[i]:
-                est[k] = max(est[k], fin[i] + (hop(k, i) if back else hop(i, k)))
-                left[k] -= 1
-                if left[k] == 0:
-                    ready.setdefault(ops[k]["q"], []).append(k)
-        return max(fin[i] + (0.0 if back else ops[i]["lat"]) for i in range(n)), fin
-
-    base = [0.0] * n
-    for i in range(n - 1, -1, -1):
-        base[i] = ops[i]["cost"] + max([base[k] + hop(i, k) for k in succ[i]] or [ops[i]["lat"]])
+    names = {}
+    number = lambda x: names.setdefault(x, len(names))
+    facts = [[(number(o["q"]), float(o["cost"][m]), [number(b) for b in sorted(o["banks"])], float(o["lat"][m])) for o in ops]
+             for m in sets]
     kinds = {}
     for i, o in enumerate(ops):
         kinds.setdefault(o["kind"], []).append(i)
-    kinds = [v for v in kinds.values() if len(v) > 2]
-    first = [-1e6 * (o["level"] + o["class"]) - i if o["level"] >= 0 else base[i] for i, o in enumerate(ops)]
-    best = min((f(pre0, succ, first, False) for f in (run, run_free)), key=lambda r: r[0])
-    rng = np.random.RandomState(1)
-    same = {i: v for v in kinds for i in v}
+    place = {i: (v, x) for v in kinds.values() for x, i in enumerate(v)}
+    above, lag = [0] * n, [[] for m in sets]
+    for i in range(n):
+        for j in pre[i]:
+            above[i] |= above[j]
+        for m in sets:
+            lag[m].append([(j, hop(j, i, m)) for j in sorted(pre[i]) if not above[i] >> j & 1])
+        for j in pre[i]:
+            above[i] |= 1 << j
+    base = [0.0] * n
+    for i in range(n - 1, -1, -1):
+        base[i] = facts[0][i][1] + max([base[k] + hop(i, k, 0) for k in succ[i]] or [facts[0][i][3]])
 
-    def longest(fin):
-        before, last = {}, {}
-        for i in sorted(range(n), key=lambda x: fin[x]):
-            before[i] = last.get(ops[i]["q"])
-            last[ops[i]["q"]] = i
-        i, res = max(range(n), key=lambda x: fin[x] + ops[x]["lat"]), []
-        while True:
-            t, j = max([(fin[j] + hop(j, i), j) for j in pre0[i]] or [(0.0, None)])
-            b = before[i]
-            if b is not None and fin[b] > t:
-                res += [(same[x], s) for x, s in ((i, 1.0), (b, -1.0)) if x in same]
-                j = b
-            if j is None:
-                return res
-            i = j
+    named = {(o["q"], o["level"], "%s%d%s" % (o["kind"][2], o["kind"][3], ("", "'", "*", "!")[o["kind"][0][1]])): i
+             for i, o in enumerate(ops) if isinstance(o["kind"], tuple)}
+    line = {q: [] for q in ("dve", "act", "pe")}
+    for level in range(-1, TV * LV + 1):
+        for q in line:
+            for x in ORDER[level % 2][q].split():
+                key = (q, level + {"-": -1, "+": 1}.get(x[0], 0), x.lstrip("+-"))
+                if key in named:
+                    line[q].append(named.pop(key))
+    assert len([k for k in named if k[0] in line]) <= 1, [k for k in named if k[0] in line]
+    listed = set(i for q in line for i in line[q])
+    left = [len(d) for d in pre]
+    ready = [i for i in range(n) if left[i] == 0]
+    fin, last, order, head = [0.0] * n, [None] * len(names), [], {q: 0 for q in line}
+    while len(order) < n:
+        best = None
+        for i in ready:
+            q, cost, banks, lat = facts[0][i]
+            if i in listed and line[ops[i]["q"]][head[ops[i]["q"]]] != i:
+                continue
+            s = max([fin[j] + h for j, h in lag[0][i]] + [0.0 if last[q] is None else fin[last[q]]]
+                    + [fin[last[b]] + HOP_OTHER[0] for b in banks if last[b] is not None and facts[0][last[b]][0] != q])
+            if best is None or (s, -base[i]) < best[0]:
+                best = ((s, -base[i]), i)
+        assert best is not None, [(ops[line[q][head[q]]]["kind"], [ops[j]["kind"] for j in pre[line[q][head[q]]] if j not in order])
+                                  for q in line]
+        i = best[1]
+        fin[i], last[facts[0][i][0]] = best[0][0] + facts[0][i][1], i
+        for b in facts[0][i][2]:
+            last[b] = i
+        if i in listed:
+            head[ops[i]["q"]] += 1
+        ready.remove(i)
+        order.append(i)
+        for k in succ[i]:
+            left[k] -= 1
+            if left[k] == 0:
+                ready.append(k)
+    mark = max(i for i, o in enumerate(ops) if o["level"] == 3 and o["q"] == "dve" and o["kind"][2] == "XT")
 
-    cur, keep, path = best, best, longest(best[1])
-    for it in range(TRIES):
-        f = run_free if it % MIX else run
-        if it % ROUNDS < 2:
-            prio = f(succ, pre0, best[1], True)[1]
-        else:
-            prio = [ops[i]["cost"] - best[1][i] for i in range(n)]
-            for _ in range(1 + it % 2):
-                d = float(rng.randn()) * NOISE
-                if rng.rand() < 0.3 or not path:
-                    k = kinds[int(rng.randint(len(kinds)))]
-                else:
-                    k, sign = path[int(rng.randint(len(path)))]
-                    d = abs(d) * sign
-                for i in k:
-                    prio[i] += d
-        res = f(pre0, succ, prio, False)
-        if res[0] <= cur[0] + WARM * (1.0 - it / TRIES) * rng.rand():
-            cur = res
-            path = longest(res[1])
-            if res[0] < keep[0]:
-                keep = res
-        best = cur
-    best = keep
-    order = sorted(range(n), key=lambda i: (best[1][i] - ops[i]["cost"], i))
-    lag = [[(j, hop(j, i)) for j in pre0[i]] for i in range(n)]
-    facts = [(o["q"], o["cost"], list(o["banks"]), o["lat"]) for o in ops]
-    place = {i: (v, x) for v in kinds for x, i in enumerate(v)}
-
-    def play(order):
-        fin, why, free, bank = [0.0] * n, [None] * n, {}, {}
-        end, last = 0.0, None
+    def play(order, m, short):
+        fin, why, last = [0.0] * n, [None] * n, [None] * len(names)
+        end, x, fact, lags, other = 0.0, None, facts[m], lag[m], float(HOP_OTHER[m])
         for i in order:
-            q, cost, banks, lat = facts[i]
+            q, cost, banks, lat = fact[i]
             s, w = 0.0, None
-            for j, h in lag[i]:
+            for j, h in lags[i]:
                 if fin[j] + h > s:
                     s, w = fin[j] + h, (j, False)
-            j = free.get(q)
+            j = last[q]
             if j is not None and fin[j] > s:
                 s, w = fin[j], (j, True)
             for b in banks:
-                j = bank.get(b)
-                if j is not None and facts[j][0] != q and fin[j] + HOP_OTHER > s:
-                    s, w = fin[j] + HOP_OTHER, (j, True)
-                bank[b] = i
-            fin[i], why[i], free[q] = s + cost, w, i
-            if fin[i] + lat > end:
-                end, last = fin[i] + lat, i
+                j = last[b]
+                if j is not None and fact[j][0] != q and fin[j] + other > s:
+                    s, w = fin[j] + other, (j, True)
+                last[b] = i
+            fin[i], why[i], last[q] = s + cost, w, i
+            if s + cost + lat > end:
+                end, x = s + cost + lat, i
         pairs = []
-        while why[last]:
-            if why[last][1]:
-                pairs.append((why[last][0], last))
-            last = why[last][0]
-        return end, fin, pairs
+        if short:
+            end, x = fin[mark], mark
+        while why[x]:
+            if why[x][1]:
+                pairs.append((why[x][0], x))
+            x = why[x][0]
+        return end, pairs, fin
+
+    def judge(order, short, unit, limit):
+        total, pairs = 0.0, []
+        part = order[:order.index(mark) + 1] if short else order
+        for m in sets:
+            res = play(part, m, short)
+            total += res[0] / unit[m]
+            pairs += res[1]
+            if total > limit[m]:
+                return None
+        return total, pairs, order
 
     def swap(order, b, i, ahead):
         x, y = order.index(b), order.index(i)
@@ -741,79 +642,58 @@ def plan(ops):
         mid = order[x:y + 1]
         move = {i if ahead else b}
         for k in (reversed(mid) if ahead else mid):
-            if k not in move and any(j in move for j in (succ[k] if ahead else pre0[k])):
+            if k not in move and any(j in move for j in (succ[k] if ahead else pre[k])):
                 move.add(k)
         if (b if ahead else i) in move:
             return order
         one, other = [k for k in mid if k in move], [k for k in mid if k not in move]
         return order[:x] + (one + other if ahead else other + one) + order[y + 1:]
 
-    cur = keep = play(order) + (order,)
-    for it in range(SWAPS):
-        b, i = cur[2][int(rng.randint(len(cur[2])))]
-        ahead, new = rng.rand() < 0.5, cur[3]
-        if b in place and i in place:
-            (vb, xb), (vi, xi) = place[b], place[i]
-            for x in range(len(vi)):
-                if 0 <= x + xb - xi < len(vb):
-                    new = swap(new, vb[x + xb - xi], vi[x], ahead)
-        else:
-            new = swap(new, b, i, ahead)
-        if new is cur[3]:
-            continue
-        res = play(new)
-        if res[0] <= cur[0] + HEAT * (1.0 - it / SWAPS) * rng.rand() ** 2:
-            cur = res + (new,)
-            if cur[0] < keep[0]:
-                keep = cur
-    best, order = keep, keep[3]
-    busy, bank = {}, {}
-    for i in range(n):
-        ops[i]["t0"] = best[1][i] - ops[i]["cost"]
-        busy[ops[i]["q"]] = busy.get(ops[i]["q"], 0.0) + ops[i]["cost"]
+    rng = np.random.RandomState(SEED)
+    first = [play(order, m, False)[0] for m in sets]
+    for short, swaps, heat, alike in ((True, SWAPS, HEAT, 1.0), (False, SWAPS // 8, HEAT / 4, 0.3)):
+        part = order[:order.index(mark) + 1] if short else order
+        unit = [play(part, m, short)[0] for m in sets]
+        cur = keep = judge(order, short, unit, [1e9] * len(FIG))
+        for it in range(swaps):
+            b, i = cur[1][int(rng.randint(len(cur[1])))]
+            ahead, new = rng.rand() < 0.5, cur[2]
+            if rng.rand() < alike:
+                (vb, xb), (vi, xi) = place[b], place[i]
+                for x in range(len(vi)):
+                    if 0 <= x + xb - xi < len(vb):
+                        new = swap(new, vb[x + xb - xi], vi[x], ahead)
+            else:
+                new = swap(new, b, i, ahead)
+            if new is cur[2]:
+                continue
+            top = cur[0] + len(FIG) * heat * (1.0 - it / swaps) * rng.rand() ** 2
+            res = judge(new, short, unit, [top * (m + 1) / len(FIG) + 0.02 * (m + 1 < len(FIG)) for m in sets])
+            if res is not None:
+                cur = res
+                if cur[0] < keep[0]:
+                    keep = cur
+        order = keep[2]
+    ends, fin, bank = [play(order, m, False)[0] for m in sets], play(order, 0, False)[2], {}
     for i in order:
+        ops[i]["t0"] = fin[i] - facts[0][i][1]
         for b in ops[i]["banks"]:
             deps[i] |= set(j for q, j in bank.get(b, {}).items() if q != ops[i]["q"])
             bank.setdefault(b, {})[ops[i]["q"]] = i
-    return order, deps, best[0], busy
+    return order, deps, ends, first
 
 
-SLACK, MIX, WARM, SWAPS, HEAT = 20.0, 2, 800.0, 16000, 500.0
-LEAN = (0.0, 30.0, 100.0, 1000.0)
 PLAN = {}
-
-
-def planned(T, topo, core):
-    ops = build(T, T.cores[(T.rank_of(core) + 1) % len(T.cores)], topo, core)
-    if "p" not in PLAN:
-        PLAN["p"] = plan(ops)
-    return ops, PLAN["p"][0], PLAN["p"][1]
-
-
-def hand_back(g, core, T, topo, owner):
-    ops, order, deps = planned(T, topo, owner)
-    rid, pid = topo.addr(owner)[:2]
-    come, gone = len(topo.engines(owner, core)), len(topo.engines(core, owner))
-    seen = {}
-    for j in [ops[i]["job"] for i in order if "job" in ops[i]]:
-        if helper_of(topo, T.cores, owner, j) == core:
-            seen[j] = seen.get(j, 0) + come
-            g.wait_ge(T.sem["fa%d" % j], seen[j])
-            c, o, s0, m = JOBS[j]
-            b, a = TILE[o + str(c)][:2]
-            x = T[b][:, a + 16 * s0:a + 16 * (s0 + m)]
-            g.remote_dma(x, x, T.sem["fb%d" % j], T.sem["back"], pid, rid, topo.mask(core, owner))
-    g.wait_ge(T.sem["back"], gone * sum(seen.values()) // come)
 
 
 def rank_program(g, core, T, topo):
     rank = T.rank_of(core)
     if rank is None:
-        for owner in T.cores:
-            if any(helper_of(topo, T.cores, owner, j) == core for j in range(len(JOBS))):
-                hand_back(g, core, T, topo, owner)
         return
-    ops, order, deps = planned(T, topo, core)
+    ops = build(T, T.cores[(rank + 1) % len(T.cores)], topo, core)
+    if "p" not in PLAN:
+        PLAN["p"] = plan(ops)
+    order, deps = PLAN["p"][:2]
     queues = {"pe": g.tensor, "dve": g.vector, "act": g.scalar, "pool": g, "sync": g.sync}
     total, mark, seen = {}, {}, {}
     for i in order:

import numpy as np
from concourse.mybir import AluOpType, ActivationFunctionType

V, L, TV, LV = 2048, 256, 4, 2
CUTS = {1: {"Q": "16v 48s 64s", "R": "16v 48v 32v 32s", "P": "16v 48v 64v", "MQ": "64v 64v", "MR_": "64v 32s 32t",
            "MP": "32t 32t 32t 32q"},
        0: {"Q": "64s 64s", "R": "64v 32v 32v", "P": "64v 32v 32v", "MQ": "128v", "MR_": "64s 32s 32s",
            "MP": "32t 32t 32t 32t"}}
ORDER = {
    0: {"dve": "-YM1! -THA1! Q1' R1' R2' MR_1' R1 R3' P2' P1' P3' -FB2! MQ1' MQ2' P1 P3 P2 R2 MQ1 R3 NC1' -MS1' HI1' -MS1 F1' FM1' "
               "E1' K1' PR1' X1' K1 NC1 ZM1' HI1 F1 FM1 E1 PR2' MN1' PR1 XT1* X1 OF1' ZM1 PR3' PR3 LZ1 OU1' XZ1 PR2 XT2* MN1 OF1 "
               "XT3* OU1 XT4* XT5*",
        "act": "Q1' Q1 Q2' -N1! KU3' R1' KU3 -MA1' MR_1' MR_2' MP1' MP2' Q2 MP3' MP4' MR_1 MP1 MP2 SB1' DI1' MR_2 MP3 -MA1 SA1' "
               "MR_3 MP4 NVA1! SB1 DI1 NVA2! LZ1' DF1' OZ1' XZ1' SA1 HH1' DF1 OZ1 LU1' HH1 +KU1' CS1' CS1 LU1",
        "pe": "-YD1! -M1 DD1' R1' DD1 R2' D1 U1' D1' U2' U3' MR_1' P2' U4' P1' U5' MQ1' MQ2' U1 DF1' U2 MP1' P2 DE1' U3 P1 MQ1 MQ2 "
              "U4 MR_1 DF1 OH2' MP1 DE1 ZB1' DIFF1' BOM1' DIFF2' ZL1' NVP1* OH2 DIFF1 OH1' HS1' ZB1 BOM1 OH1 ZL1 DIFF2 LS1' LS2' "
              "HS1 LS1 LS2 M1'"},
    1: {"dve": "Q1' P1' R1' R2' P2' P3' R3' MQ1' MQ2' P1 MR_1' R1 P2 P3 R2 MQ1 R3 NC1' -MS1' HI1' -MS1 F1' X1' FM1' E1' K1' PR1' K1 "
               "CL1' NC1 HI1 ZM1' F1 FM1 CL1 E1 MN1' PR1 OF1' OU1' X1 ZM1 AB1! XT1* LZ1 XZ1 FB1! XT2* SS1! MN1 OF1 XT3* OU1 XT4* XT5*",
        "act": "Q1' Q2' KU1 R1' Q1 MP1' MP2' Q2 MR_2' -MA1' MR_1' MP3' MP4' MR_1 MP1 -MA1 SB1' SA1' NV1' MR_2 DI1' MP2 MP3 MR_3 MP4 "
               "NV1 SB1 DI1 SA1 LZ1' OZ1' DF1' XZ1' HH1' DF1 OZ1 AX1! HH1 +KU2 +KU1' +KU1 +KU2'",
        "pe": "-M1 DD1' DD1 R2' U1' R1' U2' P2' U3' P1' U4' MQ1' MQ2' U5' MR_1' D1' U1 MP1' DF1' DE1' P2 P1 U2 U3 MQ2 MQ1 D1 U4 "
              "MR_1 OH1' DF1 OH2' MP1 DE1 ZB1' DIFF1' BOM1' OH1 NVP1* ZL1' DIFF2' NVP2* OH2 LS1! LS2! ZB1 HS1' DIFF1 BOM1 ZL1 VV2! "
              "DIFF2 VV1! HS1 ABP1! M1'"}}
STEPS, NV = {}, {}
for _c in CUTS:
    STEPS[_c] = []
    for _j, (_k, _v) in enumerate(CUTS[_c].items()):
        _s = 0
        for _x in _v.split():
            STEPS[_c].append((_s + int(_x[:-1]), _j, _k, _s, _x[-1]))
            _s += int(_x[:-1])
    _up = lambda e, k: min(x[0] for x in STEPS[_c] if x[2] == k and x[0] >= e)
    STEPS[_c] = sorted(STEPS[_c], key=lambda x: (x[3] if x[2] == "Q" else x[0] - 1 if x[2] in "PR" else
                                                 max(_up(x[0], "P"), _up(x[0], "R")) - 0.5, x[1], x[0]))
    NV[_c] = sum(x[0] - x[3] for x in STEPS[_c] if x[2] == "MR_" and x[4] == "v")
ON_SCALAR = ("KU", "LU", "DI", "MA", "LZ1", "XZ1")
PE_RUN = 8
BLK = 64
XO = 16 * BLK
ROWS = [(8 * u * (u + 1) * 128 // BLK, 16 * (u + 1)) for u in range(BLK // 16)]
WIDE = ROWS[-1][0] + 128

BF, F16, F32, I32, U16 = "bfloat16", "float16", "float32", "int32", "uint16"
WIDTH = {BF: 2, F16: 2, U16: 2, F32: 4, I32: 4}
ARENA = {BF: "SB", F16: "SH", F32: "SF", I32: "SI", U16: "SU"}
TILE, USED = {}, {}


def _sb(dtype, tags, **kw):
    for tag in tags:
        for k, n in kw.items():
            a = USED.get(dtype, 0)
            TILE[k + tag] = (ARENA[dtype], a, a + n)
            USED[dtype] = a + (n + 15) // 16 * 16


_sb(BF, [""], ONE=512, TMP=128, IB=128, IBM=128, IB2K=128, IB8K=128, BO=128, SELT=2048, SEG=WIDE, RST=128, CM=BLK, GI=16,
    BASE=64, ZB=144, XT=XO + 4096, Y=1024, N=1024, YM=256, AB=16, AX=16, NVA=768)
_sb(F16, [""], IH=128, IHM=128, J2K=256, J4K=256, I7=128, C_=128, ONH=128, ONK=128, BOH=128, BOM=128, WS=96, ZH=144, MR=128,
    IND=WIDE + 16, MK=WIDE, DG=2048, BOX=256, TH2=256, CB=384, CL=256, THA=256)
_sb(F32, [""], kc=1, pd=1, TH=1, THN=1, fu=1, fw=1, fb=1, fe=1, T1=128, T2=WIDE + 16, T3=WIDE, T4=16, T5=16, DV=16, FB=160,
    CS=16, AS=1, MS=2048)
_sb(I32, [""], thi=1, pi=1, pj=1, pk=1, pu=1, pb=1, eqi=8, CT=3584, LI=48)
_sb(U16, [""], EQL=8, ENDS=2, SS=112, LA=128)
_sb(F16, "01", P=2048, Q=2048, R=2048, MQ=2048, MR_=2048, MP=2048)
_sb(BF, "01", NV=384)
TWO = ["00", "01", "10", "11"]
_sb(BF, TWO, DF=WIDE, MN=WIDE, XZ=128, HH=128)
_sb(F16, TWO, K=512, PR=512, SA=128, SB=128, NC=128, DI=128, HI=128, X=128, E=144, ZM=128, OF=16, OZ=16, F=128)
_sb(F32, TWO, FM=8, MA=128)
_sb(U16, TWO, KU=384, LU=24, LZ=8, OU=8)
SCRATCH = {ARENA[d]: ("sbuf", [128, n], d) for d, n in USED.items()}
PLACE = {"D": ("A", 0), "ZL": ("A", 256), "ZB": ("A", 384), "ABP": ("A", 0), "YD": ("A", 256),
         "DIFF": ("B", 0), "HS": ("B", 384), "M": ("B", 0),
         "OH": ("C", 0), "DD": ("C", 256), "LS": ("C", 256), "VV": ("C", 304), "U": ("E", 0), "NVP": ("E", 0)}
PSUM = [b + s for b in "ABCE" for s in "01"]
for _k in PSUM:
    SCRATCH[_k] = ("psum", [128, 512], F32)

SEMAPHORES = (["pe", "dve", "act", "pool", "outs", "sent", "lc0", "lc1", "lli", "lx0", "lx1", "lth", "ly"]
              + ["r%s%d" % (w, t) for w in "acy" for t in range(1, TV)])
A = AluOpType
ACT = ActivationFunctionType
FIG = np.array([(0.83, 0.46, 1.56, 3.8, 120.0, 200.0, 1.0), (0.87, 0.50, 1.15, 2.5, 120.0, 200.0, 1.2),
                (1.12, 0.62, 1.9, 5.0, 120.0, 200.0, 1.2)])
CYC, PCYC, GAT, SCA, HOP_SAME, HOP_OTHER, SLOW = FIG.T
CALL = 900.0
SWAPS, HEAT, SEED = 20000, 0.003, 1


def build(T, nxt, topo, core):
    ops, now = [], {"part": None, "level": -1, "turn": 0}

    def tl(name, a=None, b=None, step=None, rows=None):
        buf, o, e = TILE[name]
        a, b = (0, e - o) if a is None else (a, b)
        return (buf, o + a, o + b, step or 1) + (rows or (0, 128))

    def ap(s):
        return T[s[0]][s[4]:s[5], s[1]:s[2]:s[3]] if s[3] > 1 else T[s[0]][s[4]:s[5], s[1]:s[2]]

    def sub(s, a, b, step=1, rows=None):
        return (s[0], s[1] + a, s[1] + b, step) + (rows or s[4:])

    def cnt(s):
        return len(range(s[1], s[2], s[3]))

    def two(*ss):
        return all(WIDTH[SCRATCH[s[0]][2]] == 2 for s in ss)

    def add(q, cost, rd, wr, fn, sem="", inc=1, lat=0.0, after=None, soft=None):
        ops.append({"q": q, "cost": cost + 0 * CYC, "rd": rd, "wr": wr, "fn": fn, "sem": q if sem == "" else sem, "inc": inc,
                    "lat": lat * SLOW, "after": after, "soft": soft, "own": sem != "", "level": now["level"], "kind": len(ops)})
        if now["part"] is not None:
            x = (wr + rd)[0]
            key = (q, now["tag"] if x[0] in PSUM else
                   [k for k, v in TILE.items() if v[0] == x[0] and v[1] <= x[1] < v[2]][0].rstrip("01"))
            now["seen"][key] = now["seen"].get(key, 0) + 1
            ops[-1]["kind"] = (now["part"],) + key + (now["seen"][key],)
        return len(ops) - 1

    def part(name):
        now["part"], now["seen"] = name, {}

    def src(s, off):
        return ap(s) if off is None else ap(s).indirect(ap(off))

    def vcost(n, f, off=None):
        return 50 + n * GAT * CYC if off is not None else 25 + max(64, n * f) * CYC

    def sc(x):
        return ap(x) if isinstance(x, tuple) else x

    def tups(*xs):
        return [x for x in xs if isinstance(x, tuple)]

    def copy(o, i, off=None):
        add("dve", vcost(cnt(o), 0.5 if two(o, i) else 1, off), tups(i, off), [o],
            lambda q: [q.tensor_copy(ap(o), src(i, off))])

    def ts(o, i, s1, op0, s2=None, op1=None, off=None):
        def fn(q):
            if op1 is None:
                return [q.tensor_scalar(ap(o), src(i, off), sc(s1), None, op0)]
            return [q.tensor_scalar(ap(o), src(i, off), sc(s1), sc(s2), op0, op1)]
        add("dve", vcost(cnt(o), 0.5 if two(o, i) else 1, off), tups(i, off, s1, s2), [o], fn)

    def tt(o, a, b, op, off=None):
        f = (1 if a[0] in PSUM or b[0] in PSUM else 2) * (0.5 if two(o, a, b) else 1)
        add("dve", vcost(cnt(o), f, off), tups(a, b, off), [o],
            lambda q: [q.tensor_tensor(ap(o), src(a, off), ap(b), op)])

    def scatter_add(win, off, a, b):
        add("dve", 50 + cnt(a) * SCA * CYC, [off, a, b], [win],
            lambda q: [q.tensor_tensor(ap(win).indirect(ap(off)), ap(a), ap(b), A.add)])

    def scan(o, d0, d1, op0, op1):
        add("dve", vcost(cnt(o), 0.5 if two(o, d0, d1) else 1), [d0, d1], [o],
            lambda q: [q.tensor_tensor_scan(ap(o), ap(d0), ap(d1), 0.0, op0, op1)])

    def fill(o, v):
        add("dve", vcost(cnt(o), 0.5 if two(o) else 1), [], [o], lambda q: [q.memset(ap(o), v)])

    def act(o, i, func, bias=None, scale=None, off=None, accum=None):
        def fn(q):
            kw = {}
            if bias is not None:
                kw["bias"] = sc(bias)
            if scale is not None:
                kw["scale"] = sc(scale)
            if accum is not None:
                kw["accum_out"] = ap(accum)
            return [q.activation(ap(o), src(i, off), func, **kw)]
        add("act", 65 + cnt(o) * (GAT if off is not None else 1) * CYC, tups(i, off, bias, scale), tups(o, accum), fn)

    def plus(name, o, i, x=0.0, off=None):
        if name in ON_SCALAR:
            act(o, i, ACT.Identity if x else ACT.Copy, bias=x or None, off=off)
        elif x:
            ts(o, i, x, A.add, off=off)
        else:
            copy(o, i, off=off)

    def mm(o, terms, start=True, stop=True, each=False):
        def fn(q):
            for j, x in enumerate(terms):
                ins = q.matmul(ap(x[2] if len(x) == 3 else o), ap(x[0]), ap(x[1]), each or (start and j == 0),
                               each or (stop and j == len(terms) - 1))
            return [ins]
        cost = 30 + sum(max(min(64, cnt(x[0])), cnt(x[1])) * PCYC + 4 for x in terms)
        rd = []
        for x in (x[:3] + (1, 0, 128) for t in terms for x in t[:2]):
            if x not in rd:
                rd.append(x)
        now["tag"] = now.get(o[:2]) if start or stop else None
        if not (start or stop):
            add("pe", cost, rd + [o], [], fn)
        else:
            add("pe", cost, rd, [o if start and stop else (o[0], 0, 512, 1, 0, 128)], fn)

    def pool(o, rd, fn):
        add("pool", 170 + 2 * cnt(o) * CYC, rd, [o], fn)

    def iota(o, pattern, base, cm):
        if SCRATCH[o[0]][2] == I32:
            pool(o, [], lambda q: [q.iota(ap(o), pattern, base, cm)])
        else:
            pool(o, [], lambda q: [q.iota(ap(o), pattern, base, cm, allow_small_or_imprecise_dtypes=True)])

    def select(o, i, pattern, op, base, cm):
        pool(o, [i], lambda q: [q.affine_select(ap(o), ap(i), pattern, op, 0.0, base, cm)])

    last = {}

    def load(q, sem, pairs, lat):
        last[q] = add(q, 60 * len(pairs), [], [o for o, i in pairs], lambda e: [e.dma_start(ap(o), i) for o, i in pairs],
                      sem=sem, inc=16 * len(pairs), lat=lat, soft=last.get(q))

    def store(o, i, lat, q="sync"):
        add(q, 60, [i], [], lambda e: [e.dma_start(o, ap(i))], sem="outs", inc=16, lat=lat)

    eng = topo.engines(core, nxt)
    rid, pid = topo.addr(nxt)[:2]

    def send(dst, s, sem, lat):
        def fn(q):
            q.remote_dma(ap(dst), ap(s), T.sem[sem], T.sem["sent"], pid, rid, topo.mask(core, nxt))
            return []
        k = add("pool", CALL, [s], [], fn, sem="sent", inc=len(eng), lat=lat)
        add("none" + sem, 0, [], [dst], None, sem=sem, inc=len(eng), after=k)

    load("sync", "lc0", [(tl("CT", 0, 1024), T.ch[:, 0:1024])], 4000)
    load("act", "lc1", [(tl("CT", 1024, 2048), T.ch[:, 1024:2048])], 4000)
    load("sync", "lli", [(tl("LI", 16 * a, 16 * a + 16), x[:]) for a, x in enumerate((T.sb, T.ia, T.ic))], 3000)
    load("act", "lx0", [(tl("XT", XO, XO + 1024), T.x[:, 0:1024])], 5000)
    load("sync", "lx1", [(tl("XT", XO + 1024, XO + V), T.x[:, 1024:2048])], 5000)
    load("sync", "lth", [(tl("thi"), T.th[:])], 5000)
    load("sync", "ly", [(tl("Y", 0, 256), T.y[:])], 5000)

    LO, HI = (0, 64), (64, 128)
    one = lambda n, rows=None: tl("ONE", 0, n, rows=rows)
    nb = 128 // BLK
    fill(tl("ONE"), 1.0)
    select(tl("IB"), one(128), [[-1, 128]], A.is_equal, 0, 1)
    select(tl("TMP"), one(128), [[-16, 8], [0, 16]], A.is_ge, 0, 1)
    select(tl("BO"), tl("TMP"), [[16, 8], [0, 16]], A.is_ge, 15, -1)
    iota(tl("pi"), [[0, 1]], 0, 1)
    iota(tl("T1"), [[0, 8], [1, 16]], 0, 0)
    iota(tl("eqi"), [[1, 8]], 0, 0)
    iota(tl("DV", 0, 8), [[512, 4], [128, 2]], 256, 1)
    iota(tl("DV", 8, 16), [[-512, 4], [-128, 2]], -256, -1)
    for u, (a, w) in enumerate(ROWS):
        iota(tl("T2", a, a + w * nb), [[BLK // 16, nb], [0, w]], u, 0)
        iota(tl("T3", a, a + w * nb), [[0, nb], [1, w]], -16 * u, 0)
    iota(tl("T2", WIDE, WIDE + 16), [[1, 16]], 0, 0)
    iota(tl("T4"), [[16, 16]], 0, 0)
    iota(tl("T5", 0, 8), [[16, BLK // 16], [0, nb]], 129, 0)
    for r in range(0, 16, 2):
        select(tl("SELT", 128 * r, 128 * r + 256), one(256), [[-1, 2], [-16, 8], [0, 16]], A.is_equal, -r, 1)
    for name, f in (("IBM", -1.0), ("IB2K", 2048.0), ("IB8K", -8192.0), ("IH", 1.0), ("IHM", -1.0), ("I7", -7.5)):
        ts(tl(name), tl("IB"), f, A.mult)
    for j in range(2):
        ts(tl("J2K", 128 * j, 128 * j + 128), tl("IB"), 2048.0 * (1 - 2 * j), A.mult)
        ts(tl("J4K", 128 * j, 128 * j + 128), tl("IB"), 4096.0 * (1 - 2 * j), A.mult)
    copy(tl("EQL"), tl("eqi"))
    ts(tl("C_"), tl("T1"), 0.0, A.is_equal)
    copy(tl("ONH"), one(128))
    ts(tl("ONK"), one(128), 1.0 / 1024, A.mult)
    copy(tl("BOH"), tl("BO"))
    ts(tl("BOM"), tl("BO"), -1.0, A.mult)
    e = 1.0 / 2048
    for j in range(2):
        ts(tl("BOX", 128 * j, 128 * j + 128), tl("BO"), -e if j else -1.0, A.mult)
    weight = {}
    for j, f in enumerate((1.0, -1.0, e, 4 * e, -2 * e)):
        weight[f] = tl("WS", 16 * j, 16 * j + 8)
        ts(weight[f], tl("BO", 0, 128, 16), f, A.mult)
    fill(tl("ZB"), 0.0)
    copy(tl("ZB", 15, 143, 16), tl("BO", 0, 128, 16))
    copy(tl("ZH"), tl("ZB"))
    sel = lambda r: tl("ZH", 15 - r, 143 - r)
    kc = tl("kc")
    ts(tl("pj"), tl("pi"), 15, A.bitwise_and)
    copy(kc, tl("pj"))
    ts(tl("pk"), tl("pi"), 4, A.arith_shift_right)
    copy(tl("pd"), tl("pk"))
    ts(tl("MR"), tl("T1"), kc, A.is_equal)
    ts(tl("IND"), tl("T2"), tl("pd"), A.is_equal)
    ts(tl("MK"), tl("T3"), kc, A.is_ge, 8192.0, A.mult)
    fill(tl("SEG"), 0.0)
    for u, (a, w) in enumerate(ROWS):
        fill(tl("SEG", a, a + w * nb, w), 1.0e12)
        ts(tl("SEG", a + w - 1, a + w * nb, w), tl("T5", nb * u, nb * u + nb), kc, A.add, -16.0, A.mult)
    ts(tl("pu"), tl("pi"), BLK // 16 - 1, A.bitwise_and)
    ts(tl("pb"), tl("pi"), 7, A.bitwise_and, BLK // 32, A.arith_shift_right)
    ts(tl("fu"), tl("pu"), 1.0, A.add)
    ts(tl("fw"), tl("pu"), nb / 2.0, A.mult, 1.0, A.add)
    tt(tl("fb"), tl("pb"), tl("fw"), A.add)
    ts(tl("fe"), tl("fb"), tl("fu"), A.mult, 16.0, A.mult)
    ts(tl("ENDS", 0, 1), tl("fe"), -1.0, A.add)
    fill(tl("RST"), 0.0)
    fill(tl("RST", 0, 128, 16), -1.0e4)
    fill(tl("CM"), -160.0)
    ts(tl("GI"), tl("T4"), kc, A.add)
    copy(tl("TH"), tl("thi"))
    ts(tl("THN"), tl("TH"), 0.5, A.add, -1.0, A.mult)
    ts(tl("TH2", 0, 128), tl("IH"), tl("THN"), A.mult)
    ts(tl("TH2", 128, 256), tl("IH"), tl("THN"), A.mult, e, A.mult)
    ts(tl("CB", 0, 128), one(128), -8.0, A.mult)
    ts(tl("CB", 128, 256), one(128), 0.0, A.mult)
    ts(tl("CB", 256, 384, rows=LO), one(128, LO), 2056.0 / 64, A.mult)
    ts(tl("CB", 256, 384, rows=HI), one(128, HI), -17.0 / 4096, A.mult)
    for t in range(TV):
        fill(tl("BASE", 16 * t, 16 * t + 16), 1.0 + t / 4)
    for j in range(16):
        act(tl("DG", 128 * j, 128 * j + 128), tl("IH"), ACT.Identity, scale=tl("DV", j, j + 1))
    for x in TWO:
        copy(tl("E" + x, 0, 16), one(16))
        if x[1] == "0":
            copy(tl("K" + x, 0, 128), one(128))
    copy(tl("SS", 96, 112), tl("LI", 0, 16))
    copy(tl("LA", 0, 32), tl("LI", 16, 48))
    copy(tl("FB", 0, 32), tl("LI", 0, 32))

    def psum(name, c, a, b):
        now[(PLACE[name][0] + str(c), PLACE[name][1] + a)] = name
        return (PLACE[name][0] + str(c), PLACE[name][1] + a, PLACE[name][1] + b, 1, 0, 128)

    def lists(LS, x, w):
        mm(LS, [(sel(r), sub(x, r, cnt(x), 16)) for r in range(8)], stop=False)
        mm(LS, [(tl("I7"), tl("ONH", 0, w), sub(LS, 0, w))] + [(sel(r), sub(x, r, cnt(x), 16)) for r in range(8, 16)], start=False)

    def chunk(c, t, lev):
        lim = V + 512 * t
        n = lim + 256 * lev + 128 * c
        st = lambda name, *a, **k: tl(name + str(c), *a, **k)
        lv = lambda name, *a, **k: tl("%s%d%d" % (name, c, lev), *a, **k)
        ps = lambda name, a, b: psum(name, c, a, b)
        xw, cw = tl("XT", XO, XO + lim), tl("CT", 0, lim - 256 if t and not lev else lim)
        if lev == 0:
            for a, at in ((1, ("SS", 96 - 32 * t)), (0, ("LA", 32 * t + 16)), (2, ("LA", 32 * t))):
                plus("KU", lv("KU", 128 * a, 128 * a + 128), cw, off=tl(at[0], at[1] + 8 * c, at[1] + 8 * c + 8))
        else:
            plus("KU", lv("KU"), cw, off=tl("LU%d0" % c))
            act(st("NV"), xw, ACT.Copy, off=tl("LU%d0" % c))
        kq = 256 if lev == 0 else 128
        plus("K", lv("K", 128, kq + 256), lv("KU", 256 - kq, 384), -2048.0)
        kid = lambda name, s0, m: lv("KU", 128 * "RQP".index(name) + s0, 128 * "RQP".index(name) + s0 + m)
        for end, j, step, s0, how in sorted(STEPS[c], key=lambda x: lev == 0 and x[2] == "MP"):
            m = end - s0
            big = lambda name: st(name, 16 * s0, 16 * end)
            if step in "QR" and how == "s":
                act(big(step), xw, ACT.Copy, off=kid(step, s0, m))
            elif step == "Q":
                copy(big("Q"), xw, off=kid("Q", s0, m))
            elif step in "RP":
                tt(big(step), xw, big("Q"), A.subtract, off=kid(step, s0, m))
            elif step == "MQ":
                ts(big("MQ"), big("P"), 1.0 / 64 - 32, A.add, -32.0, A.max)
            elif how == "s":
                act(big("MR_"), big("R"), ACT.Abs)
            elif how == "v":
                ts(big("MR_"), big("R"), 0.0, A.max, 2.0, A.mult)
            else:
                u = psum("U", now["turn"] % 2, 0, 16 * m)
                now["turn"] += 1
                if step == "MR_":
                    mm(u, [(tl("IH"), big("R")), (tl("IHM"), big("Q"))])
                else:
                    mm(u, [(tl("IH"), big("P")), (tl("IHM"), big("R"))] + ([(tl("IH"), big("Q"))] if how == "q" else []))
                act(big(step), u, ACT.Abs)
        D1, D23 = ps("D", 0, 128), ps("DD", 0, 256)
        D2, D3 = sub(D23, 0, 128), sub(D23, 128, 256)
        mm(D1, [(tl("ONK"), tl("CB", 0, 128)), (tl("ONH"), tl("TH2", 128, 256))]
           + ([(tl("ONH"), tl("THA", 128, 256))] if t else []), stop=False)
        mm(D23, [(tl("ONK"), tl("CB", 128, 384)), (tl("ONH"), tl("TH2", 0, 128), D2)]
           + ([(tl("ONH"), tl("THA", 0, 128), D2)] if t else []), stop=False)
        now[D1[:2]], now[D2[:2]] = "DE", "DF"
        for name, f, o, b in (("P", -2 * e, D3, 128), ("MQ", 4 * e, D3, 128), ("R", -1.0, D2, NV[c]), ("MR_", 1.0, D2, 128),
                              ("MP", e, D1, 128)):
            for k0 in range(0, 16 if b else 0, PE_RUN):
                mm(o, [(st(name, k, 16 * b, 16), weight[f], sub(o, k, 128, 16, rows=(0, b))) for k in range(k0, k0 + PE_RUN)],
                   start=False, stop=name in ("MR_", "MP") and k0 + PE_RUN == 16)
        act(lv("SB"), D2, ACT.Sign, scale=-1.0)
        plus("DI", lv("DI"), D3)
        tt(lv("NC"), D1, lv("SB"), A.is_lt)
        act(lv("SA"), D1, ACT.Sign, bias=-1.0, scale=-1.0)
        tt(lv("HI"), lv("DI"), lv("NC"), A.subtract)
        tt(lv("X"), D3, lv("HI"), A.is_lt)
        scan(lv("F"), tl("RST"), lv("HI"), A.add, A.max)
        copy(lv("FM"), lv("F", 15, 128, 16))
        tt(lv("E", 1, 129), lv("FM"), lv("F"), A.is_equal, off=tl("EQL"))
        star = [(lv("E", 1, 129), 1), (lv("E", 0, 128), -1), (tl("C_"), 1)]
        OH = ps("OH", 128, 256)
        mm(ps("OH", 0, 128), [(lv("NC"), tl("IH"))])
        mm(OH, [(x, tl("IH" if f > 0 else "IHM")) for x, f in reversed(star)])
        prq = lv("PR", kq, kq + 128)
        tt(prq, OH, lv("K", kq, kq + 128), A.mult)
        mm(ps("ZB", 0, 128), [(prq, tl("BOH"))])
        tt(lv("ZM"), ps("ZB", 0, 128), tl("MR"), A.mult)
        DIFF, ZL = ps("DIFF", 0, WIDE), ps("ZL", 0, 16)
        mm(DIFF, [(tl("IH"), tl("MK"))], stop=False)
        mm(DIFF, [(tl("BOM"), sub(prq, BLK * b, BLK * b + w), sub(DIFF, a + w * b, a + w * b + w))
                  for a, w in ROWS for b in range(nb)], start=False, stop=False)
        mm(ZL, [(lv("ZM"), tl("IND", WIDE, WIDE + 16))])
        mm(DIFF, [(lv("ZM"), tl("IND", 0, WIDE))], start=False)
        plus("LZ%d" % c, lv("LZ"), sub(ZL, 0, 8), 2048.0)
        act(lv("DF"), DIFF, ACT.Abs, scale=8192.0)
        act(lv("OZ"), ZL, ACT.Copy)
        scan(lv("MN"), tl("SEG"), lv("DF"), A.add, A.min)
        tt(lv("OF"), lv("MN"), lv("OZ"), A.min, off=tl("ENDS", 0, 1))
        plus("OU", lv("OU"), lv("OF", 0, 8), 2048.0 + XO)
        if lev == 0:
            tt(lv("PR", 384, 512), OH, lv("K", 384, 512), A.mult)
            tt(lv("PR", 0, 256), ps("OH", 0, 256), lv("K", 0, 256), A.mult)
            LS = ps("LS", 0, 32)
            lists(LS, lv("PR"), 8)
            plus("LU", lv("LU"), sub(LS, 8, 32), 2048.0)
            act(tl("CS", 8 * c, 8 * c + 8), sub(LS, 0, 8), ACT.Relu, scale=-64.0)
        else:
            plus("CL", tl("CL", 128 * c, 128 * c + 128), ps("OH", 0, 128))
        plus("XZ%d" % c, lv("XZ"), xw, off=lv("LZ"))
        mm(ps("HS", 0, 128), [(tl("IB"), tl("Y", 256 * t + 128 * c, 256 * t + 128 * c + 128)), (tl("IB"), lv("XZ"))])
        act(lv("HH"), ps("HS", 0, 128), ACT.Identity, bias=159.75, scale=0.5)
        M = [(tl("IH"), lv("K", kq, kq + 256)), (lv("SA"), tl("J2K")), (lv("X"), tl("J4K"))]
        if lev == 0:
            M += [(tl("IHM"), lv("PR", 256, 512))]
            for x, f in star:
                j = 128 * (2 * t + c + (0 if f > 0 else 8))
                M += [(x, tl("DG", j, j + 128), ps("M", 128 * a, 128 * a + 128)) for a in range(2)]
        mm(ps("M", 0, 256), M)
        plus("MA", lv("MA"), ps("M", 0, 128))
        tt(tl("MS", n - V, n - V + 128), ps("M", 128, 256), lv("MA"), A.max)

    for t in range(TV):
        lim = V + 512 * t
        bl = tl("SS", 96 - 32 * t, 112 - 32 * t)
        now["part"] = None
        if t < TV - 1:
            send(tl("LA", 32 * t + 48, 32 * t + 64), bl, "rc%d" % (t + 1), 3000)
        for lev in range(LV):
            n = lim + 256 * lev
            now["level"] = 2 * t + lev
            if lev == 0:
                part((0, 3))
                xw, nv = tl("XT", XO, XO + lim), tl("NVA")
                act(sub(nv, 0, 256), xw, ACT.Copy, off=bl)
                act(sub(nv, 256, 768), xw, ACT.Copy, off=tl("LA", 32 * t, 32 * t + 32))
            for c in (1, 0):
                part((lev, c))
                chunk(c, t, lev)
            part((lev, 2))
            nvp, x = psum("NVP", 1, 0, 256), psum("NVP", 1, 128, 256)
            if lev == 0:
                mm(nvp, [(tl("IB"), sub(nv, 0, 256)), (tl("IB"), sub(nv, 256, 512)), (tl("IBM"), sub(nv, 512, 768))])
            else:
                for c in (1, 0):
                    mm(sub(nvp, 128 * c, 128 * c + 128),
                       [(tl("IB" if a else "IBM"), tl("NV%d" % c, 128 * a, 128 * a + 128)) for a in range(3)])
            ts(tl("XT", XO + n, XO + n + 256), nvp, 0.0, A.max, 63.0, A.min)
            for c in (1, 0):
                for b0 in range(128 - BLK, -1, -BLK):
                    scatter_add(tl("XT", 0, XO + lim), tl("OU%d%d" % (c, lev), b0 // 16, (b0 + BLK) // 16),
                                tl("HH%d%d" % (c, lev), b0, b0 + BLK), tl("CM"))
            store(T.co[:, n - V:n - V + 256], tl("MS", n - V, n - V + 256), 2500)
            if t < TV - 1:
                select(tl("CT", n, n + 256), tl("MS", n - V, n - V + 256), [[0, 256]], A.is_ge, 0, 0)
        part((1, 3))
        LS = psum("LS", 1, 0, 16)
        lists(LS, tl("CL"), 16)
        tt(tl("AB"), LS, tl("CS"), A.is_lt)
        for a in range(2):
            mm(psum("VV", 1, 16 * a, 16 * a + 16),
               [(tl("IB"), tl("GI")), (tl("IB2K"), tl("BASE", 16 * t, 16 * t + 16)), (tl("IB8K"), tl("AB"))])
        fb = tl("FB", 32 * t + 32, 32 * t + 64)
        tt(fb, psum("VV", 1, 0, 32), tl("FB", 32 * t, 32 * t + 32), A.max)
        ABP, YD = psum("ABP", 1, 0, 256), psum("YD", 1, 0, 256)
        mm(ABP, [(tl("SELT", 128 * r, 128 * r + 128), tl("AB"), sub(ABP, r, 256, 16)) for r in range(16)], each=True)
        tt(tl("YM"), ABP, tl("Y", 256 * t, 256 * t + 256), A.mult)
        mm(YD, [(tl("IB"), tl("YM")), (tl("IBM"), tl("XT", XO + lim, XO + lim + 256))])
        yn = tl("N", 256 * t, 256 * t + 256)
        act(yn, YD, ACT.Abs)
        if t < TV - 1:
            copy(tl("SS", 64 - 32 * t, 96 - 32 * t), fb)
            la = tl("LA", 32 * t + 32, 32 * t + 48)
            send(la, tl("SS", 80 - 32 * t, 96 - 32 * t), "ra%d" % (t + 1), 3000)
            send(tl("Y", 256 * t + 256, 256 * t + 512), yn, "ry%d" % (t + 1), 3500)
            copy(sub(fb, 16, 32), la)
            act(tl("AX"), tl("AB"), ACT.Copy, accum=tl("AS"))
            ts(tl("THA"), tl("BOX"), tl("AS"), A.mult)
    part((2, 3))
    store(T.so[:], tl("FB", 128, 144), 2500)
    store(T.yo[:], tl("N", 768, 1024), 2500)
    store(T.xo[:, 3584:4096], tl("XT", XO + 3584, XO + 4096), 2500)
    store(T.xo[:, 0:1792], tl("XT", XO, XO + 1792), 3500)
    store(T.xo[:, 1792:3584], tl("XT", XO + 1792, XO + 3584), 3500, q="act")
    return ops


def plan(ops):
    n, sets = len(ops), range(len(FIG))
    deps = [set() for _ in range(n)]
    hist = {}
    cell = lambda s: [(s[0], b) for b in range(s[1] // 256, (s[2] - 1) // 256 + 1)]
    for i, o in enumerate(ops):
        for wr, ss in ((False, o["rd"]), (True, o["wr"])):
            for s in ss:
                for c in cell(s):
                    for j, w2, h in hist.get(c, []):
                        if j != i and (wr or w2) and h[1] < s[2] and s[1] < h[2] and h[4] < s[5] and s[4] < h[5]:
                            deps[i].add(j)
        for s in o["wr"]:
            if s[3] == 1:
                for c in cell(s):
                    hist[c] = [x for x in hist.get(c, [])
                               if not (s[1] <= x[2][1] and x[2][2] <= s[2] and s[4] <= x[2][4] and x[2][5] <= s[5])]
        for wr, ss in ((False, o["rd"]), (True, o["wr"])):
            for s in ss:
                for c in cell(s):
                    hist.setdefault(c, []).append((i, wr, s))
        if o["after"] is not None:
            deps[i].add(o["after"])
        o["banks"] = set(s[0] for s in o["rd"] + o["wr"] if s[0] in PSUM)
    pre = [deps[i] | ({ops[i]["soft"]} if ops[i]["soft"] is not None else set()) for i in range(n)]
    succ = [[] for _ in range(n)]
    for i in range(n):
        for j in pre[i]:
            succ[j].append(i)

    def hop(j, i, m):
        if ops[i]["soft"] == j:
            return 0.0
        if ops[j]["q"] == ops[i]["q"]:
            return float(ops[j]["lat"][m] + (0.0 if ops[i]["q"] == "pe" else HOP_SAME[m]))
        return float(ops[j]["lat"][m] + HOP_OTHER[m])

    names = {}
    number = lambda x: names.setdefault(x, len(names))
    facts = [[(number(o["q"]), float(o["cost"][m]), [number(b) for b in sorted(o["banks"])], float(o["lat"][m])) for o in ops]
             for m in sets]
    kinds = {}
    for i, o in enumerate(ops):
        kinds.setdefault(o["kind"], []).append(i)
    place = {i: (v, x) for v in kinds.values() for x, i in enumerate(v)}
    above, lag = [0] * n, [[] for m in sets]
    for i in range(n):
        for j in pre[i]:
            above[i] |= above[j]
        for m in sets:
            lag[m].append([(j, hop(j, i, m)) for j in sorted(pre[i]) if not above[i] >> j & 1])
        for j in pre[i]:
            above[i] |= 1 << j
    base = [0.0] * n
    for i in range(n - 1, -1, -1):
        base[i] = facts[0][i][1] + max([base[k] + hop(i, k, 0) for k in succ[i]] or [facts[0][i][3]])

    named = {(o["q"], o["level"], "%s%d%s" % (o["kind"][2], o["kind"][3], ("", "'", "*", "!")[o["kind"][0][1]])): i
             for i, o in enumerate(ops) if isinstance(o["kind"], tuple)}
    line = {q: [] for q in ("dve", "act", "pe")}
    for level in range(-1, TV * LV + 1):
        for q in line:
            for x in ORDER[level % 2][q].split():
                key = (q, level + {"-": -1, "+": 1}.get(x[0], 0), x.lstrip("+-"))
                if key in named:
                    line[q].append(named.pop(key))
    assert len([k for k in named if k[0] in line]) <= 1, [k for k in named if k[0] in line]
    listed = set(i for q in line for i in line[q])
    left = [len(d) for d in pre]
    ready = [i for i in range(n) if left[i] == 0]
    fin, last, order, head = [0.0] * n, [None] * len(names), [], {q: 0 for q in line}
    while len(order) < n:
        best = None
        for i in ready:
            q, cost, banks, lat = facts[0][i]
            if i in listed and line[ops[i]["q"]][head[ops[i]["q"]]] != i:
                continue
            s = max([fin[j] + h for j, h in lag[0][i]] + [0.0 if last[q] is None else fin[last[q]]]
                    + [fin[last[b]] + HOP_OTHER[0] for b in banks if last[b] is not None and facts[0][last[b]][0] != q])
            if best is None or (s, -base[i]) < best[0]:
                best = ((s, -base[i]), i)
        assert best is not None, [(ops[line[q][head[q]]]["kind"], [ops[j]["kind"] for j in pre[line[q][head[q]]] if j not in order])
                                  for q in line]
        i = best[1]
        fin[i], last[facts[0][i][0]] = best[0][0] + facts[0][i][1], i
        for b in facts[0][i][2]:
            last[b] = i
        if i in listed:
            head[ops[i]["q"]] += 1
        ready.remove(i)
        order.append(i)
        for k in succ[i]:
            left[k] -= 1
            if left[k] == 0:
                ready.append(k)
    mark = max(i for i, o in enumerate(ops) if o["level"] == 3 and o["q"] == "dve" and o["kind"][2] == "XT")

    def play(order, m, short):
        fin, why, last = [0.0] * n, [None] * n, [None] * len(names)
        end, x, fact, lags, other = 0.0, None, facts[m], lag[m], float(HOP_OTHER[m])
        for i in order:
            q, cost, banks, lat = fact[i]
            s, w = 0.0, None
            for j, h in lags[i]:
                if fin[j] + h > s:
                    s, w = fin[j] + h, (j, False)
            j = last[q]
            if j is not None and fin[j] > s:
                s, w = fin[j], (j, True)
            for b in banks:
                j = last[b]
                if j is not None and fact[j][0] != q and fin[j] + other > s:
                    s, w = fin[j] + other, (j, True)
                last[b] = i
            fin[i], why[i], last[q] = s + cost, w, i
            if s + cost + lat > end:
                end, x = s + cost + lat, i
        pairs = []
        if short:
            end, x = fin[mark], mark
        while why[x]:
            if why[x][1]:
                pairs.append((why[x][0], x))
            x = why[x][0]
        return end, pairs, fin

    def judge(order, short, unit, limit):
        total, pairs = 0.0, []
        part = order[:order.index(mark) + 1] if short else order
        for m in sets:
            res = play(part, m, short)
            total += res[0] / unit[m]
            pairs += res[1]
            if total > limit[m]:
                return None
        return total, pairs, order

    def swap(order, b, i, ahead):
        x, y = order.index(b), order.index(i)
        if x > y:
            return order
        mid = order[x:y + 1]
        move = {i if ahead else b}
        for k in (reversed(mid) if ahead else mid):
            if k not in move and any(j in move for j in (succ[k] if ahead else pre[k])):
                move.add(k)
        if (b if ahead else i) in move:
            return order
        one, other = [k for k in mid if k in move], [k for k in mid if k not in move]
        return order[:x] + (one + other if ahead else other + one) + order[y + 1:]

    rng = np.random.RandomState(SEED)
    first = [play(order, m, False)[0] for m in sets]
    for short, swaps, heat, alike in ((True, SWAPS, HEAT, 1.0), (False, SWAPS // 8, HEAT / 4, 0.3)):
        part = order[:order.index(mark) + 1] if short else order
        unit = [play(part, m, short)[0] for m in sets]
        cur = keep = judge(order, short, unit, [1e9] * len(FIG))
        for it in range(swaps):
            b, i = cur[1][int(rng.randint(len(cur[1])))]
            ahead, new = rng.rand() < 0.5, cur[2]
            if rng.rand() < alike:
                (vb, xb), (vi, xi) = place[b], place[i]
                for x in range(len(vi)):
                    if 0 <= x + xb - xi < len(vb):
                        new = swap(new, vb[x + xb - xi], vi[x], ahead)
            else:
                new = swap(new, b, i, ahead)
            if new is cur[2]:
                continue
            top = cur[0] + len(FIG) * heat * (1.0 - it / swaps) * rng.rand() ** 2
            res = judge(new, short, unit, [top * (m + 1) / len(FIG) + 0.02 * (m + 1 < len(FIG)) for m in sets])
            if res is not None:
                cur = res
                if cur[0] < keep[0]:
                    keep = cur
        order = keep[2]
    ends, fin, bank = [play(order, m, False)[0] for m in sets], play(order, 0, False)[2], {}
    for i in order:
        ops[i]["t0"] = fin[i] - facts[0][i][1]
        for b in ops[i]["banks"]:
            deps[i] |= set(j for q, j in bank.get(b, {}).items() if q != ops[i]["q"])
            bank.setdefault(b, {})[ops[i]["q"]] = i
    return order, deps, ends, first


PLAN = {}


def rank_program(g, core, T, topo):
    rank = T.rank_of(core)
    if rank is None:
        return
    ops = build(T, T.cores[(rank + 1) % len(T.cores)], topo, core)
    if "p" not in PLAN:
        PLAN["p"] = plan(ops)
    order, deps = PLAN["p"][:2]
    queues = {"pe": g.tensor, "dve": g.vector, "act": g.scalar, "pool": g, "sync": g.sync}
    total, mark, seen = {}, {}, {}
    for i in order:
        o = ops[i]
        if o["sem"] is not None:
            total[o["sem"]] = total.get(o["sem"], 0) + o["inc"]
            mark[i] = total[o["sem"]]
        if o["q"] not in queues:
            continue
        need = {}
        for j in deps[i]:
            p = ops[j]
            if p["sem"] is None or (p["q"] == "pe" and o["q"] == "pe"):
                continue
            need[p["sem"]] = max(need.get(p["sem"], 0), mark[j])
        q = queues[o["q"]]
        for s, v in sorted(need.items()):
            if seen.get((o["q"], s), 0) < v:
                q.wait_ge(T.sem[s], v)
                seen[(o["q"], s)] = v
        for ins in o["fn"](q):
            ins.then_inc(T.sem[o["sem"]], 16 if o["own"] else 1)
    for s in sorted(total):
        g.wait_ge(T.sem[s], total[s])
